import numpy as np
import ml_dtypes


def mxq(x, axis, fmt="e4m3"):
    dtype, down = {"e4m3": (ml_dtypes.float8_e4m3fn, 7), "e5m2": (ml_dtypes.float8_e5m2, 14)}[fmt]
    v = np.moveaxis(np.asarray(x, np.float32).astype(ml_dtypes.bfloat16).astype(np.float64), axis, -1)
    blocks = v.reshape(v.shape[:-1] + (-1, 32))
    amax = np.abs(blocks).max(-1, keepdims=True)
    byte = np.maximum(np.where(amax > 0, np.frexp(amax)[1] - 1 + 127, 0) - down, 1)
    scale = np.exp2(byte - 127.0)
    codes = (blocks / scale).astype(np.float32).astype(dtype).astype(np.float64)
    return np.moveaxis((codes * scale).reshape(v.shape), -1, axis)


WIDE = False


def mx_kscale(k):
    if not WIDE:
        return np.ones(k)
    levels = np.array([10, -10, 5, -5, 0])
    if k % 512:
        return np.exp2(np.random.permutation(np.resize(levels, k // 32))).repeat(32)
    a = np.empty((k // 512, 16))
    for p in range(k // 512):
        a[p, :8] = np.random.permutation(np.resize(levels, 8))
        for g in range(8):
            far = levels[np.abs(levels - a[p, g]) >= 10]
            a[p, g + 8] = far[np.random.randint(len(far))]
    return np.exp2(a.ravel()).repeat(32)


BF16 = ml_dtypes.bfloat16


def bf(x):
    return np.asarray(x, np.float32).astype(BF16)


def f64(x):
    return np.asarray(x).astype(np.float64)


E2M1 = np.array([0.0, 0.5, 1.0, 1.5, 2.0, 3.0, 4.0, 6.0, -0.0, -0.5, -1.0, -1.5, -2.0, -3.0, -4.0, -6.0])


def pack_weight(w, fmt):
    k, n = w.shape
    w = f64(bf(w)).reshape(k // 32, 32, n)
    amax = np.abs(w).max(1)
    if fmt == "e4m3":
        byte = np.frexp(amax)[1] - 1 + 127 - 7
    else:
        mant, ex = np.frexp(amax / 6.0)
        byte = np.where(mant > 0.5, ex, ex - 1) + 127
    byte = np.clip(np.where(amax > 0, byte, 1), 1, 254)
    scaled = (w * np.exp2(127.0 - byte)[:, None, :]).reshape(k, n).astype(np.float32)
    by_word = np.ascontiguousarray(scaled.reshape(k // 512, 128, 4, n).transpose(0, 1, 3, 2))
    if fmt == "e4m3":
        words = by_word.astype(ml_dtypes.float8_e4m3fn).view(np.uint8)
    else:
        c = by_word.astype(ml_dtypes.float4_e2m1fn).view(np.uint8) & 0xF
        words = c[..., 0::2] | (c[..., 1::2] << 4)
    return np.ascontiguousarray(words), np.ascontiguousarray(byte.astype(np.uint8).reshape(k // 512, 16, n))


def unpack_weight(words, scales, fmt):
    g, p, n, _ = words.shape
    if fmt == "e4m3":
        vals = np.ascontiguousarray(words).view(ml_dtypes.float8_e4m3fn).astype(np.float64)
    else:
        nib = np.empty((g, p, n, 4), np.uint8)
        nib[..., 0::2] = words & 0xF
        nib[..., 1::2] = words >> 4
        vals = E2M1[nib]
    vals = vals * np.repeat(np.exp2(scales.astype(np.float64) - 127.0), 8, axis=1)[..., None]
    return vals.transpose(0, 1, 3, 2).reshape(g * 512, n)
def pack4(w):
    words, scales = pack_weight(w, "e2m1")
    return words.reshape(words.shape[0], 128, -1), scales


def unpack4(words, scales):
    return unpack_weight(words.reshape(words.shape[0], 128, -1, 2), scales, "e2m1")


P, T, F, H = 1024, 4, 512, 512


def setup_inputs():
    s, t = mx_kscale(P), mx_kscale(F)
    x = np.random.standard_normal((P, T, F)) * s[:, None, None] * t
    a = 0.5 * np.random.standard_normal((P, P)) / np.sqrt(P) / s[:, None] * s
    b = 0.35 * np.random.standard_normal((F, F)) / np.sqrt(F) / t[:, None] * t
    c = np.random.standard_normal((P, H)) / np.sqrt(H) / s[:, None]
    sc_words, sc_scales = pack4(a)
    fb_words, fb_scales = pack4(b)
    hs_words, hs_scales = pack4(c)
    return {"x": bf(x),
            "sc_words": sc_words, "sc_scales": sc_scales,
            "fb_words": fb_words, "fb_scales": fb_scales,
            "hs_words": hs_words, "hs_scales": hs_scales,
            "gain": bf(np.random.uniform(0.5, 1.5, F) / t)}


def reference(x, sc_words, sc_scales, fb_words, fb_scales, hs_words, hs_scales, gain):
    x, gain = f64(x), f64(gain)
    a = unpack4(sc_words, sc_scales)
    b = unpack4(fb_words, fb_scales)
    c = unpack4(hs_words, hs_scales)
    d = (a.T @ mxq(x, 0, "e4m3").reshape(P, T * F)).reshape(P, T, F)
    h1 = x + np.maximum(d, 0)
    e = (mxq(h1, 2, "e4m3").reshape(P * T, F) @ b).reshape(P, T, F)
    h2 = h1 + e
    q = mxq(h2, 0, "e4m3").reshape(P, T * F)
    to_left = (c[H:].T @ q[H:]).reshape(H, T, F)
    to_right = (c[:H].T @ q[:H]).reshape(H, T, F)
    return gain * to_left, gain * to_right

@@ -1,0 +1,318 @@
+from contextlib import ExitStack
+
+import concourse.mybir as mybir
+from concourse.masks import make_identity
+
+P, T, F, H = 1024, 4, 512, 512
+FLOPS = 2 * P * P * T * F + 2 * P * T * F * F + 2 * 2 * H * H * T * F
+
+F32 = mybir.dt.float32
+BF16 = mybir.dt.bfloat16
+U32 = mybir.dt.uint32
+I32 = mybir.dt.int32
+U8 = mybir.dt.uint8
+FP8X4 = mybir.dt.float8_e4m3fn_x4
+FP4X4 = mybir.dt.float4_e2m1fn_x4
+ALU = mybir.AluOpType
+
+NP = 128
+LT, L2, L3 = 3, 8, 14
+RUN = 2
+Q1LAG = 1
+XQ_AT = (4,7)
+XCH = 4
+SPLIT = 320
+OE_V = (15,23,29,31)
+
+
+def tile_parcel_band_hemisphere_coupling_t2_kernel(
+    tc, x, sc_words, sc_scales, fb_words, fb_scales, hs_words, hs_scales, gain, out_left, out_right
+):
+    nc = tc.nc
+    outs = (out_right, out_left)
+    with ExitStack() as ctx:
+        keep = ctx.enter_context(tc.tile_pool(name="keep", bufs=1))
+        work = ctx.enter_context(tc.tile_pool(name="work", bufs=2))
+        psum = ctx.enter_context(tc.psum_pool(name="psum", bufs=2))
+        ctx.enter_context(tc.manual_schedule())
+
+        ident = keep.tile([NP, NP], F32, name="ident")
+        a_raw = keep.tile([NP, 2, 2 * P], U8, name="a_raw", align_bytes=64)
+        a_sraw = keep.tile([NP, 2, P], U8, name="a_sraw", align_bytes=64)
+        a_w = keep.tile([NP, 2, 2 * P], U8, name="a_w", align_bytes=64)
+        a_s = keep.tile([NP, 2, P], U8, name="a_s", align_bytes=64)
+        b_raw = keep.tile([NP, 2 * F], U8, name="b_raw", align_bytes=64)
+        b_sraw = keep.tile([NP, F], U8, name="b_sraw", align_bytes=64)
+        b_w = keep.tile([NP, 2 * F], U8, name="b_w", align_bytes=64)
+        b_s = keep.tile([NP, F], U8, name="b_s", align_bytes=64)
+        c_w = keep.tile([NP, 2, 2 * H], U8, name="c_w", align_bytes=64)
+        c_s = keep.tile([NP, 2, H], U8, name="c_s", align_bytes=64)
+        gain_b = keep.tile([NP, F], BF16, name="gain_b")
+        xs = {}
+        for w in range(T):
+            for k in range(2):
+                xt = keep.tile([NP, 4, F], BF16, name="x_%d_%d" % (w, k))
+                xs[w, k] = xt
+
+        nc.vector.memset(a_sraw[:].bitcast(I32), 0)
+        nc.gpsimd.memset(b_sraw[:].bitcast(I32), 0)
+        nc.gpsimd.memset(c_s[:].bitcast(I32), 0)
+        make_identity(nc, ident[:])
+
+        def load_x(w, k):
+            nc.sync.dma_start(out=xs[w, k][:], in_=x[512 * k : 512 * k + 512, w, :].rearrange("(p t) f -> p t f", t=4))
+
+        a_src = sc_words.bitcast(I32)
+        def load_a(h):
+            nc.sync.dma_start(
+                out=a_raw[:].bitcast(I32)[:, :, 256 * h : 256 * h + 256],
+                in_=a_src[:, :, 256 * h : 256 * h + 256].rearrange("g p n -> p g n"),
+            )
+
+        for q in range(4):
+            nc.scalar.dma_start(
+                out=a_sraw[32 * q : 32 * q + 4].bitcast(I32),
+                in_=sc_scales.bitcast(I32)[:, 4 * q : 4 * q + 4, :].rearrange("g q n -> q g n"),
+            )
+        load_x(0, 0)
+        load_a(0)
+        load_x(0, 1)
+        load_a(1)
+        nc.sync.dma_start(out=b_raw[:].bitcast(I32), in_=fb_words.bitcast(I32)[0])
+        for q in range(4):
+            nc.sync.dma_start(
+                out=b_sraw[32 * q : 32 * q + 4].bitcast(I32),
+                in_=fb_scales.bitcast(I32)[0, 4 * q : 4 * q + 4, :],
+            )
+        load_x(1, 0)
+        load_x(1, 1)
+        nc.sync.dma_start(out=c_w[:].bitcast(I32), in_=hs_words.bitcast(I32).rearrange("g p n -> p g n"))
+        for q in range(4):
+            nc.sync.dma_start(
+                out=c_s[32 * q : 32 * q + 4].bitcast(I32),
+                in_=hs_scales.bitcast(I32)[:, 4 * q : 4 * q + 4, :].rearrange("g q n -> q g n"),
+            )
+        for w in (2, 3):
+            for k in range(2):
+                load_x(w, k)
+        nc.sync.dma_start(out=gain_b[:], in_=gain.partition_broadcast(NP))
+
+        def perm_a(h, k):
+            nc.vector.tensor_copy(
+                out=a_w[:, k, 1024 * h : 1024 * h + 1024].rearrange("p (t m b) -> p t m b", t=4, b=2),
+                in_=a_raw[:, k, 1024 * h : 1024 * h + 1024].rearrange("p (m t b) -> p t m b", t=4, b=2),
+            )
+            nc.vector.tensor_copy(
+                out=a_s[:, k, 512 * h : 512 * h + 512].rearrange("p (t m) -> p t m", t=4),
+                in_=a_sraw[:, k, 512 * h : 512 * h + 512].rearrange("p (m t) -> p t m", t=4),
+            )
+
+        def perm_b():
+            nc.vector.tensor_copy(
+                out=b_w[:].rearrange("p (t m b) -> p t m b", t=4, b=2),
+                in_=b_raw[:].rearrange("p (m t b) -> p t m b", t=4, b=2),
+            )
+            nc.vector.tensor_copy(
+                out=b_s[:].rearrange("p (t m) -> p t m", t=4),
+                in_=b_sraw[:].rearrange("p (m t) -> p t m", t=4),
+            )
+
+        xg, xc, xsc = {}, {}, {}
+
+        def x_interleave(w, k, lo, hi, on_vector):
+            if (w, k) not in xg:
+                g = work.tile([NP, F, 4], BF16, name="xg_%d_%d" % (w, k), tag="xg", bufs=3, align_bytes=64)
+                xg[w, k] = g
+            dst = xg[w, k][:, lo:hi, :].rearrange("p (c i) t -> p c t i", i=4)
+            src = xs[w, k][:, :, lo:hi].rearrange("p t (c i) -> p c t i", i=4)
+            if on_vector:
+                nc.vector.tensor_copy(out=dst, in_=src)
+            else:
+                nc.scalar.copy(out=dst, in_=src)
+
+        def x_quantize(w, k):
+            c = work.tile([NP, F], U32, name="xc_%d_%d" % (w, k), tag="xc", bufs=4, align_bytes=64)
+            s = work.tile([NP, F], U8, name="xsc_%d_%d" % (w, k), tag="xsc", bufs=4, align_bytes=64)
+            nc.vector.quantize_mx(out=c[:].bitcast(FP8X4), scales=s[:], in_=xg[w, k][:].rearrange("p f t -> p (f t)"))
+            xc[w, k], xsc[w, k] = c, s
+
+        d, h1, h1t, h1g, h1c, h1s, e, h2g, h2c, h2s, o = ({} for i in range(11))
+
+        def mm1(i):
+            u, t = divmod(i, 4)
+            w, h = divmod(u, 2)
+            acc = psum.tile([NP, F], F32, name="d_%d" % i, tag="d", bufs=2)
+            for k in range(2):
+                nc.tensor.matmul_mx(
+                    out=acc[:],
+                    lhsT=a_w[:, k, 1024 * h + 256 * t : 1024 * h + 256 * t + 256].bitcast(FP4X4),
+                    lhsT_scale=a_s[:, k, 512 * h + 128 * t : 512 * h + 128 * t + 128],
+                    rhs=xc[w, k][:].bitcast(FP8X4),
+                    rhs_scale=xsc[w, k][:],
+                    start=(k == 0),
+                    stop=(k == 1),
+                )
+            d[i] = acc
+
+        def add1(i):
+            u, t = divmod(i, 4)
+            w, h = divmod(u, 2)
+            if t == 0:
+                tile = work.tile([NP, 4, F], F32, name="h1_%d" % u, tag="h1", bufs=4)
+                h1[u] = tile
+            nc.vector.scalar_tensor_tensor(
+                out=h1[u][:, t, :].rearrange("p (t m) -> p t m", t=4),
+                in0=d[i][:].rearrange("p (m t) -> p t m", t=4),
+                scalar=0.0,
+                in1=xs[w, h][:, t, :].rearrange("p (m t) -> p t m", t=4),
+                op0=ALU.max,
+                op1=ALU.add,
+            )
+
+        def turn(i):
+            u, t = divmod(i, 4)
+            bank = psum.tile([NP, 4, NP], F32, name="h1t_%d" % i, tag="h1t", bufs=2)
+            for b in range(4):
+                nc.tensor.transpose(bank[:, b, :], h1[u][:, t, NP * b : NP * b + NP], ident[:])
+            h1t[i] = bank
+
+        def gather1(i):
+            u, t = divmod(i, 4)
+            if t == 0:
+                tile = work.tile([NP, F, 4], BF16, name="h1g_%d" % u, tag="h1g", bufs=2, align_bytes=64)
+                h1g[u] = tile
+            nc.scalar.copy(
+                out=h1g[u][:, NP * t : NP * t + NP, :],
+                in_=h1t[i][:].rearrange("p t q -> p q t"),
+            )
+
+        def quant1(u):
+            c = work.tile([NP, F], U32, name="h1c_%d" % u, tag="h1c", bufs=3, align_bytes=64)
+            s = work.tile([NP, F], U8, name="h1s_%d" % u, tag="h1s", bufs=3, align_bytes=64)
+            nc.vector.quantize_mx(out=c[:].bitcast(FP8X4), scales=s[:], in_=h1g[u][:].rearrange("p q t -> p (q t)"))
+            h1c[u], h1s[u] = c, s
+
+        def mm2(i):
+            u, b = divmod(i, 4)
+            bank = psum.tile([NP, 4, NP], F32, name="e_%d" % i, tag="e", bufs=2)
+            for t in range(4):
+                nc.tensor.matmul_mx(
+                    out=bank[:, t, :],
+                    lhsT=h1c[u][:, NP * t : NP * t + NP].bitcast(FP8X4),
+                    lhsT_scale=h1s[u][:, NP * t : NP * t + NP],
+                    rhs=b_w[:, 256 * b : 256 * b + 256].bitcast(FP4X4),
+                    rhs_scale=b_s[:, NP * b : NP * b + NP],
+                    start=True,
+                    stop=True,
+                )
+            e[i] = bank
+
+        def add2(i):
+            u, b = divmod(i, 4)
+            if b == 0:
+                tile = work.tile([NP, F, 4], BF16, name="h2g_%d" % u, tag="h2g", bufs=2, align_bytes=64)
+                h2g[u] = tile
+            cols = slice(NP * b, NP * b + NP)
+            nc.vector.tensor_tensor(
+                out=h2g[u][:, cols, :].rearrange("p (a i) t -> p a t i", i=4),
+                in0=e[i][:].rearrange("p t (a i) -> p a t i", i=4),
+                in1=h1[u][:, :, cols].rearrange("p t (a i) -> p a t i", i=4),
+                op=ALU.add,
+            )
+
+        def quant2(u):
+            c = work.tile([NP, F], U32, name="h2c_%d" % u, tag="h2c", bufs=3, align_bytes=64)
+            s = work.tile([NP, F], U8, name="h2s_%d" % u, tag="h2s", bufs=3, align_bytes=64)
+            nc.vector.quantize_mx(out=c[:].bitcast(FP8X4), scales=s[:], in_=h2g[u][:].rearrange("p f t -> p (f t)"))
+            h2c[u], h2s[u] = c, s
+
+        def mm3(i):
+            u, m = divmod(i, 4)
+            g = u % 2
+            bank = psum.tile([NP, F], F32, name="o_%d" % i, tag="o", bufs=2)
+            nc.tensor.matmul_mx(
+                out=bank[:],
+                lhsT=c_w[:, g, 256 * m : 256 * m + 256].bitcast(FP4X4),
+                lhsT_scale=c_s[:, g, NP * m : NP * m + NP],
+                rhs=h2c[u][:].bitcast(FP8X4),
+                rhs_scale=h2s[u][:],
+                start=True,
+                stop=True,
+            )
+            o[i] = bank
+
+        def finish(i):
+            u, m = divmod(i, 4)
+            w, g = divmod(u, 2)
+            res = work.tile([NP, F], F32, name="res_%d" % i, tag="res", bufs=6)
+            if i in OE_V:
+                nc.vector.tensor_tensor(
+                    out=res[:].rearrange("p (m t) -> p m t", t=4),
+                    in0=o[i][:].rearrange("p (t m) -> p m t", t=4),
+                    in1=gain_b[:].rearrange("p (m t) -> p m t", t=4),
+                    op=ALU.mult,
+                )
+            else:
+                raw = work.tile([NP, F], F32, name="raw_%d" % i, tag="raw", bufs=4)
+                nc.scalar.copy(
+                    out=raw[:].rearrange("p (m t) -> p m t", t=4),
+                    in_=o[i][:].rearrange("p (t m) -> p m t", t=4),
+                )
+                for part in range(2):
+                    cols = slice(256 * part, 256 * part + 256)
+                    nc.gpsimd.tensor_tensor(out=res[:, cols], in0=raw[:, cols], in1=gain_b[:, cols], op=ALU.mult)
+            nc.sync.dma_start(out=outs[g][NP * m : NP * m + NP, w, :], in_=res[:])
+
+        x_interleave(0, 0, 0, SPLIT, False)
+        x_interleave(0, 1, 0, SPLIT, False)
+        x_interleave(0, 0, SPLIT, F, True)
+        perm_a(0, 0)
+        x_quantize(0, 0)
+        x_interleave(0, 1, SPLIT, F, True)
+        perm_a(0, 1)
+        x_quantize(0, 1)
+
+        n = 32
+
+        def ok(i):
+            return 0 <= i < n
+
+        for s in range(n + L3):
+            i, j = s, s - LT
+            w, r = s // 8 + 1, s % 8
+            turns = [v for v in range(j - RUN + 1, j + 1) if ok(v)] if j % RUN == RUN - 1 else []
+            for v in turns:
+                turn(v)
+            if ok(s - L3):
+                mm3(s - L3)
+            if ok(s - L2):
+                mm2(s - L2)
+            if ok(i):
+                mm1(i)
+            if s == 2:
+                perm_a(1, 0)
+                perm_a(1, 1)
+            if s == 5:
+                perm_b()
+            if w < T:
+                for c in range(2 * XCH):
+                    if c * XQ_AT[1] // (2 * XCH) == r:
+                        k, cc = divmod(c, XCH)
+                        x_interleave(w, k, F // XCH * cc, F // XCH * (cc + 1), False)
+            for v in turns:
+                gather1(v)
+            for u in range(8):
+                if 4 * u + 3 + LT == s - Q1LAG:
+                    quant1(u)
+            if w < T:
+                for k in range(2):
+                    if XQ_AT[k] == r:
+                        x_quantize(w, k)
+            if ok(s - L2):
+                add2(s - L2)
+            if ok(i):
+                add1(i)
+            if ok(s - L2) and (s - L2) % 4 == 3:
+                quant2((s - L2) // 4)
+            if ok(s - L3):
+                finish(s - L3)

@@ -11,18 +11,18 @@ BF16 = mybir.dt.bfloat16
 U32 = mybir.dt.uint32
 I32 = mybir.dt.int32
 U8 = mybir.dt.uint8
+U16 = mybir.dt.uint16
 FP8X4 = mybir.dt.float8_e4m3fn_x4
 FP4X4 = mybir.dt.float4_e2m1fn_x4
 ALU = mybir.AluOpType
 
 NP = 128
-LT, L2, L3 = 3, 8, 14
-RUN = 2
-Q1LAG = 1
-XQ_AT = (4,7)
-XCH = 4
-SPLIT = 320
-OE_V = (15,23,29,31)
+SPLIT = 192
+TB = (0, 1, 2, 0)
+OB = (0, 1, 2, 3)
+X0 = 6
+XN = (1, 1, 1, 2)
+QX = (0, 1, 2, 3, 4, 5)
 
 
 def tile_parcel_band_hemisphere_coupling_t2_kernel(
@@ -37,10 +37,12 @@ def tile_parcel_band_hemisphere_coupling_t2_kernel(
         ctx.enter_context(tc.manual_schedule())
 
         ident = keep.tile([NP, NP], F32, name="ident")
-        a_raw = keep.tile([NP, 2, 2 * P], U8, name="a_raw", align_bytes=64)
+        a_raw, a_w, a_s = {}, {}, {}
+        for h in range(2):
+            a_raw[h] = keep.tile([NP, 2, P], U8, name="a_raw_%d" % h, align_bytes=64)
+            a_w[h] = keep.tile([NP, 2, P], U8, name="a_w_%d" % h, align_bytes=64)
+            a_s[h] = keep.tile([NP, 2, H], U8, name="a_s_%d" % h, align_bytes=64)
         a_sraw = keep.tile([NP, 2, P], U8, name="a_sraw", align_bytes=64)
-        a_w = keep.tile([NP, 2, 2 * P], U8, name="a_w", align_bytes=64)
-        a_s = keep.tile([NP, 2, P], U8, name="a_s", align_bytes=64)
         b_raw = keep.tile([NP, 2 * F], U8, name="b_raw", align_bytes=64)
         b_sraw = keep.tile([NP, F], U8, name="b_sraw", align_bytes=64)
         b_w = keep.tile([NP, 2 * F], U8, name="b_w", align_bytes=64)
@@ -55,36 +57,37 @@ def tile_parcel_band_hemisphere_coupling_t2_kernel(
                 xs[w, k] = xt
 
         nc.vector.memset(a_sraw[:].bitcast(I32), 0)
-        nc.gpsimd.memset(b_sraw[:].bitcast(I32), 0)
-        nc.gpsimd.memset(c_s[:].bitcast(I32), 0)
+        nc.vector.memset(b_sraw[:].bitcast(I32), 0)
+        nc.vector.memset(c_s[:].bitcast(I32), 0)
         make_identity(nc, ident[:])
 
         def load_x(w, k):
             nc.sync.dma_start(out=xs[w, k][:], in_=x[512 * k : 512 * k + 512, w, :].rearrange("(p t) f -> p t f", t=4))
 
         a_src = sc_words.bitcast(I32)
+
         def load_a(h):
             nc.sync.dma_start(
-                out=a_raw[:].bitcast(I32)[:, :, 256 * h : 256 * h + 256],
+                out=a_raw[h][:].bitcast(I32),
                 in_=a_src[:, :, 256 * h : 256 * h + 256].rearrange("g p n -> p g n"),
             )
 
+        load_a(0)
         for q in range(4):
-            nc.scalar.dma_start(
+            nc.sync.dma_start(
                 out=a_sraw[32 * q : 32 * q + 4].bitcast(I32),
                 in_=sc_scales.bitcast(I32)[:, 4 * q : 4 * q + 4, :].rearrange("g q n -> q g n"),
             )
         load_x(0, 0)
-        load_a(0)
         load_x(0, 1)
         load_a(1)
+        load_x(1, 0)
         nc.sync.dma_start(out=b_raw[:].bitcast(I32), in_=fb_words.bitcast(I32)[0])
         for q in range(4):
             nc.sync.dma_start(
                 out=b_sraw[32 * q : 32 * q + 4].bitcast(I32),
                 in_=fb_scales.bitcast(I32)[0, 4 * q : 4 * q + 4, :],
             )
-        load_x(1, 0)
         load_x(1, 1)
         nc.sync.dma_start(out=c_w[:].bitcast(I32), in_=hs_words.bitcast(I32).rearrange("g p n -> p g n"))
         for q in range(4):
@@ -92,25 +95,25 @@ def tile_parcel_band_hemisphere_coupling_t2_kernel(
                 out=c_s[32 * q : 32 * q + 4].bitcast(I32),
                 in_=hs_scales.bitcast(I32)[:, 4 * q : 4 * q + 4, :].rearrange("g q n -> q g n"),
             )
+        nc.sync.dma_start(out=gain_b[:], in_=gain.partition_broadcast(NP))
         for w in (2, 3):
             for k in range(2):
                 load_x(w, k)
-        nc.sync.dma_start(out=gain_b[:], in_=gain.partition_broadcast(NP))
 
-        def perm_a(h, k):
+        def perm_a(h):
             nc.vector.tensor_copy(
-                out=a_w[:, k, 1024 * h : 1024 * h + 1024].rearrange("p (t m b) -> p t m b", t=4, b=2),
-                in_=a_raw[:, k, 1024 * h : 1024 * h + 1024].rearrange("p (m t b) -> p t m b", t=4, b=2),
+                out=a_w[h][:].bitcast(U16).rearrange("p g (t m) -> p g t m", t=4),
+                in_=a_raw[h][:].bitcast(U16).rearrange("p g (m t) -> p g t m", t=4),
             )
             nc.vector.tensor_copy(
-                out=a_s[:, k, 512 * h : 512 * h + 512].rearrange("p (t m) -> p t m", t=4),
-                in_=a_sraw[:, k, 512 * h : 512 * h + 512].rearrange("p (m t) -> p t m", t=4),
+                out=a_s[h][:].rearrange("p g (t m) -> p g t m", t=4),
+                in_=a_sraw[:, :, H * h : H * h + H].rearrange("p g (m t) -> p g t m", t=4),
             )
 
         def perm_b():
             nc.vector.tensor_copy(
-                out=b_w[:].rearrange("p (t m b) -> p t m b", t=4, b=2),
-                in_=b_raw[:].rearrange("p (m t b) -> p t m b", t=4, b=2),
+                out=b_w[:].bitcast(U16).rearrange("p (t m) -> p t m", t=4),
+                in_=b_raw[:].bitcast(U16).rearrange("p (m t) -> p t m", t=4),
             )
             nc.vector.tensor_copy(
                 out=b_s[:].rearrange("p (t m) -> p t m", t=4),
@@ -119,36 +122,45 @@ def tile_parcel_band_hemisphere_coupling_t2_kernel(
 
         xg, xc, xsc = {}, {}, {}
 
-        def x_interleave(w, k, lo, hi, on_vector):
-            if (w, k) not in xg:
-                g = work.tile([NP, F, 4], BF16, name="xg_%d_%d" % (w, k), tag="xg", bufs=3, align_bytes=64)
-                xg[w, k] = g
-            dst = xg[w, k][:, lo:hi, :].rearrange("p (c i) t -> p c t i", i=4)
+        def x_interleave(v, lo, hi, eng):
+            w, k = divmod(v, 2)
+            if v not in xg:
+                xg[v] = work.tile([NP, F, 4], BF16, name="xg_%d" % v, tag="xg", bufs=4, align_bytes=64)
+            dst = xg[v][:, lo:hi, :].rearrange("p (c i) t -> p c t i", i=4)
             src = xs[w, k][:, :, lo:hi].rearrange("p t (c i) -> p c t i", i=4)
-            if on_vector:
+            if eng == "V":
                 nc.vector.tensor_copy(out=dst, in_=src)
+            elif eng == "G":
+                nc.gpsimd.tensor_scalar(
+                    out=xg[v][:, lo:hi, :],
+                    in0=xs[w, k][:, :, lo:hi].rearrange("p t c -> p c t"),
+                    scalar1=1.0,
+                    scalar2=0.0,
+                    op0=ALU.mult,
+                    op1=ALU.add,
+                )
             else:
                 nc.scalar.copy(out=dst, in_=src)
 
-        def x_quantize(w, k):
-            c = work.tile([NP, F], U32, name="xc_%d_%d" % (w, k), tag="xc", bufs=4, align_bytes=64)
-            s = work.tile([NP, F], U8, name="xsc_%d_%d" % (w, k), tag="xsc", bufs=4, align_bytes=64)
-            nc.vector.quantize_mx(out=c[:].bitcast(FP8X4), scales=s[:], in_=xg[w, k][:].rearrange("p f t -> p (f t)"))
-            xc[w, k], xsc[w, k] = c, s
+        def x_quantize(v):
+            c = work.tile([NP, F], U32, name="xc_%d" % v, tag="xc", bufs=6, align_bytes=64)
+            s = work.tile([NP, F], U8, name="xsc_%d" % v, tag="xsc", bufs=6, align_bytes=64)
+            nc.vector.quantize_mx(out=c[:].bitcast(FP8X4), scales=s[:], in_=xg[v][:].rearrange("p f t -> p (f t)"))
+            xc[v], xsc[v] = c, s
 
-        d, h1, h1t, h1g, h1c, h1s, e, h2g, h2c, h2s, o = ({} for i in range(11))
+        d, h1, h1t, h1g, h1c, h1s, e, h2g, h2c, h2s, o, raw = ({} for i in range(12))
 
         def mm1(i):
             u, t = divmod(i, 4)
             w, h = divmod(u, 2)
-            acc = psum.tile([NP, F], F32, name="d_%d" % i, tag="d", bufs=2)
+            acc = psum.tile([NP, F], F32, name="d_%d" % i, tag="vb_%d" % t, bufs=1)
             for k in range(2):
                 nc.tensor.matmul_mx(
                     out=acc[:],
-                    lhsT=a_w[:, k, 1024 * h + 256 * t : 1024 * h + 256 * t + 256].bitcast(FP4X4),
-                    lhsT_scale=a_s[:, k, 512 * h + 128 * t : 512 * h + 128 * t + 128],
-                    rhs=xc[w, k][:].bitcast(FP8X4),
-                    rhs_scale=xsc[w, k][:],
+                    lhsT=a_w[h][:, k, 256 * t : 256 * t + 256].bitcast(FP4X4),
+                    lhsT_scale=a_s[h][:, k, NP * t : NP * t + NP],
+                    rhs=xc[2 * w + k][:].bitcast(FP8X4),
+                    rhs_scale=xsc[2 * w + k][:],
                     start=(k == 0),
                     stop=(k == 1),
                 )
@@ -158,8 +170,7 @@ def tile_parcel_band_hemisphere_coupling_t2_kernel(
             u, t = divmod(i, 4)
             w, h = divmod(u, 2)
             if t == 0:
-                tile = work.tile([NP, 4, F], F32, name="h1_%d" % u, tag="h1", bufs=4)
-                h1[u] = tile
+                h1[u] = work.tile([NP, 4, F], F32, name="h1_%d" % u, tag="h1", bufs=4)
             nc.vector.scalar_tensor_tensor(
                 out=h1[u][:, t, :].rearrange("p (t m) -> p t m", t=4),
                 in0=d[i][:].rearrange("p (m t) -> p t m", t=4),
@@ -171,7 +182,7 @@ def tile_parcel_band_hemisphere_coupling_t2_kernel(
 
         def turn(i):
             u, t = divmod(i, 4)
-            bank = psum.tile([NP, 4, NP], F32, name="h1t_%d" % i, tag="h1t", bufs=2)
+            bank = psum.tile([NP, 4, NP], F32, name="h1t_%d" % i, tag="sb_%d" % TB[t], bufs=1)
             for b in range(4):
                 nc.tensor.transpose(bank[:, b, :], h1[u][:, t, NP * b : NP * b + NP], ident[:])
             h1t[i] = bank
@@ -179,8 +190,7 @@ def tile_parcel_band_hemisphere_coupling_t2_kernel(
         def gather1(i):
             u, t = divmod(i, 4)
             if t == 0:
-                tile = work.tile([NP, F, 4], BF16, name="h1g_%d" % u, tag="h1g", bufs=2, align_bytes=64)
-                h1g[u] = tile
+                h1g[u] = work.tile([NP, F, 4], BF16, name="h1g_%d" % u, tag="h1g", bufs=2, align_bytes=64)
             nc.scalar.copy(
                 out=h1g[u][:, NP * t : NP * t + NP, :],
                 in_=h1t[i][:].rearrange("p t q -> p q t"),
@@ -194,7 +204,7 @@ def tile_parcel_band_hemisphere_coupling_t2_kernel(
 
         def mm2(i):
             u, b = divmod(i, 4)
-            bank = psum.tile([NP, 4, NP], F32, name="e_%d" % i, tag="e", bufs=2)
+            bank = psum.tile([NP, 4, NP], F32, name="e_%d" % i, tag="vb_%d" % b, bufs=1)
             for t in range(4):
                 nc.tensor.matmul_mx(
                     out=bank[:, t, :],
@@ -210,8 +220,7 @@ def tile_parcel_band_hemisphere_coupling_t2_kernel(
         def add2(i):
             u, b = divmod(i, 4)
             if b == 0:
-                tile = work.tile([NP, F, 4], BF16, name="h2g_%d" % u, tag="h2g", bufs=2, align_bytes=64)
-                h2g[u] = tile
+                h2g[u] = work.tile([NP, F, 4], BF16, name="h2g_%d" % u, tag="h2g", bufs=2, align_bytes=64)
             cols = slice(NP * b, NP * b + NP)
             nc.vector.tensor_tensor(
                 out=h2g[u][:, cols, :].rearrange("p (a i) t -> p a t i", i=4),
@@ -229,7 +238,7 @@ def tile_parcel_band_hemisphere_coupling_t2_kernel(
         def mm3(i):
             u, m = divmod(i, 4)
             g = u % 2
-            bank = psum.tile([NP, F], F32, name="o_%d" % i, tag="o", bufs=2)
+            bank = psum.tile([NP, F], F32, name="o_%d" % i, tag="sb_%d" % OB[m], bufs=1)
             nc.tensor.matmul_mx(
                 out=bank[:],
                 lhsT=c_w[:, g, 256 * m : 256 * m + 256].bitcast(FP4X4),
@@ -241,78 +250,121 @@ def tile_parcel_band_hemisphere_coupling_t2_kernel(
             )
             o[i] = bank
 
-        def finish(i):
+        def store(i, count, res):
             u, m = divmod(i, 4)
             w, g = divmod(u, 2)
-            res = work.tile([NP, F], F32, name="res_%d" % i, tag="res", bufs=6)
-            if i in OE_V:
-                nc.vector.tensor_tensor(
-                    out=res[:].rearrange("p (m t) -> p m t", t=4),
-                    in0=o[i][:].rearrange("p (t m) -> p m t", t=4),
-                    in1=gain_b[:].rearrange("p (m t) -> p m t", t=4),
-                    op=ALU.mult,
-                )
-            else:
-                raw = work.tile([NP, F], F32, name="raw_%d" % i, tag="raw", bufs=4)
-                nc.scalar.copy(
-                    out=raw[:].rearrange("p (m t) -> p m t", t=4),
-                    in_=o[i][:].rearrange("p (t m) -> p m t", t=4),
-                )
-                for part in range(2):
-                    cols = slice(256 * part, 256 * part + 256)
-                    nc.gpsimd.tensor_tensor(out=res[:, cols], in0=raw[:, cols], in1=gain_b[:, cols], op=ALU.mult)
-            nc.sync.dma_start(out=outs[g][NP * m : NP * m + NP, w, :], in_=res[:])
+            nc.sync.dma_start(
+                out=outs[g][NP * m : NP * (m + count), w, :].rearrange("(m p) f -> p m f", p=NP),
+                in_=res,
+            )
 
-        x_interleave(0, 0, 0, SPLIT, False)
-        x_interleave(0, 1, 0, SPLIT, False)
-        x_interleave(0, 0, SPLIT, F, True)
-        perm_a(0, 0)
-        x_quantize(0, 0)
-        x_interleave(0, 1, SPLIT, F, True)
-        perm_a(0, 1)
-        x_quantize(0, 1)
+        def finish_vector(i):
+            res = work.tile([NP, 1, F], F32, name="res_%d" % i, tag="res", bufs=8)
+            nc.vector.tensor_tensor(
+                out=res[:, 0, :].rearrange("p (m t) -> p m t", t=4),
+                in0=o[i][:].rearrange("p (t m) -> p m t", t=4),
+                in1=gain_b[:].rearrange("p (m t) -> p m t", t=4),
+                op=ALU.mult,
+            )
+            store(i, 1, res[:])
 
-        n = 32
+        def empty3(i):
+            u, m = divmod(i, 4)
+            if u not in raw:
+                raw[u] = work.tile([NP, 4, F], F32, name="raw_%d" % u, tag="raw", bufs=3)
+            nc.scalar.copy(
+                out=raw[u][:, m, :].rearrange("p (m t) -> p m t", t=4),
+                in_=o[i][:].rearrange("p (t m) -> p m t", t=4),
+            )
 
-        def ok(i):
-            return 0 <= i < n
+        def scale3(i, count):
+            u, m = divmod(i, 4)
+            part = raw[u][:, m : m + count, :]
+            nc.gpsimd.tensor_tensor(
+                out=part, in0=part, in1=gain_b[:].unsqueeze(1).to_broadcast([NP, count, F]), op=ALU.mult
+            )
+            store(i, count, part)
 
-        for s in range(n + L3):
-            i, j = s, s - LT
-            w, r = s // 8 + 1, s % 8
-            turns = [v for v in range(j - RUN + 1, j + 1) if ok(v)] if j % RUN == RUN - 1 else []
-            for v in turns:
-                turn(v)
-            if ok(s - L3):
-                mm3(s - L3)
-            if ok(s - L2):
-                mm2(s - L2)
-            if ok(i):
-                mm1(i)
-            if s == 2:
-                perm_a(1, 0)
-                perm_a(1, 1)
-            if s == 5:
+        x_interleave(0, 0, SPLIT, "S")
+        x_interleave(1, 0, SPLIT, "S")
+        perm_a(0)
+        x_interleave(0, SPLIT, F, "V")
+        x_interleave(1, SPLIT, F, "V")
+        x_quantize(0)
+        x_quantize(1)
+        pieces = list(range(8, 32))
+
+        def x_pieces(count):
+            for c in pieces[:count]:
+                x_interleave(c // 4, NP * (c % 4), NP * (c % 4) + NP, "S")
+                pieces.remove(c)
+
+        x_pieces(X0)
+        for t in range(3):
+            mm1(t)
+        perm_a(1)
+
+        def ok(u):
+            return 0 <= u < 8
+
+        for k in range(10):
+            u1, u2 = k - 1, k - 2
+            n_g = 3 if k < 8 else 2 if k == 8 else 0
+            if k > 0:
+                for v in range(2, 8):
+                    if QX[v - 2] == k:
+                        x_quantize(v)
+            if ok(u2):
+                quant2(u2)
+            if ok(u1):
+                quant1(u1)
+            if ok(u2):
+                for t in range(4):
+                    mm3(4 * u2 + t)
+                    if t < n_g:
+                        empty3(4 * u2 + t)
+                if n_g == 3:
+                    scale3(4 * u2, 1)
+                    scale3(4 * u2 + 1, 2)
+                if n_g == 2:
+                    scale3(4 * u2, 2)
+            x_pieces(XN[0] if k < 2 else XN[1])
+            if ok(k):
+                mm1(4 * k + 3)
+                add1(4 * k)
+                add1(4 * k + 1)
+            if ok(u1):
+                mm2(4 * u1)
+                mm2(4 * u1 + 1)
+            if ok(k):
+                turn(4 * k)
+                turn(4 * k + 1)
+                add1(4 * k + 2)
+                add1(4 * k + 3)
+            if k == 0:
                 perm_b()
-            if w < T:
-                for c in range(2 * XCH):
-                    if c * XQ_AT[1] // (2 * XCH) == r:
-                        k, cc = divmod(c, XCH)
-                        x_interleave(w, k, F // XCH * cc, F // XCH * (cc + 1), False)
-            for v in turns:
-                gather1(v)
-            for u in range(8):
-                if 4 * u + 3 + LT == s - Q1LAG:
-                    quant1(u)
-            if w < T:
-                for k in range(2):
-                    if XQ_AT[k] == r:
-                        x_quantize(w, k)
-            if ok(s - L2):
-                add2(s - L2)
-            if ok(i):
-                add1(i)
-            if ok(s - L2) and (s - L2) % 4 == 3:
-                quant2((s - L2) // 4)
-            if ok(s - L3):
-                finish(s - L3)
+                for v in range(2, 8):
+                    if QX[v - 2] == k:
+                        x_quantize(v)
+            if ok(u2) and k >= 8:
+                for t in range(n_g, 3):
+                    finish_vector(4 * u2 + t)
+            if ok(u1):
+                for t in range(2, 4):
+                    mm2(4 * u1 + t)
+            if ok(k):
+                gather1(4 * k)
+                gather1(4 * k + 1)
+                x_pieces(XN[2])
+                turn(4 * k + 2)
+                turn(4 * k + 3)
+                gather1(4 * k + 2)
+                gather1(4 * k + 3)
+            for t in range(4):
+                if ok(u1):
+                    add2(4 * u1 + t)
+                if ok(k + 1) and t < 3:
+                    mm1(4 * k + 4 + t)
+            if ok(u2):
+                finish_vector(4 * u2 + 3)
+            x_pieces(XN[3])

@@ -18,11 +18,8 @@ ALU = mybir.AluOpType
 
 NP = 128
 SPLIT = 192
-TB = (0, 1, 2, 0)
-OB = (0, 1, 2, 3)
-X0 = 6
-XN = (1, 1, 1, 2)
-QX = (0, 1, 2, 3, 4, 5)
+SPLIT1 = 256
+TAILG = 2
 
 
 def tile_parcel_band_hemisphere_coupling_t2_kernel(
@@ -73,12 +70,12 @@ def tile_parcel_band_hemisphere_coupling_t2_kernel(
             )
 
         load_a(0)
+        load_x(0, 0)
         for q in range(4):
             nc.sync.dma_start(
                 out=a_sraw[32 * q : 32 * q + 4].bitcast(I32),
                 in_=sc_scales.bitcast(I32)[:, 4 * q : 4 * q + 4, :].rearrange("g q n -> q g n"),
             )
-        load_x(0, 0)
         load_x(0, 1)
         load_a(1)
         load_x(1, 0)
@@ -100,11 +97,13 @@ def tile_parcel_band_hemisphere_coupling_t2_kernel(
             for k in range(2):
                 load_x(w, k)
 
-        def perm_a(h):
+        def perm_aw(h):
             nc.vector.tensor_copy(
                 out=a_w[h][:].bitcast(U16).rearrange("p g (t m) -> p g t m", t=4),
                 in_=a_raw[h][:].bitcast(U16).rearrange("p g (m t) -> p g t m", t=4),
             )
+
+        def perm_as(h):
             nc.vector.tensor_copy(
                 out=a_s[h][:].rearrange("p g (t m) -> p g t m", t=4),
                 in_=a_sraw[:, :, H * h : H * h + H].rearrange("p g (m t) -> p g t m", t=4),
@@ -150,10 +149,20 @@ def tile_parcel_band_hemisphere_coupling_t2_kernel(
 
         d, h1, h1t, h1g, h1c, h1s, e, h2g, h2c, h2s, o, raw = ({} for i in range(12))
 
+        free_banks = ["bank_%d" % b for b in range(8)]
+        bank_of = {}
+
+        def take_bank(kind, i):
+            bank_of[kind, i] = free_banks.pop(0)
+            return bank_of[kind, i]
+
+        def give_bank(kind, i):
+            free_banks.append(bank_of[kind, i])
+
         def mm1(i):
             u, t = divmod(i, 4)
             w, h = divmod(u, 2)
-            acc = psum.tile([NP, F], F32, name="d_%d" % i, tag="vb_%d" % t, bufs=1)
+            acc = psum.tile([NP, F], F32, name="d_%d" % i, tag=take_bank("d", i), bufs=1)
             for k in range(2):
                 nc.tensor.matmul_mx(
                     out=acc[:],
@@ -179,10 +188,11 @@ def tile_parcel_band_hemisphere_coupling_t2_kernel(
                 op0=ALU.max,
                 op1=ALU.add,
             )
+            give_bank("d", i)
 
         def turn(i):
             u, t = divmod(i, 4)
-            bank = psum.tile([NP, 4, NP], F32, name="h1t_%d" % i, tag="sb_%d" % TB[t], bufs=1)
+            bank = psum.tile([NP, 4, NP], F32, name="h1t_%d" % i, tag=take_bank("t", i), bufs=1)
             for b in range(4):
                 nc.tensor.transpose(bank[:, b, :], h1[u][:, t, NP * b : NP * b + NP], ident[:])
             h1t[i] = bank
@@ -195,6 +205,7 @@ def tile_parcel_band_hemisphere_coupling_t2_kernel(
                 out=h1g[u][:, NP * t : NP * t + NP, :],
                 in_=h1t[i][:].rearrange("p t q -> p q t"),
             )
+            give_bank("t", i)
 
         def quant1(u):
             c = work.tile([NP, F], U32, name="h1c_%d" % u, tag="h1c", bufs=3, align_bytes=64)
@@ -204,7 +215,7 @@ def tile_parcel_band_hemisphere_coupling_t2_kernel(
 
         def mm2(i):
             u, b = divmod(i, 4)
-            bank = psum.tile([NP, 4, NP], F32, name="e_%d" % i, tag="vb_%d" % b, bufs=1)
+            bank = psum.tile([NP, 4, NP], F32, name="e_%d" % i, tag=take_bank("e", i), bufs=1)
             for t in range(4):
                 nc.tensor.matmul_mx(
                     out=bank[:, t, :],
@@ -220,14 +231,15 @@ def tile_parcel_band_hemisphere_coupling_t2_kernel(
         def add2(i):
             u, b = divmod(i, 4)
             if b == 0:
-                h2g[u] = work.tile([NP, F, 4], BF16, name="h2g_%d" % u, tag="h2g", bufs=2, align_bytes=64)
+                h2g[u] = work.tile([NP, F, 4], BF16, name="h2g_%d" % u, tag="h2g_%d" % (u % 3), bufs=1, align_bytes=64)
             cols = slice(NP * b, NP * b + NP)
             nc.vector.tensor_tensor(
-                out=h2g[u][:, cols, :].rearrange("p (a i) t -> p a t i", i=4),
-                in0=e[i][:].rearrange("p t (a i) -> p a t i", i=4),
-                in1=h1[u][:, :, cols].rearrange("p t (a i) -> p a t i", i=4),
+                out=h2g[u][:, cols, :].rearrange("p (a i) t -> p a t i", i=2),
+                in0=e[i][:].rearrange("p t (a i) -> p a t i", i=2),
+                in1=h1[u][:, :, cols].rearrange("p t (a i) -> p a t i", i=2),
                 op=ALU.add,
             )
+            give_bank("e", i)
 
         def quant2(u):
             c = work.tile([NP, F], U32, name="h2c_%d" % u, tag="h2c", bufs=3, align_bytes=64)
@@ -238,7 +250,7 @@ def tile_parcel_band_hemisphere_coupling_t2_kernel(
         def mm3(i):
             u, m = divmod(i, 4)
             g = u % 2
-            bank = psum.tile([NP, F], F32, name="o_%d" % i, tag="sb_%d" % OB[m], bufs=1)
+            bank = psum.tile([NP, F], F32, name="o_%d" % i, tag=take_bank("o", i), bufs=1)
             nc.tensor.matmul_mx(
                 out=bank[:],
                 lhsT=c_w[:, g, 256 * m : 256 * m + 256].bitcast(FP4X4),
@@ -250,10 +262,10 @@ def tile_parcel_band_hemisphere_coupling_t2_kernel(
             )
             o[i] = bank
 
-        def store(i, count, res):
+        def store(i, count, res, queue=nc.sync):
             u, m = divmod(i, 4)
             w, g = divmod(u, 2)
-            nc.sync.dma_start(
+            queue.dma_start(
                 out=outs[g][NP * m : NP * (m + count), w, :].rearrange("(m p) f -> p m f", p=NP),
                 in_=res,
             )
@@ -266,6 +278,7 @@ def tile_parcel_band_hemisphere_coupling_t2_kernel(
                 in1=gain_b[:].rearrange("p (m t) -> p m t", t=4),
                 op=ALU.mult,
             )
+            give_bank("o", i)
             store(i, 1, res[:])
 
         def empty3(i):
@@ -276,95 +289,103 @@ def tile_parcel_band_hemisphere_coupling_t2_kernel(
                 out=raw[u][:, m, :].rearrange("p (m t) -> p m t", t=4),
                 in_=o[i][:].rearrange("p (t m) -> p m t", t=4),
             )
+            give_bank("o", i)
 
-        def scale3(i, count):
+        def scale3(i, count, after=None):
             u, m = divmod(i, 4)
             part = raw[u][:, m : m + count, :]
+            if after is None:
+                res = part
+            else:
+                late = work.tile([NP, count, F], F32, name="late_%d" % i, tag="h2g_%d" % (after % 3), bufs=1, align_bytes=64)
+                res = late[:]
             nc.gpsimd.tensor_tensor(
-                out=part, in0=part, in1=gain_b[:].unsqueeze(1).to_broadcast([NP, count, F]), op=ALU.mult
+                out=res, in0=part, in1=gain_b[:].unsqueeze(1).to_broadcast([NP, count, F]), op=ALU.mult
             )
-            store(i, count, part)
+            store(i, count, res, nc.scalar if after == 7 else nc.sync)
 
         x_interleave(0, 0, SPLIT, "S")
-        x_interleave(1, 0, SPLIT, "S")
-        perm_a(0)
+        x_interleave(1, 0, SPLIT1, "S")
+        perm_aw(0)
         x_interleave(0, SPLIT, F, "V")
-        x_interleave(1, SPLIT, F, "V")
+        perm_as(0)
         x_quantize(0)
+        x_interleave(1, SPLIT1, F, "V")
+        perm_aw(1)
         x_quantize(1)
-        pieces = list(range(8, 32))
-
-        def x_pieces(count):
-            for c in pieces[:count]:
-                x_interleave(c // 4, NP * (c % 4), NP * (c % 4) + NP, "S")
-                pieces.remove(c)
-
-        x_pieces(X0)
-        for t in range(3):
+        perm_as(1)
+        x_interleave(2, 0, F, "S")
+        for t in range(4):
             mm1(t)
-        perm_a(1)
 
         def ok(u):
             return 0 <= u < 8
 
-        for k in range(10):
-            u1, u2 = k - 1, k - 2
-            n_g = 3 if k < 8 else 2 if k == 8 else 0
-            if k > 0:
-                for v in range(2, 8):
-                    if QX[v - 2] == k:
-                        x_quantize(v)
-            if ok(u2):
-                quant2(u2)
+        for k in range(8):
+            u1, u2, u3 = k - 1, k - 2, k - 3
             if ok(u1):
                 quant1(u1)
+            if k >= 3 and ok(k + 2):
+                x_quantize(k + 2)
             if ok(u2):
-                for t in range(4):
-                    mm3(4 * u2 + t)
-                    if t < n_g:
-                        empty3(4 * u2 + t)
-                if n_g == 3:
-                    scale3(4 * u2, 1)
-                    scale3(4 * u2 + 1, 2)
-                if n_g == 2:
-                    scale3(4 * u2, 2)
-            x_pieces(XN[0] if k < 2 else XN[1])
-            if ok(k):
-                mm1(4 * k + 3)
-                add1(4 * k)
-                add1(4 * k + 1)
+                quant2(u2)
+            if k == 2:
+                x_quantize(4)
+            if ok(u3):
+                scale3(4 * u3 + 2, 1, u2)
             if ok(u1):
                 mm2(4 * u1)
                 mm2(4 * u1 + 1)
-            if ok(k):
-                turn(4 * k)
-                turn(4 * k + 1)
-                add1(4 * k + 2)
-                add1(4 * k + 3)
+            for t in range(6):
+                if ok(u2) and t < 4:
+                    mm3(4 * u2 + t)
+                if ok(u2) and t >= 3:
+                    empty3(4 * u2 + t - 3)
+                if 1 <= t < 5:
+                    add1(4 * k + t - 1)
+            if ok(u2):
+                scale3(4 * u2, 2)
             if k == 0:
                 perm_b()
-                for v in range(2, 8):
-                    if QX[v - 2] == k:
-                        x_quantize(v)
-            if ok(u2) and k >= 8:
-                for t in range(n_g, 3):
-                    finish_vector(4 * u2 + t)
-            if ok(u1):
-                for t in range(2, 4):
-                    mm2(4 * u1 + t)
-            if ok(k):
-                gather1(4 * k)
-                gather1(4 * k + 1)
-                x_pieces(XN[2])
-                turn(4 * k + 2)
-                turn(4 * k + 3)
-                gather1(4 * k + 2)
-                gather1(4 * k + 3)
+                x_quantize(2)
             for t in range(4):
-                if ok(u1):
-                    add2(4 * u1 + t)
-                if ok(k + 1) and t < 3:
-                    mm1(4 * k + 4 + t)
+                turn(4 * k + t)
+                gather1(4 * k + t)
+                if t == 1 and ok(u1):
+                    add2(4 * u1)
+                    add2(4 * u1 + 1)
             if ok(u2):
                 finish_vector(4 * u2 + 3)
-            x_pieces(XN[3])
+            if k < 2:
+                x_interleave(k + 3, 0, F, "S")
+            if k >= 1 and ok(k + 4):
+                x_interleave(k + 4, 0, F, "S")
+            if k == 1:
+                x_quantize(3)
+            if ok(u1):
+                mm2(4 * u1 + 2)
+                mm2(4 * u1 + 3)
+                add2(4 * u1 + 2)
+                add2(4 * u1 + 3)
+            if ok(k + 1):
+                for t in range(4):
+                    mm1(4 * k + 4 + t)
+
+        quant1(7)
+        quant2(6)
+        scale3(4 * 5 + 2, 1, 6)
+        for t in range(4):
+            mm2(28 + t)
+        for t in range(4):
+            mm3(24 + t)
+            if t < TAILG:
+                empty3(24 + t)
+            add2(28 + t)
+        finish_vector(27)
+        quant2(7)
+        scale3(24, TAILG, 7)
+        for t in range(TAILG, 3):
+            finish_vector(24 + t)
+        for t in range(4):
+            mm3(28 + t)
+            finish_vector(28 + t)

@@ -18,8 +18,9 @@ ALU = mybir.AluOpType
 
 NP = 128
 SPLIT = 192
-SPLIT1 = 256
-TAILG = 2
+SPLIT1 = 240
+K0 = 2
+G_EXTRA = 256
 
 
 def tile_parcel_band_hemisphere_coupling_t2_kernel(
@@ -40,13 +41,12 @@ def tile_parcel_band_hemisphere_coupling_t2_kernel(
             a_w[h] = keep.tile([NP, 2, P], U8, name="a_w_%d" % h, align_bytes=64)
             a_s[h] = keep.tile([NP, 2, H], U8, name="a_s_%d" % h, align_bytes=64)
         a_sraw = keep.tile([NP, 2, P], U8, name="a_sraw", align_bytes=64)
-        b_raw = keep.tile([NP, 2 * F], U8, name="b_raw", align_bytes=64)
-        b_sraw = keep.tile([NP, F], U8, name="b_sraw", align_bytes=64)
         b_w = keep.tile([NP, 2 * F], U8, name="b_w", align_bytes=64)
-        b_s = keep.tile([NP, F], U8, name="b_s", align_bytes=64)
+        b_s = keep.tile([NP, 1, F], U8, name="b_s", align_bytes=64)
         c_w = keep.tile([NP, 2, 2 * H], U8, name="c_w", align_bytes=64)
         c_s = keep.tile([NP, 2, H], U8, name="c_s", align_bytes=64)
-        gain_b = keep.tile([NP, F], BF16, name="gain_b")
+        gain_t = keep.tile([NP, 2 * F], BF16, name="gain_t")
+        gain_b = gain_t[:, :F]
         xs = {}
         for w in range(T):
             for k in range(2):
@@ -54,7 +54,7 @@ def tile_parcel_band_hemisphere_coupling_t2_kernel(
                 xs[w, k] = xt
 
         nc.vector.memset(a_sraw[:].bitcast(I32), 0)
-        nc.vector.memset(b_sraw[:].bitcast(I32), 0)
+        nc.vector.memset(b_s[:].bitcast(I32), 0)
         nc.vector.memset(c_s[:].bitcast(I32), 0)
         make_identity(nc, ident[:])
 
@@ -69,38 +69,34 @@ def tile_parcel_band_hemisphere_coupling_t2_kernel(
                 in_=a_src[:, :, 256 * h : 256 * h + 256].rearrange("g p n -> p g n"),
             )
 
-        load_a(0)
-        load_x(0, 0)
-        for q in range(4):
-            nc.sync.dma_start(
-                out=a_sraw[32 * q : 32 * q + 4].bitcast(I32),
-                in_=sc_scales.bitcast(I32)[:, 4 * q : 4 * q + 4, :].rearrange("g q n -> q g n"),
-            )
-        load_x(0, 1)
-        load_a(1)
-        load_x(1, 0)
-        nc.sync.dma_start(out=b_raw[:].bitcast(I32), in_=fb_words.bitcast(I32)[0])
-        for q in range(4):
-            nc.sync.dma_start(
-                out=b_sraw[32 * q : 32 * q + 4].bitcast(I32),
-                in_=fb_scales.bitcast(I32)[0, 4 * q : 4 * q + 4, :],
-            )
-        load_x(1, 1)
-        nc.sync.dma_start(out=c_w[:].bitcast(I32), in_=hs_words.bitcast(I32).rearrange("g p n -> p g n"))
-        for q in range(4):
-            nc.sync.dma_start(
-                out=c_s[32 * q : 32 * q + 4].bitcast(I32),
-                in_=hs_scales.bitcast(I32)[:, 4 * q : 4 * q + 4, :].rearrange("g q n -> q g n"),
-            )
-        nc.sync.dma_start(out=gain_b[:], in_=gain.partition_broadcast(NP))
-        for w in (2, 3):
-            for k in range(2):
-                load_x(w, k)
+        def load_scales(dst, src):
+            for q in range(4):
+                nc.sync.dma_start(
+                    out=dst[32 * q : 32 * q + 4].bitcast(I32),
+                    in_=src.bitcast(I32)[:, 4 * q : 4 * q + 4, :].rearrange("g q n -> q g n"),
+                )
 
-        def perm_aw(h):
+        load_a(0)
+        load_scales(a_sraw, sc_scales)
+        load_x(0, 0)
+        load_x(0, 1)
+        load_x(1, 0)
+        load_a(1)
+        load_x(1, 1)
+        load_scales(b_s, fb_scales)
+        load_scales(c_s, hs_scales)
+        nc.sync.dma_start(out=b_w[:].bitcast(I32), in_=fb_words.bitcast(I32)[0])
+        load_x(2, 0)
+        load_x(2, 1)
+        load_x(3, 0)
+        load_x(3, 1)
+        nc.sync.dma_start(out=c_w[:].bitcast(I32), in_=hs_words.bitcast(I32).rearrange("g p n -> p g n"))
+        nc.sync.dma_start(out=gain_b, in_=gain.partition_broadcast(NP))
+
+        def perm_aw(h, lo=0, hi=4):
             nc.vector.tensor_copy(
-                out=a_w[h][:].bitcast(U16).rearrange("p g (t m) -> p g t m", t=4),
-                in_=a_raw[h][:].bitcast(U16).rearrange("p g (m t) -> p g t m", t=4),
+                out=a_w[h][:].bitcast(U16).rearrange("p g (t m) -> p g t m", t=4)[:, :, lo:hi, :],
+                in_=a_raw[h][:].bitcast(U16).rearrange("p g (m t) -> p g t m", t=4)[:, :, lo:hi, :],
             )
 
         def perm_as(h):
@@ -109,45 +105,45 @@ def tile_parcel_band_hemisphere_coupling_t2_kernel(
                 in_=a_sraw[:, :, H * h : H * h + H].rearrange("p g (m t) -> p g t m", t=4),
             )
 
-        def perm_b():
-            nc.vector.tensor_copy(
-                out=b_w[:].bitcast(U16).rearrange("p (t m) -> p t m", t=4),
-                in_=b_raw[:].bitcast(U16).rearrange("p (m t) -> p t m", t=4),
-            )
-            nc.vector.tensor_copy(
-                out=b_s[:].rearrange("p (t m) -> p t m", t=4),
-                in_=b_sraw[:].rearrange("p (m t) -> p t m", t=4),
-            )
+        xg, xc, xsc, xslot = {}, {}, {}, {}
 
-        xg, xc, xsc = {}, {}, {}
-
-        def x_interleave(v, lo, hi, eng):
+        def x_interleave(v, lo, hi, eng, slot=None):
             w, k = divmod(v, 2)
-            if v not in xg:
-                xg[v] = work.tile([NP, F, 4], BF16, name="xg_%d" % v, tag="xg", bufs=4, align_bytes=64)
-            dst = xg[v][:, lo:hi, :].rearrange("p (c i) t -> p c t i", i=4)
-            src = xs[w, k][:, :, lo:hi].rearrange("p t (c i) -> p c t i", i=4)
-            if eng == "V":
-                nc.vector.tensor_copy(out=dst, in_=src)
-            elif eng == "G":
+            if slot is not None:
+                tile = work.tile([NP, F, 4], BF16, name="xg_%d_%d" % (v, lo), tag=slot, bufs=1, align_bytes=64)
+                xg[v] = xg.get(v, []) + [(lo, tile)]
+                xslot[v] = slot
+            tile = xg[v][-1][1]
+            if eng == "G":
                 nc.gpsimd.tensor_scalar(
-                    out=xg[v][:, lo:hi, :],
+                    out=tile[:, lo:hi, :],
                     in0=xs[w, k][:, :, lo:hi].rearrange("p t c -> p c t"),
                     scalar1=1.0,
                     scalar2=0.0,
                     op0=ALU.mult,
                     op1=ALU.add,
                 )
+                return
+            dst = tile[:, lo:hi, :].rearrange("p (c i) t -> p c t i", i=4)
+            src = xs[w, k][:, :, lo:hi].rearrange("p t (c i) -> p c t i", i=4)
+            if eng == "V":
+                nc.vector.tensor_copy(out=dst, in_=src)
             else:
                 nc.scalar.copy(out=dst, in_=src)
 
         def x_quantize(v):
             c = work.tile([NP, F], U32, name="xc_%d" % v, tag="xc", bufs=6, align_bytes=64)
             s = work.tile([NP, F], U8, name="xsc_%d" % v, tag="xsc", bufs=6, align_bytes=64)
-            nc.vector.quantize_mx(out=c[:].bitcast(FP8X4), scales=s[:], in_=xg[v][:].rearrange("p f t -> p (f t)"))
+            width = F // len(xg[v])
+            for lo, tile in xg[v]:
+                nc.vector.quantize_mx(
+                    out=c[:, lo : lo + width].bitcast(FP8X4),
+                    scales=s[:, lo : lo + width],
+                    in_=tile[:, lo : lo + width, :].rearrange("p f t -> p (f t)"),
+                )
             xc[v], xsc[v] = c, s
 
-        d, h1, h1t, h1g, h1c, h1s, e, h2g, h2c, h2s, o, raw = ({} for i in range(12))
+        d, h1, h1t, h1g, h1c, h1s, e, h2g, h2c, h2s, o, raw, h1b = ({} for i in range(13))
 
         free_banks = ["bank_%d" % b for b in range(8)]
         bank_of = {}
@@ -159,11 +155,13 @@ def tile_parcel_band_hemisphere_coupling_t2_kernel(
         def give_bank(kind, i):
             free_banks.append(bank_of[kind, i])
 
-        def mm1(i):
+        def mm1(i, passes=(0, 1)):
             u, t = divmod(i, 4)
             w, h = divmod(u, 2)
-            acc = psum.tile([NP, F], F32, name="d_%d" % i, tag=take_bank("d", i), bufs=1)
-            for k in range(2):
+            if i not in d:
+                d[i] = psum.tile([NP, F], F32, name="d_%d" % i, tag=take_bank("d", i), bufs=1)
+            acc = d[i]
+            for k in passes:
                 nc.tensor.matmul_mx(
                     out=acc[:],
                     lhsT=a_w[h][:, k, 256 * t : 256 * t + 256].bitcast(FP4X4),
@@ -173,7 +171,6 @@ def tile_parcel_band_hemisphere_coupling_t2_kernel(
                     start=(k == 0),
                     stop=(k == 1),
                 )
-            d[i] = acc
 
         def add1(i):
             u, t = divmod(i, 4)
@@ -181,36 +178,47 @@ def tile_parcel_band_hemisphere_coupling_t2_kernel(
             if t == 0:
                 h1[u] = work.tile([NP, 4, F], F32, name="h1_%d" % u, tag="h1", bufs=4)
             nc.vector.scalar_tensor_tensor(
-                out=h1[u][:, t, :].rearrange("p (t m) -> p t m", t=4),
-                in0=d[i][:].rearrange("p (m t) -> p t m", t=4),
+                out=h1[u][:, t, :],
+                in0=d[i][:],
                 scalar=0.0,
-                in1=xs[w, h][:, t, :].rearrange("p (m t) -> p t m", t=4),
+                in1=xs[w, h][:, t, :],
                 op0=ALU.max,
                 op1=ALU.add,
             )
             give_bank("d", i)
 
-        def turn(i):
-            u, t = divmod(i, 4)
-            bank = psum.tile([NP, 4, NP], F32, name="h1t_%d" % i, tag=take_bank("t", i), bufs=1)
-            for b in range(4):
-                nc.tensor.transpose(bank[:, b, :], h1[u][:, t, NP * b : NP * b + NP], ident[:])
-            h1t[i] = bank
-
-        def gather1(i):
+        def round1(i):
             u, t = divmod(i, 4)
             if t == 0:
-                h1g[u] = work.tile([NP, F, 4], BF16, name="h1g_%d" % u, tag="h1g", bufs=2, align_bytes=64)
+                h1b[u] = work.tile([NP, 4, F], BF16, name="h1b_%d" % u, tag="h1b", bufs=2)
             nc.scalar.copy(
-                out=h1g[u][:, NP * t : NP * t + NP, :],
-                in_=h1t[i][:].rearrange("p t q -> p q t"),
+                out=h1b[u][:, t, :].rearrange("p (a m e) -> p a m e", a=2, e=2),
+                in_=h1[u][:, t, :].rearrange("p (m a e) -> p a m e", a=2, e=2),
             )
-            give_bank("t", i)
+
+        def turn(j):
+            u, c = divmod(j, 2)
+            bank = psum.tile([NP, 2, 2, NP], F32, name="h1t_%d" % j, tag=take_bank("t", j), bufs=1)
+            for t in range(2):
+                words = h1b[u][:, 2 * c + t, :].bitcast(F32)
+                for a in range(2):
+                    nc.tensor.transpose(bank[:, t, a, :], words[:, NP * a : NP * a + NP], ident[:])
+            h1t[j] = bank
+
+        def gather1(j):
+            u, c = divmod(j, 2)
+            if c == 0:
+                h1g[u] = work.tile([NP, 4, NP, 2], F32, name="h1g_%d" % u, tag="h1g_%d" % (u % 4), bufs=1, align_bytes=64)
+            nc.scalar.copy(
+                out=h1g[u][:, 2 * c : 2 * c + 2, :, :],
+                in_=h1t[j][:].rearrange("p t a q -> p t q a"),
+            )
+            give_bank("t", j)
 
         def quant1(u):
             c = work.tile([NP, F], U32, name="h1c_%d" % u, tag="h1c", bufs=3, align_bytes=64)
             s = work.tile([NP, F], U8, name="h1s_%d" % u, tag="h1s", bufs=3, align_bytes=64)
-            nc.vector.quantize_mx(out=c[:].bitcast(FP8X4), scales=s[:], in_=h1g[u][:].rearrange("p q t -> p (q t)"))
+            nc.vector.quantize_mx(out=c[:].bitcast(FP8X4), scales=s[:], in_=h1g[u][:].rearrange("p t q a -> p (t q a)").bitcast(BF16))
             h1c[u], h1s[u] = c, s
 
         def mm2(i):
@@ -222,7 +230,7 @@ def tile_parcel_band_hemisphere_coupling_t2_kernel(
                     lhsT=h1c[u][:, NP * t : NP * t + NP].bitcast(FP8X4),
                     lhsT_scale=h1s[u][:, NP * t : NP * t + NP],
                     rhs=b_w[:, 256 * b : 256 * b + 256].bitcast(FP4X4),
-                    rhs_scale=b_s[:, NP * b : NP * b + NP],
+                    rhs_scale=b_s[:, 0, NP * b : NP * b + NP],
                     start=True,
                     stop=True,
                 )
@@ -231,7 +239,7 @@ def tile_parcel_band_hemisphere_coupling_t2_kernel(
         def add2(i):
             u, b = divmod(i, 4)
             if b == 0:
-                h2g[u] = work.tile([NP, F, 4], BF16, name="h2g_%d" % u, tag="h2g_%d" % (u % 3), bufs=1, align_bytes=64)
+                h2g[u] = work.tile([NP, F, 4], BF16, name="h2g_%d" % u, tag="h2g", bufs=2, align_bytes=64)
             cols = slice(NP * b, NP * b + NP)
             nc.vector.tensor_tensor(
                 out=h2g[u][:, cols, :].rearrange("p (a i) t -> p a t i", i=2),
@@ -270,122 +278,172 @@ def tile_parcel_band_hemisphere_coupling_t2_kernel(
                 in_=res,
             )
 
-        def finish_vector(i):
-            res = work.tile([NP, 1, F], F32, name="res_%d" % i, tag="res", bufs=8)
+        def finish_vector(i, lo=0):
+            u, m = divmod(i, 4)
+            w, g = divmod(u, 2)
+            res = work.tile([NP, F - lo], F32, name="res_%d" % i, tag="res", bufs=8)
             nc.vector.tensor_tensor(
-                out=res[:, 0, :].rearrange("p (m t) -> p m t", t=4),
-                in0=o[i][:].rearrange("p (t m) -> p m t", t=4),
-                in1=gain_b[:].rearrange("p (m t) -> p m t", t=4),
+                out=res[:],
+                in0=o[i][:, lo:],
+                in1=gain_b[:, lo:],
                 op=ALU.mult,
             )
-            give_bank("o", i)
-            store(i, 1, res[:])
+            if lo == 0:
+                give_bank("o", i)
+            nc.sync.dma_start(out=outs[g][NP * m : NP * m + NP, w, lo:], in_=res[:])
 
-        def empty3(i):
+        def empty3(i, hi=F):
             u, m = divmod(i, 4)
             if u not in raw:
                 raw[u] = work.tile([NP, 4, F], F32, name="raw_%d" % u, tag="raw", bufs=3)
             nc.scalar.copy(
-                out=raw[u][:, m, :].rearrange("p (m t) -> p m t", t=4),
-                in_=o[i][:].rearrange("p (t m) -> p m t", t=4),
+                out=raw[u][:, m, :hi],
+                in_=o[i][:, :hi],
             )
             give_bank("o", i)
 
-        def scale3(i, count, after=None):
+        def scale_now(i, count):
             u, m = divmod(i, 4)
             part = raw[u][:, m : m + count, :]
-            if after is None:
-                res = part
-            else:
-                late = work.tile([NP, count, F], F32, name="late_%d" % i, tag="h2g_%d" % (after % 3), bufs=1, align_bytes=64)
-                res = late[:]
             nc.gpsimd.tensor_tensor(
-                out=res, in0=part, in1=gain_b[:].unsqueeze(1).to_broadcast([NP, count, F]), op=ALU.mult
+                out=part, in0=part, in1=gain_b.unsqueeze(1).to_broadcast([NP, count, F]), op=ALU.mult
             )
-            store(i, count, res, nc.scalar if after == 7 else nc.sync)
+            store(i, count, part)
 
-        x_interleave(0, 0, SPLIT, "S")
-        x_interleave(1, 0, SPLIT1, "S")
+        def scale_late(i, extra, after, queue=nc.sync):
+            u, m = divmod(i, 4)
+            w, g = divmod(u, 2)
+            late = work.tile([NP, F + extra], F32, name="late_%d" % i, tag=after, bufs=1, align_bytes=64)
+            nc.gpsimd.tensor_tensor(
+                out=late[:],
+                in0=raw[u][:].rearrange("p m f -> p (m f)")[:, F * m : F * m + F + extra],
+                in1=gain_t[:, : F + extra],
+                op=ALU.mult,
+            )
+            queue.dma_start(out=outs[g][NP * m : NP * m + NP, w, :], in_=late[:, :F])
+            if extra:
+                queue.dma_start(out=outs[g][NP * m + NP : NP * m + 2 * NP, w, :extra], in_=late[:, F:])
+
+        x_interleave(0, 0, SPLIT, "S", "xg_0")
         perm_aw(0)
-        x_interleave(0, SPLIT, F, "V")
         perm_as(0)
+        x_interleave(0, SPLIT, F, "V")
         x_quantize(0)
+        for t in range(K0):
+            mm1(t, (0,))
+        x_interleave(1, 0, SPLIT1, "S", "xg_1")
         x_interleave(1, SPLIT1, F, "V")
-        perm_aw(1)
-        x_quantize(1)
         perm_as(1)
-        x_interleave(2, 0, F, "S")
+        x_quantize(1)
+        perm_aw(1)
+        x_interleave(2, 0, F, "S", "xg_2")
+        x_interleave(3, 0, F, "G", "xg_3")
+
         for t in range(4):
-            mm1(t)
-
-        def ok(u):
-            return 0 <= u < 8
-
-        for k in range(8):
+            mm1(t, (1,) if t < K0 else (0, 1))
+            add1(t)
+            round1(t)
+        mm1(4)
+        mm1(5)
+        add1(4)
+        x_quantize(2)
+        x_quantize(3)
+        for c in range(2):
+            turn(c)
+            gather1(c)
+        mm1(6)
+        mm1(7)
+        add1(5)
+        quant1(0)
+        x_interleave(4, 0, F, "G", "h1g_0")
+        add1(6)
+        add1(7)
+        for t in range(4):
+            if t == 2:
+                x_interleave(5, 0, F // 4, "S", "xg_0")
+            round1(4 + t)
+            mm2(t)
+        nc.scalar.copy(out=gain_t[:, F:], in_=gain_b)
+        for c in range(2):
+            turn(2 + c)
+            gather1(2 + c)
+        for t in range(4):
+            add2(t)
+        mm1(8)
+        mm1(9)
+        x_interleave(5, F // 4, F // 2, "S")
+        x_interleave(6, 0, F // 2, "S", "xg_1")
+        for k in range(2, 8):
             u1, u2, u3 = k - 1, k - 2, k - 3
-            if ok(u1):
-                quant1(u1)
-            if k >= 3 and ok(k + 2):
+            quant2(u2)
+            quant1(u1)
+            last = "h1g_%d" % (u1 % 4)
+            if k < 6:
                 x_quantize(k + 2)
-            if ok(u2):
-                quant2(u2)
+                last = xslot[k + 2]
             if k == 2:
-                x_quantize(4)
-            if ok(u3):
-                scale3(4 * u3 + 2, 1, u2)
-            if ok(u1):
-                mm2(4 * u1)
-                mm2(4 * u1 + 1)
-            for t in range(6):
-                if ok(u2) and t < 4:
-                    mm3(4 * u2 + t)
-                if ok(u2) and t >= 3:
-                    empty3(4 * u2 + t - 3)
-                if 1 <= t < 5:
-                    add1(4 * k + t - 1)
-            if ok(u2):
-                scale3(4 * u2, 2)
-            if k == 0:
-                perm_b()
-                x_quantize(2)
-            for t in range(4):
-                turn(4 * k + t)
-                gather1(4 * k + t)
-                if t == 1 and ok(u1):
-                    add2(4 * u1)
-                    add2(4 * u1 + 1)
-            if ok(u2):
-                finish_vector(4 * u2 + 3)
-            if k < 2:
-                x_interleave(k + 3, 0, F, "S")
-            if k >= 1 and ok(k + 4):
-                x_interleave(k + 4, 0, F, "S")
-            if k == 1:
-                x_quantize(3)
-            if ok(u1):
-                mm2(4 * u1 + 2)
-                mm2(4 * u1 + 3)
-                add2(4 * u1 + 2)
-                add2(4 * u1 + 3)
-            if ok(k + 1):
-                for t in range(4):
-                    mm1(4 * k + 4 + t)
+                x_interleave(5, F // 2, F, "G", last)
+            else:
+                scale_late(4 * u3 + 2, G_EXTRA, last)
+            mm3(4 * u2)
+            mm3(4 * u2 + 1)
+            empty3(4 * u2)
+            if k == 2:
+                x_interleave(6, F // 2, 3 * F // 4, "S")
+            add1(4 * k)
+            round1(4 * k)
+            mm1(4 * k + 2)
+            mm1(4 * k + 3)
+            empty3(4 * u2 + 1)
+            scale_now(4 * u2, 2)
+            for t in range(1, 4):
+                add1(4 * k + t)
+                round1(4 * k + t)
+                if t < 3:
+                    mm2(4 * u1 + t - 1)
+                    mm3(4 * u2 + t + 1)
+            add2(4 * u1)
+            mm2(4 * u1 + 2)
+            add2(4 * u1 + 1)
+            mm2(4 * u1 + 3)
+            for c in range(2):
+                turn(2 * k + c)
+                gather1(2 * k + c)
+            add2(4 * u1 + 2)
+            if k < 7:
+                mm1(4 * k + 4)
+            add2(4 * u1 + 3)
+            if k < 7:
+                mm1(4 * k + 5)
+            finish_vector(4 * u2 + 3, G_EXTRA)
+            if k == 4:
+                x_interleave(7, 3 * F // 4, F, "S")
+            empty3(4 * u2 + 2)
+            if G_EXTRA:
+                empty3(4 * u2 + 3, G_EXTRA)
+            if k == 2:
+                x_interleave(6, 3 * F // 4, F, "S")
+                x_interleave(7, 0, F // 4, "S", "xg_2")
+            if k == 3:
+                x_interleave(7, F // 4, 3 * F // 4, "S")
 
-        quant1(7)
         quant2(6)
-        scale3(4 * 5 + 2, 1, 6)
+        quant1(7)
+        scale_late(22, G_EXTRA, "h1g_3")
+        mm3(24)
+        mm3(25)
         for t in range(4):
             mm2(28 + t)
+        mm3(26)
+        mm3(27)
+        empty3(24)
+        finish_vector(25)
         for t in range(4):
-            mm3(24 + t)
-            if t < TAILG:
-                empty3(24 + t)
             add2(28 + t)
-        finish_vector(27)
+        scale_now(24, 1)
+        finish_vector(26)
         quant2(7)
-        scale3(24, TAILG, 7)
-        for t in range(TAILG, 3):
-            finish_vector(24 + t)
+        finish_vector(27)
         for t in range(4):
             mm3(28 + t)
             finish_vector(28 + t)

@@ -20,7 +20,7 @@ NP = 128
 SPLIT = 192
 SPLIT1 = 240
 K0 = 2
-G_EXTRA = 256
+G_COLS = 384
 
 
 def tile_parcel_band_hemisphere_coupling_t2_kernel(
@@ -45,8 +45,8 @@ def tile_parcel_band_hemisphere_coupling_t2_kernel(
         b_s = keep.tile([NP, 1, F], U8, name="b_s", align_bytes=64)
         c_w = keep.tile([NP, 2, 2 * H], U8, name="c_w", align_bytes=64)
         c_s = keep.tile([NP, 2, H], U8, name="c_s", align_bytes=64)
-        gain_t = keep.tile([NP, 2 * F], BF16, name="gain_t")
-        gain_b = gain_t[:, :F]
+        gain_t = keep.tile([NP, F], BF16, name="gain_t")
+        gain_b = gain_t[:]
         xs = {}
         for w in range(T):
             for k in range(2):
@@ -99,10 +99,10 @@ def tile_parcel_band_hemisphere_coupling_t2_kernel(
                 in_=a_raw[h][:].bitcast(U16).rearrange("p g (m t) -> p g t m", t=4)[:, :, lo:hi, :],
             )
 
-        def perm_as(h):
+        def perm_as(h, lo=0, hi=4):
             nc.vector.tensor_copy(
-                out=a_s[h][:].rearrange("p g (t m) -> p g t m", t=4),
-                in_=a_sraw[:, :, H * h : H * h + H].rearrange("p g (m t) -> p g t m", t=4),
+                out=a_s[h][:].rearrange("p g (t m) -> p g t m", t=4)[:, :, lo:hi, :],
+                in_=a_sraw[:, :, H * h : H * h + H].rearrange("p g (m t) -> p g t m", t=4)[:, :, lo:hi, :],
             )
 
         xg, xc, xsc, xslot = {}, {}, {}, {}
@@ -192,8 +192,8 @@ def tile_parcel_band_hemisphere_coupling_t2_kernel(
             if t == 0:
                 h1b[u] = work.tile([NP, 4, F], BF16, name="h1b_%d" % u, tag="h1b", bufs=2)
             nc.scalar.copy(
-                out=h1b[u][:, t, :].rearrange("p (a m e) -> p a m e", a=2, e=2),
-                in_=h1[u][:, t, :].rearrange("p (m a e) -> p a m e", a=2, e=2),
+                out=h1b[u][:, t, :].rearrange("p (a n m e) -> p n a m e", a=2, m=4, e=2),
+                in_=h1[u][:, t, :].rearrange("p (n m a e) -> p n a m e", a=2, m=4, e=2),
             )
 
         def turn(j):
@@ -239,12 +239,12 @@ def tile_parcel_band_hemisphere_coupling_t2_kernel(
         def add2(i):
             u, b = divmod(i, 4)
             if b == 0:
-                h2g[u] = work.tile([NP, F, 4], BF16, name="h2g_%d" % u, tag="h2g", bufs=2, align_bytes=64)
+                h2g[u] = work.tile([NP, F, 4], BF16, name="h2g_%d" % u, tag="h2g_%d" % (u % 2), bufs=1, align_bytes=64)
             cols = slice(NP * b, NP * b + NP)
             nc.vector.tensor_tensor(
-                out=h2g[u][:, cols, :].rearrange("p (a i) t -> p a t i", i=2),
-                in0=e[i][:].rearrange("p t (a i) -> p a t i", i=2),
-                in1=h1[u][:, :, cols].rearrange("p t (a i) -> p a t i", i=2),
+                out=h2g[u][:, cols, :].rearrange("p (a i) t -> p a t i", i=4),
+                in0=e[i][:].rearrange("p t (a i) -> p a t i", i=4),
+                in1=h1[u][:, :, cols].rearrange("p t (a i) -> p a t i", i=4),
                 op=ALU.add,
             )
             give_bank("e", i)
@@ -310,30 +310,41 @@ def tile_parcel_band_hemisphere_coupling_t2_kernel(
             )
             store(i, count, part)
 
-        def scale_late(i, extra, after, queue=nc.sync):
-            u, m = divmod(i, 4)
+        def scale_late(u, after):
             w, g = divmod(u, 2)
-            late = work.tile([NP, F + extra], F32, name="late_%d" % i, tag=after, bufs=1, align_bytes=64)
+            late = work.tile([NP, 2, G_COLS], F32, name="late_%d" % u, tag=after, bufs=1, align_bytes=64)
             nc.gpsimd.tensor_tensor(
                 out=late[:],
-                in0=raw[u][:].rearrange("p m f -> p (m f)")[:, F * m : F * m + F + extra],
-                in1=gain_t[:, : F + extra],
+                in0=raw[u][:, 2:4, :G_COLS],
+                in1=gain_b[:, :G_COLS].unsqueeze(1).to_broadcast([NP, 2, G_COLS]),
                 op=ALU.mult,
             )
-            queue.dma_start(out=outs[g][NP * m : NP * m + NP, w, :], in_=late[:, :F])
-            if extra:
-                queue.dma_start(out=outs[g][NP * m + NP : NP * m + 2 * NP, w, :extra], in_=late[:, F:])
+            nc.sync.dma_start(
+                out=outs[g][2 * NP : 4 * NP, w, :G_COLS].rearrange("(m p) f -> p m f", p=NP), in_=late[:]
+            )
+
+        def finish_rest(u):
+            w, g = divmod(u, 2)
+            res = work.tile([NP, 2, F - G_COLS], F32, name="rest_%d" % u, tag="rest", bufs=3)
+            for m in range(2):
+                nc.vector.tensor_tensor(
+                    out=res[:, m, :], in0=o[4 * u + 2 + m][:, G_COLS:], in1=gain_b[:, G_COLS:], op=ALU.mult
+                )
+            nc.sync.dma_start(
+                out=outs[g][2 * NP : 4 * NP, w, G_COLS:].rearrange("(m p) f -> p m f", p=NP), in_=res[:]
+            )
 
         x_interleave(0, 0, SPLIT, "S", "xg_0")
         perm_aw(0)
         perm_as(0)
+        perm_as(1, 0, 2)
         x_interleave(0, SPLIT, F, "V")
         x_quantize(0)
         for t in range(K0):
             mm1(t, (0,))
         x_interleave(1, 0, SPLIT1, "S", "xg_1")
         x_interleave(1, SPLIT1, F, "V")
-        perm_as(1)
+        perm_as(1, 2, 4)
         x_quantize(1)
         perm_aw(1)
         x_interleave(2, 0, F, "S", "xg_2")
@@ -363,7 +374,6 @@ def tile_parcel_band_hemisphere_coupling_t2_kernel(
                 x_interleave(5, 0, F // 4, "S", "xg_0")
             round1(4 + t)
             mm2(t)
-        nc.scalar.copy(out=gain_t[:, F:], in_=gain_b)
         for c in range(2):
             turn(2 + c)
             gather1(2 + c)
@@ -384,7 +394,7 @@ def tile_parcel_band_hemisphere_coupling_t2_kernel(
             if k == 2:
                 x_interleave(5, F // 2, F, "G", last)
             else:
-                scale_late(4 * u3 + 2, G_EXTRA, last)
+                scale_late(u3, last)
             mm3(4 * u2)
             mm3(4 * u2 + 1)
             empty3(4 * u2)
@@ -415,12 +425,11 @@ def tile_parcel_band_hemisphere_coupling_t2_kernel(
             add2(4 * u1 + 3)
             if k < 7:
                 mm1(4 * k + 5)
-            finish_vector(4 * u2 + 3, G_EXTRA)
+            finish_rest(u2)
             if k == 4:
                 x_interleave(7, 3 * F // 4, F, "S")
-            empty3(4 * u2 + 2)
-            if G_EXTRA:
-                empty3(4 * u2 + 3, G_EXTRA)
+            empty3(4 * u2 + 2, G_COLS)
+            empty3(4 * u2 + 3, G_COLS)
             if k == 2:
                 x_interleave(6, 3 * F // 4, F, "S")
                 x_interleave(7, 0, F // 4, "S", "xg_2")
@@ -429,18 +438,19 @@ def tile_parcel_band_hemisphere_coupling_t2_kernel(
 
         quant2(6)
         quant1(7)
-        scale_late(22, G_EXTRA, "h1g_3")
+        scale_late(5, "h1g_3")
         mm3(24)
+        mm2(28)
         mm3(25)
-        for t in range(4):
+        for t in range(1, 4):
             mm2(28 + t)
         mm3(26)
         mm3(27)
-        empty3(24)
-        finish_vector(25)
+        finish_vector(24)
+        empty3(25)
         for t in range(4):
             add2(28 + t)
-        scale_now(24, 1)
+        scale_now(25, 1)
         finish_vector(26)
         quant2(7)
         finish_vector(27)

@@ -37,7 +37,7 @@ def tile_parcel_band_hemisphere_coupling_t2_kernel(
         ident = keep.tile([NP, NP], F32, name="ident")
         a_raw, a_w, a_s = {}, {}, {}
         for h in range(2):
-            a_raw[h] = keep.tile([NP, 2, P], U8, name="a_raw_%d" % h, align_bytes=64)
+            a_raw[h] = work.tile([NP, 2, P], U8, name="a_raw_%d" % h, tag="a_raw_%d" % h, bufs=1, align_bytes=64)
             a_w[h] = keep.tile([NP, 2, P], U8, name="a_w_%d" % h, align_bytes=64)
             a_s[h] = keep.tile([NP, 2, H], U8, name="a_s_%d" % h, align_bytes=64)
         a_sraw = keep.tile([NP, 2, P], U8, name="a_sraw", align_bytes=64)
@@ -84,11 +84,11 @@ def tile_parcel_band_hemisphere_coupling_t2_kernel(
         load_a(1)
         load_x(1, 1)
         load_scales(b_s, fb_scales)
-        load_scales(c_s, hs_scales)
         nc.sync.dma_start(out=b_w[:].bitcast(I32), in_=fb_words.bitcast(I32)[0])
         load_x(2, 0)
         load_x(2, 1)
         load_x(3, 0)
+        load_scales(c_s, hs_scales)
         load_x(3, 1)
         nc.sync.dma_start(out=c_w[:].bitcast(I32), in_=hs_words.bitcast(I32).rearrange("g p n -> p g n"))
         nc.sync.dma_start(out=gain_b, in_=gain.partition_broadcast(NP))
@@ -348,7 +348,7 @@ def tile_parcel_band_hemisphere_coupling_t2_kernel(
         x_quantize(1)
         perm_aw(1)
         x_interleave(2, 0, F, "S", "xg_2")
-        x_interleave(3, 0, F, "G", "xg_3")
+        x_interleave(3, 0, F, "G", "a_raw_1")
 
         for t in range(4):
             mm1(t, (1,) if t < K0 else (0, 1))
@@ -398,14 +398,14 @@ def tile_parcel_band_hemisphere_coupling_t2_kernel(
             mm3(4 * u2)
             mm3(4 * u2 + 1)
             empty3(4 * u2)
+            add1(4 * k)
+            empty3(4 * u2 + 1)
+            scale_now(4 * u2, 2)
             if k == 2:
                 x_interleave(6, F // 2, 3 * F // 4, "S")
-            add1(4 * k)
             round1(4 * k)
             mm1(4 * k + 2)
             mm1(4 * k + 3)
-            empty3(4 * u2 + 1)
-            scale_now(4 * u2, 2)
             for t in range(1, 4):
                 add1(4 * k + t)
                 round1(4 * k + t)

@@ -20,6 +20,8 @@ NP = 128
 SPLIT = 192
 SPLIT1 = 240
 K0 = 2
+H1G = (0, 1, 2, 3, 4, 2, 3, 4)
+G_LAST = 256
 G_COLS = 384
 
 
@@ -77,8 +79,8 @@ def tile_parcel_band_hemisphere_coupling_t2_kernel(
                 )
 
         load_a(0)
-        load_scales(a_sraw, sc_scales)
         load_x(0, 0)
+        load_scales(a_sraw, sc_scales)
         load_x(0, 1)
         load_x(1, 0)
         load_a(1)
@@ -208,7 +210,7 @@ def tile_parcel_band_hemisphere_coupling_t2_kernel(
         def gather1(j):
             u, c = divmod(j, 2)
             if c == 0:
-                h1g[u] = work.tile([NP, 4, NP, 2], F32, name="h1g_%d" % u, tag="h1g_%d" % (u % 4), bufs=1, align_bytes=64)
+                h1g[u] = work.tile([NP, 4, NP, 2], F32, name="h1g_%d" % u, tag="h1g_%d" % H1G[u], bufs=1, align_bytes=64)
             nc.scalar.copy(
                 out=h1g[u][:, 2 * c : 2 * c + 2, :, :],
                 in_=h1t[j][:].rearrange("p t a q -> p t q a"),
@@ -278,21 +280,21 @@ def tile_parcel_band_hemisphere_coupling_t2_kernel(
                 in_=res,
             )
 
-        def finish_vector(i, lo=0):
+        def finish_vector(i, lo=0, hi=F):
             u, m = divmod(i, 4)
             w, g = divmod(u, 2)
-            res = work.tile([NP, F - lo], F32, name="res_%d" % i, tag="res", bufs=8)
+            res = work.tile([NP, hi - lo], F32, name="res_%d_%d" % (i, lo), tag="res", bufs=8)
             nc.vector.tensor_tensor(
                 out=res[:],
-                in0=o[i][:, lo:],
-                in1=gain_b[:, lo:],
+                in0=o[i][:, lo:hi],
+                in1=gain_b[:, lo:hi],
                 op=ALU.mult,
             )
-            if lo == 0:
+            if hi == F:
                 give_bank("o", i)
-            nc.sync.dma_start(out=outs[g][NP * m : NP * m + NP, w, lo:], in_=res[:])
+            nc.sync.dma_start(out=outs[g][NP * m : NP * m + NP, w, lo:hi], in_=res[:])
 
-        def empty3(i, hi=F):
+        def empty3(i, hi=F, free=True):
             u, m = divmod(i, 4)
             if u not in raw:
                 raw[u] = work.tile([NP, 4, F], F32, name="raw_%d" % u, tag="raw", bufs=3)
@@ -300,7 +302,8 @@ def tile_parcel_band_hemisphere_coupling_t2_kernel(
                 out=raw[u][:, m, :hi],
                 in_=o[i][:, :hi],
             )
-            give_bank("o", i)
+            if free:
+                give_bank("o", i)
 
         def scale_now(i, count):
             u, m = divmod(i, 4)
@@ -310,35 +313,31 @@ def tile_parcel_band_hemisphere_coupling_t2_kernel(
             )
             store(i, count, part)
 
-        def scale_late(u, after):
+        def scale_late(u, cols, after):
             w, g = divmod(u, 2)
-            late = work.tile([NP, 2, G_COLS], F32, name="late_%d" % u, tag=after, bufs=1, align_bytes=64)
+            late = work.tile([NP, 2, cols], F32, name="late_%d" % u, tag=after, bufs=1, align_bytes=64)
             nc.gpsimd.tensor_tensor(
                 out=late[:],
-                in0=raw[u][:, 2:4, :G_COLS],
-                in1=gain_b[:, :G_COLS].unsqueeze(1).to_broadcast([NP, 2, G_COLS]),
+                in0=raw[u][:, 2:4, :cols],
+                in1=gain_b[:, :cols].unsqueeze(1).to_broadcast([NP, 2, cols]),
                 op=ALU.mult,
             )
-            nc.sync.dma_start(
-                out=outs[g][2 * NP : 4 * NP, w, :G_COLS].rearrange("(m p) f -> p m f", p=NP), in_=late[:]
-            )
+            nc.sync.dma_start(out=outs[g][2 * NP : 4 * NP, w, :cols].rearrange("(m p) f -> p m f", p=NP), in_=late[:])
 
-        def finish_rest(u):
+        def finish_rest(u, lo, hi):
             w, g = divmod(u, 2)
-            res = work.tile([NP, 2, F - G_COLS], F32, name="rest_%d" % u, tag="rest", bufs=3)
+            res = work.tile([NP, 2, hi - lo], F32, name="rest_%d_%d" % (u, lo), tag="rest", bufs=3)
             for m in range(2):
                 nc.vector.tensor_tensor(
-                    out=res[:, m, :], in0=o[4 * u + 2 + m][:, G_COLS:], in1=gain_b[:, G_COLS:], op=ALU.mult
+                    out=res[:, m, :], in0=o[4 * u + 2 + m][:, lo:hi], in1=gain_b[:, lo:hi], op=ALU.mult
                 )
-            nc.sync.dma_start(
-                out=outs[g][2 * NP : 4 * NP, w, G_COLS:].rearrange("(m p) f -> p m f", p=NP), in_=res[:]
-            )
+            nc.sync.dma_start(out=outs[g][2 * NP : 4 * NP, w, lo:hi].rearrange("(m p) f -> p m f", p=NP), in_=res[:])
 
         x_interleave(0, 0, SPLIT, "S", "xg_0")
         perm_aw(0)
         perm_as(0)
-        perm_as(1, 0, 2)
         x_interleave(0, SPLIT, F, "V")
+        perm_as(1, 0, 2)
         x_quantize(0)
         for t in range(K0):
             mm1(t, (0,))
@@ -381,28 +380,27 @@ def tile_parcel_band_hemisphere_coupling_t2_kernel(
             add2(t)
         mm1(8)
         mm1(9)
-        x_interleave(5, F // 4, F // 2, "S")
-        x_interleave(6, 0, F // 2, "S", "xg_1")
+        x_interleave(5, F // 4, F, "S")
         for k in range(2, 8):
             u1, u2, u3 = k - 1, k - 2, k - 3
+            if 3 <= k < 7:
+                x_quantize(k + 1)
+            if k in (4, 6):
+                mm1(4 * k, (1,))
+                mm1(4 * k + 1, (1,))
             quant2(u2)
             quant1(u1)
-            last = "h1g_%d" % (u1 % 4)
-            if k < 6:
-                x_quantize(k + 2)
-                last = xslot[k + 2]
+            last = "h1g_%d" % H1G[u1]
             if k == 2:
-                x_interleave(5, F // 2, F, "G", last)
+                x_interleave(6, 0, F // 2, "G", last)
             else:
-                scale_late(u3, last)
+                scale_late(u3, G_COLS, last)
             mm3(4 * u2)
             mm3(4 * u2 + 1)
             empty3(4 * u2)
             add1(4 * k)
             empty3(4 * u2 + 1)
             scale_now(4 * u2, 2)
-            if k == 2:
-                x_interleave(6, F // 2, 3 * F // 4, "S")
             round1(4 * k)
             mm1(4 * k + 2)
             mm1(4 * k + 3)
@@ -421,28 +419,29 @@ def tile_parcel_band_hemisphere_coupling_t2_kernel(
                 gather1(2 * k + c)
             add2(4 * u1 + 2)
             if k < 7:
-                mm1(4 * k + 4)
+                mm1(4 * k + 4, (0,) if k in (3, 5) else (0, 1))
             add2(4 * u1 + 3)
             if k < 7:
-                mm1(4 * k + 5)
-            finish_rest(u2)
-            if k == 4:
-                x_interleave(7, 3 * F // 4, F, "S")
-            empty3(4 * u2 + 2, G_COLS)
-            empty3(4 * u2 + 3, G_COLS)
+                mm1(4 * k + 5, (0,) if k in (3, 5) else (0, 1))
+            finish_rest(u2, G_COLS, F)
+            empty3(4 * u2 + 2, G_COLS if k < 7 else G_LAST, k < 7)
+            empty3(4 * u2 + 3, G_COLS if k < 7 else G_LAST, k < 7)
             if k == 2:
-                x_interleave(6, 3 * F // 4, F, "S")
-                x_interleave(7, 0, F // 4, "S", "xg_2")
+                x_interleave(6, F // 2, F, "S")
             if k == 3:
-                x_interleave(7, F // 4, 3 * F // 4, "S")
+                x_interleave(7, 0, F // 2, "S", "xg_2")
+            if k == 4:
+                x_interleave(7, F // 2, F, "S")
 
         quant2(6)
         quant1(7)
-        scale_late(5, "h1g_3")
+        scale_late(5, G_LAST, "h1g_%d" % H1G[7])
+        finish_rest(5, G_LAST, G_COLS)
+        give_bank("o", 22)
+        give_bank("o", 23)
         mm3(24)
-        mm2(28)
         mm3(25)
-        for t in range(1, 4):
+        for t in range(4):
             mm2(28 + t)
         mm3(26)
         mm3(27)
@@ -451,8 +450,9 @@ def tile_parcel_band_hemisphere_coupling_t2_kernel(
         for t in range(4):
             add2(28 + t)
         scale_now(25, 1)
-        finish_vector(26)
+        finish_vector(26, 0, F // 2)
         quant2(7)
+        finish_vector(26, F // 2, F)
         finish_vector(27)
         for t in range(4):
             mm3(28 + t)

@@ -72,15 +72,15 @@ def tile_parcel_band_hemisphere_coupling_t2_kernel(
             )
 
         def load_scales(dst, src):
-            for q in range(4):
+            for r in range(4):
                 nc.sync.dma_start(
-                    out=dst[32 * q : 32 * q + 4].bitcast(I32),
-                    in_=src.bitcast(I32)[:, 4 * q : 4 * q + 4, :].rearrange("g q n -> q g n"),
+                    out=dst[r:NP:32].bitcast(I32),
+                    in_=src.bitcast(I32)[:, r:16:4, :].rearrange("g q n -> q g n"),
                 )
 
         load_a(0)
-        load_x(0, 0)
         load_scales(a_sraw, sc_scales)
+        load_x(0, 0)
         load_x(0, 1)
         load_x(1, 0)
         load_a(1)
@@ -336,8 +336,8 @@ def tile_parcel_band_hemisphere_coupling_t2_kernel(
         x_interleave(0, 0, SPLIT, "S", "xg_0")
         perm_aw(0)
         perm_as(0)
-        x_interleave(0, SPLIT, F, "V")
         perm_as(1, 0, 2)
+        x_interleave(0, SPLIT, F, "V")
         x_quantize(0)
         for t in range(K0):
             mm1(t, (0,))
@@ -356,6 +356,7 @@ def tile_parcel_band_hemisphere_coupling_t2_kernel(
         mm1(4)
         mm1(5)
         add1(4)
+        add1(5)
         x_quantize(2)
         x_quantize(3)
         for c in range(2):
@@ -363,7 +364,6 @@ def tile_parcel_band_hemisphere_coupling_t2_kernel(
             gather1(c)
         mm1(6)
         mm1(7)
-        add1(5)
         quant1(0)
         x_interleave(4, 0, F, "G", "h1g_0")
         add1(6)

@@ -19,10 +19,17 @@ ALU = mybir.AluOpType
 NP = 128
 SPLIT = 192
 SPLIT1 = 240
-K0 = 2
+K0 = 3
 H1G = (0, 1, 2, 3, 4, 2, 3, 4)
-G_LAST = 256
-G_COLS = 384
+G_COLS = 256
+X2_S = 320
+X5_V = 416
+X5_S = 352
+X6_G = 96
+X7_G = 192
+P_HEAD = (192, 192, 192)
+P_GAP = 96
+P_END = 192
 
 
 def tile_parcel_band_hemisphere_coupling_t2_kernel(
@@ -47,15 +54,15 @@ def tile_parcel_band_hemisphere_coupling_t2_kernel(
         b_s = keep.tile([NP, 1, F], U8, name="b_s", align_bytes=64)
         c_w = keep.tile([NP, 2, 2 * H], U8, name="c_w", align_bytes=64)
         c_s = keep.tile([NP, 2, H], U8, name="c_s", align_bytes=64)
-        gain_t = keep.tile([NP, F], BF16, name="gain_t")
-        gain_b = gain_t[:]
+        gain3 = keep.tile([NP, 2 * F + G_COLS], BF16, name="gain3")
+        gain_b = gain3[:, :F]
         xs = {}
         for w in range(T):
             for k in range(2):
                 xt = keep.tile([NP, 4, F], BF16, name="x_%d_%d" % (w, k))
                 xs[w, k] = xt
 
-        nc.vector.memset(a_sraw[:].bitcast(I32), 0)
+        nc.gpsimd.memset(a_sraw[:].bitcast(I32), 0)
         nc.vector.memset(b_s[:].bitcast(I32), 0)
         nc.vector.memset(c_s[:].bitcast(I32), 0)
         make_identity(nc, ident[:])
@@ -82,8 +89,8 @@ def tile_parcel_band_hemisphere_coupling_t2_kernel(
         load_scales(a_sraw, sc_scales)
         load_x(0, 0)
         load_x(0, 1)
-        load_x(1, 0)
         load_a(1)
+        load_x(1, 0)
         load_x(1, 1)
         load_scales(b_s, fb_scales)
         nc.sync.dma_start(out=b_w[:].bitcast(I32), in_=fb_words.bitcast(I32)[0])
@@ -113,10 +120,10 @@ def tile_parcel_band_hemisphere_coupling_t2_kernel(
             w, k = divmod(v, 2)
             if slot is not None:
                 tile = work.tile([NP, F, 4], BF16, name="xg_%d_%d" % (v, lo), tag=slot, bufs=1, align_bytes=64)
-                xg[v] = xg.get(v, []) + [(lo, tile)]
+                xg[v] = [(0, tile)]
                 xslot[v] = slot
             tile = xg[v][-1][1]
-            if eng == "G":
+            if eng in ("G", "G2"):
                 nc.gpsimd.tensor_scalar(
                     out=tile[:, lo:hi, :],
                     in0=xs[w, k][:, :, lo:hi].rearrange("p t c -> p c t"),
@@ -133,11 +140,24 @@ def tile_parcel_band_hemisphere_coupling_t2_kernel(
             else:
                 nc.scalar.copy(out=dst, in_=src)
 
+        todo = [[5, 0, X5_S], [6, 0, F], [7, 0, F - X6_G - X7_G]]
+
+        def s_interleave(width):
+            while width > 0 and todo:
+                v, lo, hi = todo[0]
+                n = min(width, hi - lo)
+                x_interleave(v, lo, lo + n, "S", "xg_1" if v not in xg else None)
+                width = width - n
+                if lo + n == hi:
+                    todo.pop(0)
+                else:
+                    todo[0] = [v, lo + n, hi]
+
         def x_quantize(v):
             c = work.tile([NP, F], U32, name="xc_%d" % v, tag="xc", bufs=6, align_bytes=64)
             s = work.tile([NP, F], U8, name="xsc_%d" % v, tag="xsc", bufs=6, align_bytes=64)
-            width = F // len(xg[v])
-            for lo, tile in xg[v]:
+            for n, (lo, tile) in enumerate(xg[v]):
+                width = (xg[v][n + 1][0] if n + 1 < len(xg[v]) else F) - lo
                 nc.vector.quantize_mx(
                     out=c[:, lo : lo + width].bitcast(FP8X4),
                     scales=s[:, lo : lo + width],
@@ -174,20 +194,21 @@ def tile_parcel_band_hemisphere_coupling_t2_kernel(
                     stop=(k == 1),
                 )
 
-        def add1(i):
+        def add1(i, lo=0, hi=F):
             u, t = divmod(i, 4)
             w, h = divmod(u, 2)
             if t == 0:
                 h1[u] = work.tile([NP, 4, F], F32, name="h1_%d" % u, tag="h1", bufs=4)
             nc.vector.scalar_tensor_tensor(
-                out=h1[u][:, t, :],
-                in0=d[i][:],
+                out=h1[u][:, t, lo:hi],
+                in0=d[i][:, lo:hi],
                 scalar=0.0,
-                in1=xs[w, h][:, t, :],
+                in1=xs[w, h][:, t, lo:hi],
                 op0=ALU.max,
                 op1=ALU.add,
             )
-            give_bank("d", i)
+            if hi == F:
+                give_bank("d", i)
 
         def round1(i):
             u, t = divmod(i, 4)
@@ -280,7 +301,7 @@ def tile_parcel_band_hemisphere_coupling_t2_kernel(
                 in_=res,
             )
 
-        def finish_vector(i, lo=0, hi=F):
+        def finish_vector(i, lo=0, hi=F, free=True):
             u, m = divmod(i, 4)
             w, g = divmod(u, 2)
             res = work.tile([NP, hi - lo], F32, name="res_%d_%d" % (i, lo), tag="res", bufs=8)
@@ -290,7 +311,7 @@ def tile_parcel_band_hemisphere_coupling_t2_kernel(
                 in1=gain_b[:, lo:hi],
                 op=ALU.mult,
             )
-            if hi == F:
+            if hi == F and free:
                 give_bank("o", i)
             nc.sync.dma_start(out=outs[g][NP * m : NP * m + NP, w, lo:hi], in_=res[:])
 
@@ -313,31 +334,33 @@ def tile_parcel_band_hemisphere_coupling_t2_kernel(
             )
             store(i, count, part)
 
+        lates = {}
+
         def scale_late(u, cols, after):
             w, g = divmod(u, 2)
-            late = work.tile([NP, 2, cols], F32, name="late_%d" % u, tag=after, bufs=1, align_bytes=64)
+            first = 2 if u == 0 else 1
+            width = (3 - first) * F + cols
+            late = work.tile([NP, width], F32, name="late_%d" % u, tag=after, bufs=1, align_bytes=64)
             nc.gpsimd.tensor_tensor(
                 out=late[:],
-                in0=raw[u][:, 2:4, :cols],
-                in1=gain_b[:, :cols].unsqueeze(1).to_broadcast([NP, 2, cols]),
+                in0=raw[u][:].rearrange("p m f -> p (m f)")[:, first * F : first * F + width],
+                in1=gain3[:, :width],
                 op=ALU.mult,
             )
-            nc.sync.dma_start(out=outs[g][2 * NP : 4 * NP, w, :cols].rearrange("(m p) f -> p m f", p=NP), in_=late[:])
+            lates[u] = late
 
-        def finish_rest(u, lo, hi):
+        def store_late(u, cols):
             w, g = divmod(u, 2)
-            res = work.tile([NP, 2, hi - lo], F32, name="rest_%d_%d" % (u, lo), tag="rest", bufs=3)
-            for m in range(2):
-                nc.vector.tensor_tensor(
-                    out=res[:, m, :], in0=o[4 * u + 2 + m][:, lo:hi], in1=gain_b[:, lo:hi], op=ALU.mult
-                )
-            nc.sync.dma_start(out=outs[g][2 * NP : 4 * NP, w, lo:hi].rearrange("(m p) f -> p m f", p=NP), in_=res[:])
+            first = 2 if u == 0 else 1
+            late = lates[u]
+            store(4 * u + first, 3 - first, late[:, : (3 - first) * F].rearrange("p (m f) -> p m f", f=F))
+            nc.sync.dma_start(out=outs[g][3 * NP : 4 * NP, w, :cols], in_=late[:, (3 - first) * F :])
 
         x_interleave(0, 0, SPLIT, "S", "xg_0")
         perm_aw(0)
         perm_as(0)
-        perm_as(1, 0, 2)
         x_interleave(0, SPLIT, F, "V")
+        perm_as(1, 0, 2)
         x_quantize(0)
         for t in range(K0):
             mm1(t, (0,))
@@ -346,43 +369,60 @@ def tile_parcel_band_hemisphere_coupling_t2_kernel(
         perm_as(1, 2, 4)
         x_quantize(1)
         perm_aw(1)
-        x_interleave(2, 0, F, "S", "xg_2")
-        x_interleave(3, 0, F, "G", "a_raw_1")
+        x_interleave(2, X2_S, F, "G", "a_raw_1")
+        x_interleave(2, 0, X2_S, "S")
+        x_interleave(3, 0, F, "G", "xg_2")
 
         for t in range(4):
             mm1(t, (1,) if t < K0 else (0, 1))
             add1(t)
             round1(t)
-        mm1(4)
-        mm1(5)
-        add1(4)
-        add1(5)
+        for t in range(4, 7):
+            mm1(t)
+            add1(t)
+        turn(0)
+        gather1(0)
+        mm1(7)
+        round1(4)
+        turn(1)
+        gather1(1)
         x_quantize(2)
         x_quantize(3)
-        for c in range(2):
-            turn(c)
-            gather1(c)
-        mm1(6)
-        mm1(7)
+        x_interleave(5, X5_V, F, "V", "xg_0")
         quant1(0)
         x_interleave(4, 0, F, "G", "h1g_0")
-        add1(6)
-        add1(7)
-        for t in range(4):
-            if t == 2:
-                x_interleave(5, 0, F // 4, "S", "xg_0")
-            round1(4 + t)
-            mm2(t)
-        for c in range(2):
-            turn(2 + c)
-            gather1(2 + c)
-        for t in range(4):
-            add2(t)
+        x_interleave(5, X5_S, X5_V, "G")
         mm1(8)
+        add1(7)
+        round1(5)
+        round1(6)
+        s_interleave(P_HEAD[0])
+        round1(7)
+        for t in range(3):
+            mm2(t)
+        add1(8)
+        turn(2)
+        gather1(2)
+        s_interleave(P_HEAD[1])
+        add2(0)
+        mm2(3)
         mm1(9)
-        x_interleave(5, F // 4, F, "S")
+        add2(1)
+        turn(3)
+        gather1(3)
+        add2(2)
+        mm1(10)
+        add2(3)
+        mm1(11)
+        add1(9, 0, F // 2)
+        round1(8)
+        s_interleave(P_HEAD[2])
         for k in range(2, 8):
             u1, u2, u3 = k - 1, k - 2, k - 3
+            ahead = (0,) if k in (3, 5) else (0, 1)
+            if k == 3:
+                nc.vector.tensor_copy(out=gain3[:, F : 2 * F], in_=gain_b)
+                nc.vector.tensor_copy(out=gain3[:, 2 * F :], in_=gain_b[:, :G_COLS])
             if 3 <= k < 7:
                 x_quantize(k + 1)
             if k in (4, 6):
@@ -392,67 +432,86 @@ def tile_parcel_band_hemisphere_coupling_t2_kernel(
             quant1(u1)
             last = "h1g_%d" % H1G[u1]
             if k == 2:
-                x_interleave(6, 0, F // 2, "G", last)
+                x_interleave(7, F - X6_G, F, "G", last)
             else:
                 scale_late(u3, G_COLS, last)
-            mm3(4 * u2)
-            mm3(4 * u2 + 1)
-            empty3(4 * u2)
-            add1(4 * k)
-            empty3(4 * u2 + 1)
-            scale_now(4 * u2, 2)
-            round1(4 * k)
-            mm1(4 * k + 2)
-            mm1(4 * k + 3)
-            for t in range(1, 4):
-                add1(4 * k + t)
-                round1(4 * k + t)
-                if t < 3:
-                    mm2(4 * u1 + t - 1)
-                    mm3(4 * u2 + t + 1)
-            add2(4 * u1)
-            mm2(4 * u1 + 2)
-            add2(4 * u1 + 1)
-            mm2(4 * u1 + 3)
-            for c in range(2):
-                turn(2 * k + c)
-                gather1(2 * k + c)
-            add2(4 * u1 + 2)
-            if k < 7:
-                mm1(4 * k + 4, (0,) if k in (3, 5) else (0, 1))
-            add2(4 * u1 + 3)
-            if k < 7:
-                mm1(4 * k + 5, (0,) if k in (3, 5) else (0, 1))
-            finish_rest(u2, G_COLS, F)
-            empty3(4 * u2 + 2, G_COLS if k < 7 else G_LAST, k < 7)
-            empty3(4 * u2 + 3, G_COLS if k < 7 else G_LAST, k < 7)
-            if k == 2:
-                x_interleave(6, F // 2, F, "S")
+                store_late(u3, G_COLS)
             if k == 3:
-                x_interleave(7, 0, F // 2, "S", "xg_2")
-            if k == 4:
-                x_interleave(7, F // 2, F, "S")
+                x_interleave(7, F - X6_G - X7_G, F - X6_G, "G")
+            mm3(4 * u2)
+            if k in (4, 6):
+                mm1(4 * k + 2, (1,))
+            if k > 2:
+                mm1(4 * k + 3)
+            empty3(4 * u2)
+            scale_now(4 * u2, 1)
+            if k == 2:
+                mm3(1)
+                empty3(1)
+                scale_now(1, 1)
+                add1(9, F // 2, F)
+                round1(9)
+            else:
+                add1(4 * k)
+                round1(4 * k)
+            mm2(4 * u1)
+            mm2(4 * u1 + 1)
+            if k > 2:
+                add1(4 * k + 1)
+                round1(4 * k + 1)
+            mm2(4 * u1 + 2)
+            mm2(4 * u1 + 3)
+            add1(4 * k + 2)
+            round1(4 * k + 2)
+            if k > 2:
+                mm3(4 * u2 + 1)
+            add1(4 * k + 3)
+            round1(4 * k + 3)
+            if k < 7:
+                mm3(4 * u2 + 3)
+            add2(4 * u1)
+            turn(2 * k)
+            add2(4 * u1 + 1)
+            add2(4 * u1 + 2)
+            gather1(2 * k)
+            if k > 2:
+                empty3(4 * u2 + 1)
+            else:
+                s_interleave(P_GAP)
+            turn(2 * k + 1)
+            if k == 7:
+                mm3(4 * u2 + 3)
+            mm3(4 * u2 + 2)
+            add2(4 * u1 + 3)
+            finish_vector(4 * u2 + 3, G_COLS, F, False)
+            gather1(2 * k + 1)
+            if k == 5:
+                s_interleave(F)
+            empty3(4 * u2 + 2)
+            if k < 7:
+                for t in range(3):
+                    mm1(4 * k + 4 + t, ahead)
+            empty3(4 * u2 + 3, G_COLS)
+            if k < 5:
+                s_interleave(P_END)
 
         quant2(6)
         quant1(7)
-        scale_late(5, G_LAST, "h1g_%d" % H1G[7])
-        finish_rest(5, G_LAST, G_COLS)
-        give_bank("o", 22)
-        give_bank("o", 23)
+        scale_late(5, G_COLS, "h1g_%d" % H1G[7])
         mm3(24)
         mm3(25)
         for t in range(4):
             mm2(28 + t)
-        mm3(26)
-        mm3(27)
         finish_vector(24)
-        empty3(25)
+        mm3(26)
+        finish_vector(25, 0, F // 2)
         for t in range(4):
             add2(28 + t)
-        scale_now(25, 1)
-        finish_vector(26, 0, F // 2)
+        store_late(5, G_COLS)
+        finish_vector(25, F // 2, F)
+        mm3(27)
         quant2(7)
-        finish_vector(26, F // 2, F)
+        finish_vector(26)
         finish_vector(27)
         for t in range(4):
             mm3(28 + t)

@@ -21,13 +21,12 @@ SPLIT = 192
 SPLIT1 = 240
 K0 = 3
 H1G = (0, 1, 2, 3, 4, 2, 3, 4)
-G_COLS = 256
+G_COLS = 224
 X2_S = 320
-X5_V = 416
-X5_S = 352
+X5_S = 448
 X6_G = 96
-X7_G = 192
-P_HEAD = (192, 192, 192)
+X7_G = 256
+P_HEAD = (224, 224)
 P_GAP = 96
 P_END = 192
 
@@ -140,7 +139,7 @@ def tile_parcel_band_hemisphere_coupling_t2_kernel(
             else:
                 nc.scalar.copy(out=dst, in_=src)
 
-        todo = [[5, 0, X5_S], [6, 0, F], [7, 0, F - X6_G - X7_G]]
+        todo = [[5, 0, X5_S], [6, 0, F - X6_G - X7_G], [7, 0, F]]
 
         def s_interleave(width):
             while width > 0 and todo:
@@ -336,10 +335,23 @@ def tile_parcel_band_hemisphere_coupling_t2_kernel(
 
         lates = {}
 
-        def scale_late(u, cols, after):
+        def g_cols(u):
+            return G_COLS if 0 < u < 4 else 0
+
+        def scale_half(i):
+            u, m = divmod(i, 4)
+            part = raw[u][:, m, : F // 2]
+            nc.gpsimd.tensor_tensor(out=part, in0=part, in1=gain_b[:, : F // 2], op=ALU.mult)
+
+        def store_half(i):
+            u, m = divmod(i, 4)
+            nc.sync.dma_start(out=outs[u % 2][NP * m : NP * m + NP, u // 2, : F // 2], in_=raw[u][:, m, : F // 2])
+
+        def scale_late(u, cols, after, whole=2):
             w, g = divmod(u, 2)
             first = 2 if u == 0 else 1
-            width = (3 - first) * F + cols
+            whole = 1 if u == 0 else whole
+            width = whole * F + cols
             late = work.tile([NP, width], F32, name="late_%d" % u, tag=after, bufs=1, align_bytes=64)
             nc.gpsimd.tensor_tensor(
                 out=late[:],
@@ -349,12 +361,15 @@ def tile_parcel_band_hemisphere_coupling_t2_kernel(
             )
             lates[u] = late
 
-        def store_late(u, cols):
+        def store_late(u, cols, whole=2):
             w, g = divmod(u, 2)
             first = 2 if u == 0 else 1
+            whole = 1 if u == 0 else whole
             late = lates[u]
-            store(4 * u + first, 3 - first, late[:, : (3 - first) * F].rearrange("p (m f) -> p m f", f=F))
-            nc.sync.dma_start(out=outs[g][3 * NP : 4 * NP, w, :cols], in_=late[:, (3 - first) * F :])
+            store(4 * u + first, whole, late[:, : whole * F].rearrange("p (m f) -> p m f", f=F))
+            if cols:
+                m = first + whole
+                nc.sync.dma_start(out=outs[g][m * NP : m * NP + NP, w, :cols], in_=late[:, whole * F :])
 
         x_interleave(0, 0, SPLIT, "S", "xg_0")
         perm_aw(0)
@@ -380,49 +395,39 @@ def tile_parcel_band_hemisphere_coupling_t2_kernel(
         for t in range(4, 7):
             mm1(t)
             add1(t)
-        turn(0)
-        gather1(0)
+        for c in range(2):
+            turn(c)
+            gather1(c)
         mm1(7)
-        round1(4)
-        turn(1)
-        gather1(1)
         x_quantize(2)
         x_quantize(3)
-        x_interleave(5, X5_V, F, "V", "xg_0")
+        x_interleave(5, X5_S, F, "V", "xg_0")
         quant1(0)
         x_interleave(4, 0, F, "G", "h1g_0")
-        x_interleave(5, X5_S, X5_V, "G")
         mm1(8)
+        mm1(9)
         add1(7)
-        round1(5)
-        round1(6)
-        s_interleave(P_HEAD[0])
-        round1(7)
-        for t in range(3):
+        for t in range(4, 8):
+            round1(t)
+        for t in range(4):
             mm2(t)
         add1(8)
-        turn(2)
-        gather1(2)
-        s_interleave(P_HEAD[1])
+        s_interleave(P_HEAD[0])
         add2(0)
-        mm2(3)
-        mm1(9)
         add2(1)
-        turn(3)
-        gather1(3)
+        for c in range(2, 4):
+            turn(c)
+            gather1(c)
         add2(2)
         mm1(10)
         add2(3)
         mm1(11)
         add1(9, 0, F // 2)
         round1(8)
-        s_interleave(P_HEAD[2])
+        s_interleave(P_HEAD[1])
         for k in range(2, 8):
             u1, u2, u3 = k - 1, k - 2, k - 3
             ahead = (0,) if k in (3, 5) else (0, 1)
-            if k == 3:
-                nc.vector.tensor_copy(out=gain3[:, F : 2 * F], in_=gain_b)
-                nc.vector.tensor_copy(out=gain3[:, 2 * F :], in_=gain_b[:, :G_COLS])
             if 3 <= k < 7:
                 x_quantize(k + 1)
             if k in (4, 6):
@@ -432,17 +437,20 @@ def tile_parcel_band_hemisphere_coupling_t2_kernel(
             quant1(u1)
             last = "h1g_%d" % H1G[u1]
             if k == 2:
-                x_interleave(7, F - X6_G, F, "G", last)
+                x_interleave(6, F - X6_G, F, "G", last)
             else:
-                scale_late(u3, G_COLS, last)
-                store_late(u3, G_COLS)
+                scale_late(u3, g_cols(u3), last)
+                store_late(u3, g_cols(u3))
             if k == 3:
-                x_interleave(7, F - X6_G - X7_G, F - X6_G, "G")
+                x_interleave(6, F - X6_G - X7_G, F - X6_G, "G")
             mm3(4 * u2)
             if k in (4, 6):
                 mm1(4 * k + 2, (1,))
             if k > 2:
                 mm1(4 * k + 3)
+            if k == 3:
+                nc.scalar.copy(out=gain3[:, F : 2 * F], in_=gain_b)
+                nc.scalar.copy(out=gain3[:, 2 * F :], in_=gain_b[:, :G_COLS])
             empty3(4 * u2)
             scale_now(4 * u2, 1)
             if k == 2:
@@ -460,6 +468,8 @@ def tile_parcel_band_hemisphere_coupling_t2_kernel(
                 add1(4 * k + 1)
                 round1(4 * k + 1)
             mm2(4 * u1 + 2)
+            if k == 7:
+                break
             mm2(4 * u1 + 3)
             add1(4 * k + 2)
             round1(4 * k + 2)
@@ -467,49 +477,75 @@ def tile_parcel_band_hemisphere_coupling_t2_kernel(
                 mm3(4 * u2 + 1)
             add1(4 * k + 3)
             round1(4 * k + 3)
-            if k < 7:
-                mm3(4 * u2 + 3)
+            mm3(4 * u2 + 3)
             add2(4 * u1)
-            turn(2 * k)
+            mm1(4 * k + 4, ahead)
+            if k == 2:
+                s_interleave(P_GAP)
+            elif k < 6:
+                empty3(4 * u2 + 1)
             add2(4 * u1 + 1)
             add2(4 * u1 + 2)
-            gather1(2 * k)
-            if k > 2:
-                empty3(4 * u2 + 1)
-            else:
-                s_interleave(P_GAP)
-            turn(2 * k + 1)
-            if k == 7:
-                mm3(4 * u2 + 3)
+            for c in range(2):
+                turn(2 * k + c)
+                gather1(2 * k + c)
             mm3(4 * u2 + 2)
             add2(4 * u1 + 3)
-            finish_vector(4 * u2 + 3, G_COLS, F, False)
-            gather1(2 * k + 1)
-            if k == 5:
-                s_interleave(F)
+            finish_vector(4 * u2 + 3, g_cols(u2), F, g_cols(u2) == 0)
+            if k == 6:
+                empty3(4 * u2 + 1)
             empty3(4 * u2 + 2)
-            if k < 7:
-                for t in range(3):
-                    mm1(4 * k + 4 + t, ahead)
-            empty3(4 * u2 + 3, G_COLS)
+            for t in range(1, 3):
+                mm1(4 * k + 4 + t, ahead)
+            if g_cols(u2):
+                empty3(4 * u2 + 3, g_cols(u2))
             if k < 5:
-                s_interleave(P_END)
+                s_interleave(P_END if k < 4 else F)
 
+        for t in (2, 3):
+            add1(28 + t)
+            round1(28 + t)
+        turn(14)
+        mm2(27)
+        mm3(23)
+        turn(15)
+        gather1(14)
+        gather1(15)
+        hold = [free_banks.pop(0) for n in range(len(free_banks))]
+        add2(24)
+        hold.append(free_banks.pop(0))
+        add2(25)
+        mm3(21)
+        add2(26)
+        mm3(22)
+        free_banks.extend(hold)
+        add2(27)
+        finish_vector(23, 0, F // 2)
+        empty3(21)
+        empty3(22, F // 2, False)
         quant2(6)
         quant1(7)
-        scale_late(5, G_COLS, "h1g_%d" % H1G[7])
+        scale_late(5, F // 2, "h1g_%d" % H1G[7], 1)
         mm3(24)
         mm3(25)
+        finish_vector(23, F // 2, F)
+        finish_vector(22, F // 2, F)
         for t in range(4):
             mm2(28 + t)
         finish_vector(24)
+        empty3(25, F // 2, False)
+        scale_half(25)
+        add2(28)
+        hold = [free_banks.pop(0) for n in range(len(free_banks))]
+        add2(29)
         mm3(26)
-        finish_vector(25, 0, F // 2)
-        for t in range(4):
-            add2(28 + t)
-        store_late(5, G_COLS)
-        finish_vector(25, F // 2, F)
+        add2(30)
         mm3(27)
+        free_banks.extend(hold)
+        store_late(5, F // 2, 1)
+        add2(31)
+        store_half(25)
+        finish_vector(25, F // 2, F)
         quant2(7)
         finish_vector(26)
         finish_vector(27)

@@ -17,7 +17,7 @@ FP4X4 = mybir.dt.float4_e2m1fn_x4
 ALU = mybir.AluOpType
 
 NP = 128
-SPLIT = 192
+SPLIT = 160
 SPLIT1 = 240
 K0 = 3
 H1G = (0, 1, 2, 3, 4, 2, 3, 4)
@@ -45,10 +45,14 @@ def tile_parcel_band_hemisphere_coupling_t2_kernel(
         ident = keep.tile([NP, NP], F32, name="ident")
         a_raw, a_w, a_s = {}, {}, {}
         for h in range(2):
-            a_raw[h] = work.tile([NP, 2, P], U8, name="a_raw_%d" % h, tag="a_raw_%d" % h, bufs=1, align_bytes=64)
             a_w[h] = keep.tile([NP, 2, P], U8, name="a_w_%d" % h, align_bytes=64)
             a_s[h] = keep.tile([NP, 2, H], U8, name="a_s_%d" % h, align_bytes=64)
-        a_sraw = keep.tile([NP, 2, P], U8, name="a_sraw", align_bytes=64)
+        for h, lo, hi in ((0, 0, 1), (0, 1, 2), (1, 0, 2)):
+            tag = "a_raw_%d_%d" % (h, lo)
+            a_raw[h, lo] = work.tile([NP, hi - lo, P], U8, name=tag, tag=tag, bufs=1, align_bytes=64)
+        a_sraw = {}
+        for h in range(2):
+            a_sraw[h] = work.tile([NP, 2, H], U8, name="a_sraw_%d" % h, tag="a_sraw_%d" % h, bufs=1, align_bytes=64)
         b_w = keep.tile([NP, 2 * F], U8, name="b_w", align_bytes=64)
         b_s = keep.tile([NP, 1, F], U8, name="b_s", align_bytes=64)
         c_w = keep.tile([NP, 2, 2 * H], U8, name="c_w", align_bytes=64)
@@ -61,7 +65,8 @@ def tile_parcel_band_hemisphere_coupling_t2_kernel(
                 xt = keep.tile([NP, 4, F], BF16, name="x_%d_%d" % (w, k))
                 xs[w, k] = xt
 
-        nc.gpsimd.memset(a_sraw[:].bitcast(I32), 0)
+        nc.gpsimd.memset(a_sraw[0][:].bitcast(I32), 0)
+        nc.vector.memset(a_sraw[1][:].bitcast(I32), 0)
         nc.vector.memset(b_s[:].bitcast(I32), 0)
         nc.vector.memset(c_s[:].bitcast(I32), 0)
         make_identity(nc, ident[:])
@@ -71,46 +76,45 @@ def tile_parcel_band_hemisphere_coupling_t2_kernel(
 
         a_src = sc_words.bitcast(I32)
 
-        def load_a(h):
+        def load_a(h, lo, hi):
             nc.sync.dma_start(
-                out=a_raw[h][:].bitcast(I32),
-                in_=a_src[:, :, 256 * h : 256 * h + 256].rearrange("g p n -> p g n"),
+                out=a_raw[h, lo][:].bitcast(I32),
+                in_=a_src[lo:hi, :, 256 * h : 256 * h + 256].rearrange("g p n -> p g n"),
             )
 
         def load_scales(dst, src):
             for r in range(4):
-                nc.sync.dma_start(
-                    out=dst[r:NP:32].bitcast(I32),
-                    in_=src.bitcast(I32)[:, r:16:4, :].rearrange("g q n -> q g n"),
-                )
+                nc.sync.dma_start(out=dst[r:NP:32].bitcast(I32), in_=src[:, r:16:4, :].rearrange("g q n -> q g n"))
 
-        load_a(0)
-        load_scales(a_sraw, sc_scales)
+        load_a(0, 0, 1)
+        load_scales(a_sraw[0], sc_scales.bitcast(I32)[:, :, :NP])
         load_x(0, 0)
         load_x(0, 1)
-        load_a(1)
+        load_a(0, 1, 2)
+        load_a(1, 0, 2)
+        load_scales(a_sraw[1], sc_scales.bitcast(I32)[:, :, NP:])
         load_x(1, 0)
         load_x(1, 1)
-        load_scales(b_s, fb_scales)
+        load_scales(b_s, fb_scales.bitcast(I32))
         nc.sync.dma_start(out=b_w[:].bitcast(I32), in_=fb_words.bitcast(I32)[0])
         load_x(2, 0)
         load_x(2, 1)
         load_x(3, 0)
-        load_scales(c_s, hs_scales)
+        load_scales(c_s, hs_scales.bitcast(I32))
         load_x(3, 1)
         nc.sync.dma_start(out=c_w[:].bitcast(I32), in_=hs_words.bitcast(I32).rearrange("g p n -> p g n"))
         nc.sync.dma_start(out=gain_b, in_=gain.partition_broadcast(NP))
 
-        def perm_aw(h, lo=0, hi=4):
+        def perm_aw(h, lo, hi):
             nc.vector.tensor_copy(
-                out=a_w[h][:].bitcast(U16).rearrange("p g (t m) -> p g t m", t=4)[:, :, lo:hi, :],
-                in_=a_raw[h][:].bitcast(U16).rearrange("p g (m t) -> p g t m", t=4)[:, :, lo:hi, :],
+                out=a_w[h][:, lo:hi, :].bitcast(U16).rearrange("p g (t m) -> p g t m", t=4),
+                in_=a_raw[h, lo][:].bitcast(U16).rearrange("p g (m t) -> p g t m", t=4),
             )
 
-        def perm_as(h, lo=0, hi=4):
+        def perm_as(h):
             nc.vector.tensor_copy(
-                out=a_s[h][:].rearrange("p g (t m) -> p g t m", t=4)[:, :, lo:hi, :],
-                in_=a_sraw[:, :, H * h : H * h + H].rearrange("p g (m t) -> p g t m", t=4)[:, :, lo:hi, :],
+                out=a_s[h][:].rearrange("p g (t m) -> p g t m", t=4),
+                in_=a_sraw[h][:].rearrange("p g (m t) -> p g t m", t=4),
             )
 
         xg, xc, xsc, xslot = {}, {}, {}, {}
@@ -303,7 +307,7 @@ def tile_parcel_band_hemisphere_coupling_t2_kernel(
         def finish_vector(i, lo=0, hi=F, free=True):
             u, m = divmod(i, 4)
             w, g = divmod(u, 2)
-            res = work.tile([NP, hi - lo], F32, name="res_%d_%d" % (i, lo), tag="res", bufs=8)
+            res = work.tile([NP, hi - lo], F32, name="res_%d_%d" % (i, lo), bufs=1)
             nc.vector.tensor_tensor(
                 out=res[:],
                 in0=o[i][:, lo:hi],
@@ -372,44 +376,54 @@ def tile_parcel_band_hemisphere_coupling_t2_kernel(
                 nc.sync.dma_start(out=outs[g][m * NP : m * NP + NP, w, :cols], in_=late[:, whole * F :])
 
         x_interleave(0, 0, SPLIT, "S", "xg_0")
-        perm_aw(0)
+        perm_aw(0, 0, 1)
         perm_as(0)
         x_interleave(0, SPLIT, F, "V")
-        perm_as(1, 0, 2)
         x_quantize(0)
         for t in range(K0):
             mm1(t, (0,))
         x_interleave(1, 0, SPLIT1, "S", "xg_1")
         x_interleave(1, SPLIT1, F, "V")
-        perm_as(1, 2, 4)
+        perm_aw(0, 1, 2)
         x_quantize(1)
-        perm_aw(1)
-        x_interleave(2, X2_S, F, "G", "a_raw_1")
+        perm_aw(1, 0, 2)
+        perm_as(1)
+        x_interleave(2, X2_S, F, "G", "a_raw_1_0")
         x_interleave(2, 0, X2_S, "S")
         x_interleave(3, 0, F, "G", "xg_2")
 
-        for t in range(4):
-            mm1(t, (1,) if t < K0 else (0, 1))
+        mm1(1, (1,))
+        mm1(0, (1,))
+        mm1(3)
+        mm1(2, (1,))
+        mm1(5)
+        mm1(4)
+        for t in range(2):
             add1(t)
             round1(t)
-        for t in range(4, 7):
-            mm1(t)
+        mm1(6)
+        for t in range(2, 4):
             add1(t)
+            round1(t)
         for c in range(2):
             turn(c)
             gather1(c)
         mm1(7)
+        for t in range(4, 7):
+            add1(t)
         x_quantize(2)
+        mm1(8, (0,))
+        mm1(9, (0,))
         x_quantize(3)
+        mm1(9, (1,))
+        mm1(8, (1,))
         x_interleave(5, X5_S, F, "V", "xg_0")
         quant1(0)
         x_interleave(4, 0, F, "G", "h1g_0")
-        mm1(8)
-        mm1(9)
         add1(7)
         for t in range(4, 8):
             round1(t)
-        for t in range(4):
+        for t in (0, 2, 1, 3):
             mm2(t)
         add1(8)
         s_interleave(P_HEAD[0])
@@ -419,9 +433,9 @@ def tile_parcel_band_hemisphere_coupling_t2_kernel(
             turn(c)
             gather1(c)
         add2(2)
-        mm1(10)
-        add2(3)
         mm1(11)
+        add2(3)
+        mm1(10)
         add1(9, 0, F // 2)
         round1(8)
         s_interleave(P_HEAD[1])
@@ -444,64 +458,69 @@ def tile_parcel_band_hemisphere_coupling_t2_kernel(
             if k == 3:
                 x_interleave(6, F - X6_G - X7_G, F - X6_G, "G")
             mm3(4 * u2)
+            if k == 2:
+                mm3(1)
             if k in (4, 6):
+                mm1(4 * k + 3, (1,))
                 mm1(4 * k + 2, (1,))
-            if k > 2:
+            if k in (3, 7):
                 mm1(4 * k + 3)
+            mm2(4 * u1 + 1)
+            mm2(4 * u1)
             if k == 3:
                 nc.scalar.copy(out=gain3[:, F : 2 * F], in_=gain_b)
                 nc.scalar.copy(out=gain3[:, 2 * F :], in_=gain_b[:, :G_COLS])
-            empty3(4 * u2)
-            scale_now(4 * u2, 1)
             if k == 2:
-                mm3(1)
-                empty3(1)
-                scale_now(1, 1)
                 add1(9, F // 2, F)
+                for m in range(2):
+                    empty3(m)
+                    scale_now(m, 1)
                 round1(9)
             else:
+                if k < 7:
+                    mm3(4 * u2 + 1)
                 add1(4 * k)
+                empty3(4 * u2)
+                scale_now(4 * u2, 1)
                 round1(4 * k)
-            mm2(4 * u1)
-            mm2(4 * u1 + 1)
-            if k > 2:
                 add1(4 * k + 1)
                 round1(4 * k + 1)
-            mm2(4 * u1 + 2)
             if k == 7:
                 break
-            mm2(4 * u1 + 3)
-            add1(4 * k + 2)
-            round1(4 * k + 2)
-            if k > 2:
-                mm3(4 * u2 + 1)
-            add1(4 * k + 3)
-            round1(4 * k + 3)
             mm3(4 * u2 + 3)
+            mm2(4 * u1 + 3)
+            mm2(4 * u1 + 2)
+            for t in (2, 3):
+                add1(4 * k + t)
+                round1(4 * k + t)
+            mm1(4 * k + 6, ahead)
             add2(4 * u1)
-            mm1(4 * k + 4, ahead)
+            add2(4 * u1 + 1)
             if k == 2:
                 s_interleave(P_GAP)
             elif k < 6:
                 empty3(4 * u2 + 1)
-            add2(4 * u1 + 1)
             add2(4 * u1 + 2)
-            for c in range(2):
-                turn(2 * k + c)
-                gather1(2 * k + c)
+            turn(2 * k)
+            turn(2 * k + 1)
             mm3(4 * u2 + 2)
             add2(4 * u1 + 3)
-            finish_vector(4 * u2 + 3, g_cols(u2), F, g_cols(u2) == 0)
+            for t in (1, 0) if k in (2, 6) else (1, 3, 0):
+                mm1(4 * k + 4 + t, ahead)
+            gather1(2 * k)
+            gather1(2 * k + 1)
+            finish_vector(4 * u2 + 3, g_cols(u2), F, False)
             if k == 6:
                 empty3(4 * u2 + 1)
             empty3(4 * u2 + 2)
-            for t in range(1, 3):
-                mm1(4 * k + 4 + t, ahead)
             if g_cols(u2):
                 empty3(4 * u2 + 3, g_cols(u2))
+            else:
+                give_bank("o", 4 * u2 + 3)
             if k < 5:
                 s_interleave(P_END if k < 4 else F)
 
+        mm2(26)
         for t in (2, 3):
             add1(28 + t)
             round1(28 + t)
@@ -530,7 +549,7 @@ def tile_parcel_band_hemisphere_coupling_t2_kernel(
         mm3(25)
         finish_vector(23, F // 2, F)
         finish_vector(22, F // 2, F)
-        for t in range(4):
+        for t in (0, 2, 1, 3):
             mm2(28 + t)
         finish_vector(24)
         empty3(25, F // 2, False)
@@ -549,6 +568,7 @@ def tile_parcel_band_hemisphere_coupling_t2_kernel(
         quant2(7)
         finish_vector(26)
         finish_vector(27)
-        for t in range(4):
+        for t in (0, 2, 1, 3):
             mm3(28 + t)
+        for t in range(4):
             finish_vector(28 + t)

@@ -20,6 +20,7 @@ NP = 128
 SPLIT = 160
 SPLIT1 = 240
 K0 = 3
+RUN = 2
 H1G = (0, 1, 2, 3, 4, 2, 3, 4)
 G_COLS = 224
 X2_S = 320
@@ -117,16 +118,23 @@ def tile_parcel_band_hemisphere_coupling_t2_kernel(
                 in_=a_sraw[h][:].rearrange("p g (m t) -> p g t m", t=4),
             )
 
-        xg, xc, xsc, xslot = {}, {}, {}, {}
+        xg, xc, xsc, both, h2g = {}, {}, {}, {}, {}
 
         def x_interleave(v, lo, hi, eng, slot=None):
             w, k = divmod(v, 2)
             if slot is not None:
-                tile = work.tile([NP, F, 4], BF16, name="xg_%d_%d" % (v, lo), tag=slot, bufs=1, align_bytes=64)
-                xg[v] = [(0, tile)]
-                xslot[v] = slot
-            tile = xg[v][-1][1]
-            if eng in ("G", "G2"):
+                if v in (2, 4, 6):
+                    both[v] = work.tile([NP, 2 * F, 4], BF16, name="xg_%d" % v, tag=slot, bufs=1, align_bytes=64)
+                    xg[v] = both[v][:, :F, :]
+                    if v == 2:
+                        xg[3] = both[v][:, F:, :]
+                    else:
+                        h2g[v - 3] = both[v][:, F:, :]
+                else:
+                    one = work.tile([NP, F, 4], BF16, name="xg_%d" % v, tag=slot, bufs=1, align_bytes=64)
+                    xg[v] = one[:]
+            tile = xg[v]
+            if eng == "G":
                 nc.gpsimd.tensor_scalar(
                     out=tile[:, lo:hi, :],
                     in0=xs[w, k][:, :, lo:hi].rearrange("p t c -> p c t"),
@@ -157,18 +165,22 @@ def tile_parcel_band_hemisphere_coupling_t2_kernel(
                     todo[0] = [v, lo + n, hi]
 
         def x_quantize(v):
-            c = work.tile([NP, F], U32, name="xc_%d" % v, tag="xc", bufs=6, align_bytes=64)
-            s = work.tile([NP, F], U8, name="xsc_%d" % v, tag="xsc", bufs=6, align_bytes=64)
-            for n, (lo, tile) in enumerate(xg[v]):
-                width = (xg[v][n + 1][0] if n + 1 < len(xg[v]) else F) - lo
-                nc.vector.quantize_mx(
-                    out=c[:, lo : lo + width].bitcast(FP8X4),
-                    scales=s[:, lo : lo + width],
-                    in_=tile[:, lo : lo + width, :].rearrange("p f t -> p (f t)"),
-                )
-            xc[v], xsc[v] = c, s
+            c = work.tile([NP, F], U32, name="xc_%d" % v, tag="xc", bufs=4, align_bytes=64)
+            s = work.tile([NP, F], U8, name="xsc_%d" % v, tag="xsc", bufs=4, align_bytes=64)
+            nc.vector.quantize_mx(out=c[:].bitcast(FP8X4), scales=s[:], in_=xg[v].rearrange("p f t -> p (f t)"))
+            xc[v], xsc[v] = c[:], s[:]
 
-        d, h1, h1t, h1g, h1c, h1s, e, h2g, h2c, h2s, o, raw, h1b = ({} for i in range(13))
+        def both_quantize(v):
+            c = work.tile([NP, 2 * F], U32, name="bc_%d" % v, bufs=1, align_bytes=64)
+            s = work.tile([NP, 2 * F], U8, name="bs_%d" % v, bufs=1, align_bytes=64)
+            nc.vector.quantize_mx(out=c[:].bitcast(FP8X4), scales=s[:], in_=both[v][:].rearrange("p f t -> p (f t)"))
+            xc[v], xsc[v] = c[:, :F], s[:, :F]
+            if v == 2:
+                xc[3], xsc[3] = c[:, F:], s[:, F:]
+            else:
+                h2c[v - 3], h2s[v - 3] = c[:, F:], s[:, F:]
+
+        d, h1, h1t, h1g, h1c, h1s, e, h2c, h2s, o, raw, h1b = ({} for i in range(12))
 
         free_banks = ["bank_%d" % b for b in range(8)]
         bank_of = {}
@@ -191,8 +203,8 @@ def tile_parcel_band_hemisphere_coupling_t2_kernel(
                     out=acc[:],
                     lhsT=a_w[h][:, k, 256 * t : 256 * t + 256].bitcast(FP4X4),
                     lhsT_scale=a_s[h][:, k, NP * t : NP * t + NP],
-                    rhs=xc[2 * w + k][:].bitcast(FP8X4),
-                    rhs_scale=xsc[2 * w + k][:],
+                    rhs=xc[2 * w + k].bitcast(FP8X4),
+                    rhs_scale=xsc[2 * w + k],
                     start=(k == 0),
                     stop=(k == 1),
                 )
@@ -264,13 +276,14 @@ def tile_parcel_band_hemisphere_coupling_t2_kernel(
 
         def add2(i):
             u, b = divmod(i, 4)
-            if b == 0:
-                h2g[u] = work.tile([NP, F, 4], BF16, name="h2g_%d" % u, tag="h2g_%d" % (u % 2), bufs=1, align_bytes=64)
+            if u not in h2g:
+                one = work.tile([NP, F, 4], BF16, name="h2g_%d" % u, tag="h2g", bufs=2, align_bytes=64)
+                h2g[u] = one[:]
             cols = slice(NP * b, NP * b + NP)
             nc.vector.tensor_tensor(
-                out=h2g[u][:, cols, :].rearrange("p (a i) t -> p a t i", i=4),
-                in0=e[i][:].rearrange("p t (a i) -> p a t i", i=4),
-                in1=h1[u][:, :, cols].rearrange("p t (a i) -> p a t i", i=4),
+                out=h2g[u][:, cols, :].rearrange("p (a i) t -> p a t i", i=RUN),
+                in0=e[i][:].rearrange("p t (a i) -> p a t i", i=RUN),
+                in1=h1[u][:, :, cols].rearrange("p t (a i) -> p a t i", i=RUN),
                 op=ALU.add,
             )
             give_bank("e", i)
@@ -278,8 +291,8 @@ def tile_parcel_band_hemisphere_coupling_t2_kernel(
         def quant2(u):
             c = work.tile([NP, F], U32, name="h2c_%d" % u, tag="h2c", bufs=3, align_bytes=64)
             s = work.tile([NP, F], U8, name="h2s_%d" % u, tag="h2s", bufs=3, align_bytes=64)
-            nc.vector.quantize_mx(out=c[:].bitcast(FP8X4), scales=s[:], in_=h2g[u][:].rearrange("p f t -> p (f t)"))
-            h2c[u], h2s[u] = c, s
+            nc.vector.quantize_mx(out=c[:].bitcast(FP8X4), scales=s[:], in_=h2g[u].rearrange("p f t -> p (f t)"))
+            h2c[u], h2s[u] = c[:], s[:]
 
         def mm3(i):
             u, m = divmod(i, 4)
@@ -289,8 +302,8 @@ def tile_parcel_band_hemisphere_coupling_t2_kernel(
                 out=bank[:],
                 lhsT=c_w[:, g, 256 * m : 256 * m + 256].bitcast(FP4X4),
                 lhsT_scale=c_s[:, g, NP * m : NP * m + NP],
-                rhs=h2c[u][:].bitcast(FP8X4),
-                rhs_scale=h2s[u][:],
+                rhs=h2c[u].bitcast(FP8X4),
+                rhs_scale=h2s[u],
                 start=True,
                 stop=True,
             )
@@ -390,7 +403,7 @@ def tile_parcel_band_hemisphere_coupling_t2_kernel(
         perm_as(1)
         x_interleave(2, X2_S, F, "G", "a_raw_1_0")
         x_interleave(2, 0, X2_S, "S")
-        x_interleave(3, 0, F, "G", "xg_2")
+        x_interleave(3, 0, F, "G")
 
         mm1(1, (1,))
         mm1(0, (1,))
@@ -411,13 +424,9 @@ def tile_parcel_band_hemisphere_coupling_t2_kernel(
         mm1(7)
         for t in range(4, 7):
             add1(t)
-        x_quantize(2)
-        mm1(8, (0,))
-        mm1(9, (0,))
-        x_quantize(3)
-        mm1(9, (1,))
-        mm1(8, (1,))
         x_interleave(5, X5_S, F, "V", "xg_0")
+        both_quantize(2)
+        mm1(8)
         quant1(0)
         x_interleave(4, 0, F, "G", "h1g_0")
         add1(7)
@@ -425,6 +434,7 @@ def tile_parcel_band_hemisphere_coupling_t2_kernel(
             round1(t)
         for t in (0, 2, 1, 3):
             mm2(t)
+        mm1(9)
         add1(8)
         s_interleave(P_HEAD[0])
         add2(0)
@@ -442,12 +452,14 @@ def tile_parcel_band_hemisphere_coupling_t2_kernel(
         for k in range(2, 8):
             u1, u2, u3 = k - 1, k - 2, k - 3
             ahead = (0,) if k in (3, 5) else (0, 1)
-            if 3 <= k < 7:
-                x_quantize(k + 1)
             if k in (4, 6):
+                x_quantize(k + 1)
                 mm1(4 * k, (1,))
                 mm1(4 * k + 1, (1,))
-            quant2(u2)
+            if k in (3, 5):
+                both_quantize(k + 1)
+            else:
+                quant2(u2)
             quant1(u1)
             last = "h1g_%d" % H1G[u1]
             if k == 2:

@@ -21,15 +21,12 @@ SPLIT = 160
 SPLIT1 = 240
 K0 = 3
 RUN = 2
-H1G = (0, 1, 2, 3, 4, 2, 3, 4)
-G_COLS = 224
-X2_S = 320
-X5_S = 448
-X6_G = 96
-X7_G = 256
-P_HEAD = (224, 224)
-P_GAP = 96
-P_END = 192
+G_COLS = 352
+T_COLS = 128
+X2_S = 384
+X5_S = 224
+X7_G = 384
+P_HEAD = (224, 288)
 
 
 def tile_parcel_band_hemisphere_coupling_t2_kernel(
@@ -63,7 +60,7 @@ def tile_parcel_band_hemisphere_coupling_t2_kernel(
         xs = {}
         for w in range(T):
             for k in range(2):
-                xt = keep.tile([NP, 4, F], BF16, name="x_%d_%d" % (w, k))
+                xt = work.tile([NP, 4, F], BF16, name="x_%d_%d" % (w, k), tag="x_%d_%d" % (w, k), bufs=1, align_bytes=64)
                 xs[w, k] = xt
 
         nc.gpsimd.memset(a_sraw[0][:].bitcast(I32), 0)
@@ -118,21 +115,16 @@ def tile_parcel_band_hemisphere_coupling_t2_kernel(
                 in_=a_sraw[h][:].rearrange("p g (m t) -> p g t m", t=4),
             )
 
-        xg, xc, xsc, both, h2g = {}, {}, {}, {}, {}
+        xg, xc, xsc, window, pair = {}, {}, {}, {}, {}
 
         def x_interleave(v, lo, hi, eng, slot=None):
             w, k = divmod(v, 2)
-            if slot is not None:
-                if v in (2, 4, 6):
-                    both[v] = work.tile([NP, 2 * F, 4], BF16, name="xg_%d" % v, tag=slot, bufs=1, align_bytes=64)
-                    xg[v] = both[v][:, :F, :]
-                    if v == 2:
-                        xg[3] = both[v][:, F:, :]
-                    else:
-                        h2g[v - 3] = both[v][:, F:, :]
-                else:
-                    one = work.tile([NP, F, 4], BF16, name="xg_%d" % v, tag=slot, bufs=1, align_bytes=64)
-                    xg[v] = one[:]
+            if slot is not None and w == 0:
+                one = work.tile([NP, F, 4], BF16, name="xg_%d" % v, tag=slot, bufs=1, align_bytes=64)
+                xg[v] = one[:]
+            elif slot is not None:
+                window[w] = work.tile([NP, 2 * F, 4], BF16, name="xw_%d" % w, tag=slot, bufs=1, align_bytes=64)
+                xg[2 * w], xg[2 * w + 1] = window[w][:, :F, :], window[w][:, F:, :]
             tile = xg[v]
             if eng == "G":
                 nc.gpsimd.tensor_scalar(
@@ -151,36 +143,45 @@ def tile_parcel_band_hemisphere_coupling_t2_kernel(
             else:
                 nc.scalar.copy(out=dst, in_=src)
 
-        todo = [[5, 0, X5_S], [6, 0, F - X6_G - X7_G], [7, 0, F]]
+        todo = [[5, 0, X5_S], [6, 0, F], [7, 0, F - X7_G]]
 
         def s_interleave(width):
             while width > 0 and todo:
                 v, lo, hi = todo[0]
                 n = min(width, hi - lo)
-                x_interleave(v, lo, lo + n, "S", "xg_1" if v not in xg else None)
+                x_interleave(v, lo, lo + n, "S", "xg_0" if v not in xg else None)
                 width = width - n
                 if lo + n == hi:
                     todo.pop(0)
                 else:
                     todo[0] = [v, lo + n, hi]
 
+        def quantize(src, name, tag, bufs):
+            width = src.shape[1] // 4
+            c = work.tile([NP, width], U32, name="c_" + name, tag="c_" + tag, bufs=bufs, align_bytes=64)
+            s = work.tile([NP, width], U8, name="s_" + name, tag="s_" + tag, bufs=bufs, align_bytes=64)
+            nc.vector.quantize_mx(out=c[:].bitcast(FP8X4), scales=s[:], in_=src)
+            return c[:], s[:]
+
         def x_quantize(v):
-            c = work.tile([NP, F], U32, name="xc_%d" % v, tag="xc", bufs=4, align_bytes=64)
-            s = work.tile([NP, F], U8, name="xsc_%d" % v, tag="xsc", bufs=4, align_bytes=64)
-            nc.vector.quantize_mx(out=c[:].bitcast(FP8X4), scales=s[:], in_=xg[v].rearrange("p f t -> p (f t)"))
-            xc[v], xsc[v] = c[:], s[:]
+            xc[v], xsc[v] = quantize(xg[v].rearrange("p f t -> p (f t)"), "x%d" % v, "one", 4)
 
-        def both_quantize(v):
-            c = work.tile([NP, 2 * F], U32, name="bc_%d" % v, bufs=1, align_bytes=64)
-            s = work.tile([NP, 2 * F], U8, name="bs_%d" % v, bufs=1, align_bytes=64)
-            nc.vector.quantize_mx(out=c[:].bitcast(FP8X4), scales=s[:], in_=both[v][:].rearrange("p f t -> p (f t)"))
-            xc[v], xsc[v] = c[:, :F], s[:, :F]
-            if v == 2:
-                xc[3], xsc[3] = c[:, F:], s[:, F:]
-            else:
-                h2c[v - 3], h2s[v - 3] = c[:, F:], s[:, F:]
+        def window_quantize(w):
+            c, s = quantize(window[w][:].rearrange("p f t -> p (f t)"), "w%d" % w, "window", 2)
+            for k in range(2):
+                xc[2 * w + k], xsc[2 * w + k] = c[:, F * k : F * k + F], s[:, F * k : F * k + F]
 
-        d, h1, h1t, h1g, h1c, h1s, e, h2c, h2s, o, raw, h1b = ({} for i in range(12))
+        def pair_half(k, half):
+            if k not in pair:
+                pair[k] = work.tile([NP, 2, 4 * F], BF16, name="pair_%d" % k, tag="pair", bufs=2, align_bytes=64)
+            return pair[k][:, half, :]
+
+        def pair_quantize(k):
+            c, s = quantize(pair[k][:].rearrange("p h n -> p (h n)"), "p%d" % k, "pair", 2)
+            h1c[k - 2], h1s[k - 2] = c[:, :F], s[:, :F]
+            h2c[k - 3], h2s[k - 3] = c[:, F:], s[:, F:]
+
+        d, h1, h1t, h1g, h1c, h1s, e, h2g, h2c, h2s, o, raw, h1b = ({} for i in range(13))
 
         free_banks = ["bank_%d" % b for b in range(8)]
         bank_of = {}
@@ -245,19 +246,20 @@ def tile_parcel_band_hemisphere_coupling_t2_kernel(
 
         def gather1(j):
             u, c = divmod(j, 2)
-            if c == 0:
-                h1g[u] = work.tile([NP, 4, NP, 2], F32, name="h1g_%d" % u, tag="h1g_%d" % H1G[u], bufs=1, align_bytes=64)
+            if c == 0 and u in (0, 7):
+                one = work.tile([NP, 4 * F], BF16, name="h1g_%d" % u, tag="h1g_%d" % u, bufs=1, align_bytes=64)
+                h1g[u] = one[:]
+            elif c == 0:
+                h1g[u] = pair_half(u + 2, 0)
+            words = h1g[u].bitcast(F32).rearrange("p (t q a) -> p t q a", t=4, a=2)
             nc.scalar.copy(
-                out=h1g[u][:, 2 * c : 2 * c + 2, :, :],
+                out=words[:, 2 * c : 2 * c + 2, :, :],
                 in_=h1t[j][:].rearrange("p t a q -> p t q a"),
             )
             give_bank("t", j)
 
         def quant1(u):
-            c = work.tile([NP, F], U32, name="h1c_%d" % u, tag="h1c", bufs=3, align_bytes=64)
-            s = work.tile([NP, F], U8, name="h1s_%d" % u, tag="h1s", bufs=3, align_bytes=64)
-            nc.vector.quantize_mx(out=c[:].bitcast(FP8X4), scales=s[:], in_=h1g[u][:].rearrange("p t q a -> p (t q a)").bitcast(BF16))
-            h1c[u], h1s[u] = c, s
+            h1c[u], h1s[u] = quantize(h1g[u], "h1_%d" % u, "one", 4)
 
         def mm2(i):
             u, b = divmod(i, 4)
@@ -276,9 +278,11 @@ def tile_parcel_band_hemisphere_coupling_t2_kernel(
 
         def add2(i):
             u, b = divmod(i, 4)
-            if u not in h2g:
-                one = work.tile([NP, F, 4], BF16, name="h2g_%d" % u, tag="h2g", bufs=2, align_bytes=64)
+            if b == 0 and u >= 6:
+                one = work.tile([NP, F, 4], BF16, name="h2g_%d" % u, tag="h2g_%d" % u, bufs=1, align_bytes=64)
                 h2g[u] = one[:]
+            elif b == 0:
+                h2g[u] = pair_half(u + 3, 1).rearrange("p (f t) -> p f t", t=4)
             cols = slice(NP * b, NP * b + NP)
             nc.vector.tensor_tensor(
                 out=h2g[u][:, cols, :].rearrange("p (a i) t -> p a t i", i=RUN),
@@ -289,10 +293,7 @@ def tile_parcel_band_hemisphere_coupling_t2_kernel(
             give_bank("e", i)
 
         def quant2(u):
-            c = work.tile([NP, F], U32, name="h2c_%d" % u, tag="h2c", bufs=3, align_bytes=64)
-            s = work.tile([NP, F], U8, name="h2s_%d" % u, tag="h2s", bufs=3, align_bytes=64)
-            nc.vector.quantize_mx(out=c[:].bitcast(FP8X4), scales=s[:], in_=h2g[u].rearrange("p f t -> p (f t)"))
-            h2c[u], h2s[u] = c[:], s[:]
+            h2c[u], h2s[u] = quantize(h2g[u].rearrange("p f t -> p (f t)"), "h2_%d" % u, "one", 4)
 
         def mm3(i):
             u, m = divmod(i, 4)
@@ -309,84 +310,53 @@ def tile_parcel_band_hemisphere_coupling_t2_kernel(
             )
             o[i] = bank
 
-        def store(i, count, res, queue=nc.sync):
+        def store(i, lo, hi, res):
             u, m = divmod(i, 4)
-            w, g = divmod(u, 2)
-            queue.dma_start(
-                out=outs[g][NP * m : NP * (m + count), w, :].rearrange("(m p) f -> p m f", p=NP),
-                in_=res,
-            )
+            nc.sync.dma_start(out=outs[u % 2][NP * m : NP * m + NP, u // 2, lo:hi], in_=res)
 
         def finish_vector(i, lo=0, hi=F, free=True):
-            u, m = divmod(i, 4)
-            w, g = divmod(u, 2)
-            res = work.tile([NP, hi - lo], F32, name="res_%d_%d" % (i, lo), bufs=1)
-            nc.vector.tensor_tensor(
-                out=res[:],
-                in0=o[i][:, lo:hi],
-                in1=gain_b[:, lo:hi],
-                op=ALU.mult,
-            )
-            if hi == F and free:
+            res = work.tile([NP, hi - lo], F32, name="res_%d_%d" % (i, lo), tag="res", bufs=8)
+            nc.vector.tensor_tensor(out=res[:], in0=o[i][:, lo:hi], in1=gain_b[:, lo:hi], op=ALU.mult)
+            if free:
                 give_bank("o", i)
-            nc.sync.dma_start(out=outs[g][NP * m : NP * m + NP, w, lo:hi], in_=res[:])
+            store(i, lo, hi, res[:])
 
         def empty3(i, hi=F, free=True):
             u, m = divmod(i, 4)
             if u not in raw:
-                raw[u] = work.tile([NP, 4, F], F32, name="raw_%d" % u, tag="raw", bufs=3)
-            nc.scalar.copy(
-                out=raw[u][:, m, :hi],
-                in_=o[i][:, :hi],
-            )
+                raw[u] = work.tile([NP, 4 * F], F32, name="raw_%d" % u, tag="raw", bufs=3)
+            nc.scalar.copy(out=raw[u][:, F * m : F * m + hi], in_=o[i][:, :hi])
             if free:
                 give_bank("o", i)
 
-        def scale_now(i, count):
+        scaled = {}
+
+        def scale_gpsimd(i, width, after=None):
             u, m = divmod(i, 4)
-            part = raw[u][:, m : m + count, :]
-            nc.gpsimd.tensor_tensor(
-                out=part, in0=part, in1=gain_b.unsqueeze(1).to_broadcast([NP, count, F]), op=ALU.mult
+            src = raw[u][:, F * m : F * m + width]
+            dst = src
+            if after is not None:
+                late = work.tile([NP, width], F32, name="late_%d" % i, tag=after, bufs=1, align_bytes=64)
+                dst = late[:]
+            nc.gpsimd.tensor_tensor(out=dst, in0=src, in1=gain3[:, :width], op=ALU.mult)
+            scaled[i] = dst
+
+        def store_scaled(i):
+            width = scaled[i].shape[1]
+            for n in range((width + F - 1) // F):
+                cols = min(F, width - F * n)
+                store(i + n, 0, cols, scaled[i][:, F * n : F * n + cols])
+
+        def round_gpsimd(i):
+            u, t = divmod(i, 4)
+            nc.gpsimd.tensor_scalar(
+                out=h1b[u][:, t, :].rearrange("p (a m e) -> p a m e", a=2, e=2),
+                in0=h1[u][:, t, :].rearrange("p (m a e) -> p a m e", a=2, e=2),
+                scalar1=1.0,
+                scalar2=0.0,
+                op0=ALU.mult,
+                op1=ALU.add,
             )
-            store(i, count, part)
-
-        lates = {}
-
-        def g_cols(u):
-            return G_COLS if 0 < u < 4 else 0
-
-        def scale_half(i):
-            u, m = divmod(i, 4)
-            part = raw[u][:, m, : F // 2]
-            nc.gpsimd.tensor_tensor(out=part, in0=part, in1=gain_b[:, : F // 2], op=ALU.mult)
-
-        def store_half(i):
-            u, m = divmod(i, 4)
-            nc.sync.dma_start(out=outs[u % 2][NP * m : NP * m + NP, u // 2, : F // 2], in_=raw[u][:, m, : F // 2])
-
-        def scale_late(u, cols, after, whole=2):
-            w, g = divmod(u, 2)
-            first = 2 if u == 0 else 1
-            whole = 1 if u == 0 else whole
-            width = whole * F + cols
-            late = work.tile([NP, width], F32, name="late_%d" % u, tag=after, bufs=1, align_bytes=64)
-            nc.gpsimd.tensor_tensor(
-                out=late[:],
-                in0=raw[u][:].rearrange("p m f -> p (m f)")[:, first * F : first * F + width],
-                in1=gain3[:, :width],
-                op=ALU.mult,
-            )
-            lates[u] = late
-
-        def store_late(u, cols, whole=2):
-            w, g = divmod(u, 2)
-            first = 2 if u == 0 else 1
-            whole = 1 if u == 0 else whole
-            late = lates[u]
-            store(4 * u + first, whole, late[:, : whole * F].rearrange("p (m f) -> p m f", f=F))
-            if cols:
-                m = first + whole
-                nc.sync.dma_start(out=outs[g][m * NP : m * NP + NP, w, :cols], in_=late[:, whole * F :])
 
         x_interleave(0, 0, SPLIT, "S", "xg_0")
         perm_aw(0, 0, 1)
@@ -424,11 +394,11 @@ def tile_parcel_band_hemisphere_coupling_t2_kernel(
         mm1(7)
         for t in range(4, 7):
             add1(t)
-        x_interleave(5, X5_S, F, "V", "xg_0")
-        both_quantize(2)
+        window_quantize(1)
         mm1(8)
         quant1(0)
         x_interleave(4, 0, F, "G", "h1g_0")
+        x_interleave(5, X5_S, F, "G")
         add1(7)
         for t in range(4, 8):
             round1(t)
@@ -439,148 +409,198 @@ def tile_parcel_band_hemisphere_coupling_t2_kernel(
         s_interleave(P_HEAD[0])
         add2(0)
         add2(1)
-        for c in range(2, 4):
+        for c in (2, 3):
             turn(c)
             gather1(c)
+        mm1(10)
         add2(2)
         mm1(11)
         add2(3)
-        mm1(10)
-        add1(9, 0, F // 2)
         round1(8)
+        add1(9)
+        round1(9)
+        mm1(12)
+        add1(10)
+        round1(10)
+        mm1(13)
+        add1(11)
+        mm1(14)
         s_interleave(P_HEAD[1])
-        for k in range(2, 8):
-            u1, u2, u3 = k - 1, k - 2, k - 3
-            ahead = (0,) if k in (3, 5) else (0, 1)
-            if k in (4, 6):
-                x_quantize(k + 1)
-                mm1(4 * k, (1,))
-                mm1(4 * k + 1, (1,))
-            if k in (3, 5):
-                both_quantize(k + 1)
-            else:
-                quant2(u2)
-            quant1(u1)
-            last = "h1g_%d" % H1G[u1]
-            if k == 2:
-                x_interleave(6, F - X6_G, F, "G", last)
-            else:
-                scale_late(u3, g_cols(u3), last)
-                store_late(u3, g_cols(u3))
-            if k == 3:
-                x_interleave(6, F - X6_G - X7_G, F - X6_G, "G")
-            mm3(4 * u2)
-            if k == 2:
-                mm3(1)
-            if k in (4, 6):
-                mm1(4 * k + 3, (1,))
-                mm1(4 * k + 2, (1,))
-            if k in (3, 7):
+
+        def late(u, cols, after):
+            scale_gpsimd(4 * u + 1, 2 * F + cols, after)
+            store_scaled(4 * u + 1)
+
+        def now(u):
+            empty3(4 * u)
+            scale_gpsimd(4 * u, F)
+            store_scaled(4 * u)
+
+        for k in range(3, 7):
+            u1, u2 = k - 2, k - 3
+            if k % 2 == 0:
+                window_quantize(k // 2)
+                mm1(4 * k)
+                mm1(4 * k + 1)
+                pair_quantize(k)
+                late(k - 4, G_COLS, "h1g_0" if k == 4 else "xg_0")
+                for c in range(2):
+                    gather1(2 * k - 2 + c)
+                mm2(4 * u1)
+                mm2(4 * u1 + 1)
+                mm3(4 * u2)
+                for t in range(2):
+                    add1(4 * k + t)
+                    round1(4 * k + t)
+                mm2(4 * u1 + 2)
+                mm2(4 * u1 + 3)
+                now(u2)
+                s_interleave(F)
+                add2(4 * u1)
+                mm3(4 * u2 + 3)
+                add2(4 * u1 + 1)
+                mm3(4 * u2 + 1)
+                mm1(4 * k + 2)
+                add2(4 * u1 + 2)
+                finish_vector(4 * u2 + 3, G_COLS, F, False)
                 mm1(4 * k + 3)
-            mm2(4 * u1 + 1)
-            mm2(4 * u1)
-            if k == 3:
-                nc.scalar.copy(out=gain3[:, F : 2 * F], in_=gain_b)
-                nc.scalar.copy(out=gain3[:, 2 * F :], in_=gain_b[:, :G_COLS])
-            if k == 2:
-                add1(9, F // 2, F)
-                for m in range(2):
-                    empty3(m)
-                    scale_now(m, 1)
-                round1(9)
+                empty3(4 * u2 + 3, G_COLS)
+                add2(4 * u1 + 3)
+                mm3(4 * u2 + 2)
+                empty3(4 * u2 + 1)
+                add1(4 * k + 2)
+                mm1(4 * k + 4)
+                empty3(4 * u2 + 2)
+                round1(4 * k + 2)
+                add1(4 * k + 3)
+                mm1(4 * k + 5)
+                mm1(4 * k + 6)
+                round1(4 * k + 3)
             else:
-                if k < 7:
-                    mm3(4 * u2 + 1)
+                pair_quantize(k)
+                if k == 3:
+                    round_gpsimd(11)
+                    x_interleave(7, F - X7_G, F, "G")
+                else:
+                    late(k - 4, G_COLS, "x_%d_0" % (k // 2))
+                mm3(4 * u2)
+                mm2(4 * u1)
+                mm1(4 * k + 3)
                 add1(4 * k)
-                empty3(4 * u2)
-                scale_now(4 * u2, 1)
                 round1(4 * k)
+                now(u2)
+                if k == 3:
+                    nc.scalar.copy(out=gain3[:, F : 2 * F], in_=gain_b)
+                    nc.scalar.copy(out=gain3[:, 2 * F :], in_=gain_b[:, :G_COLS])
                 add1(4 * k + 1)
                 round1(4 * k + 1)
-            if k == 7:
-                break
-            mm3(4 * u2 + 3)
-            mm2(4 * u1 + 3)
-            mm2(4 * u1 + 2)
-            for t in (2, 3):
-                add1(4 * k + t)
-                round1(4 * k + t)
-            mm1(4 * k + 6, ahead)
-            add2(4 * u1)
-            add2(4 * u1 + 1)
-            if k == 2:
-                s_interleave(P_GAP)
-            elif k < 6:
+                mm2(4 * u1 + 1)
+                add1(4 * k + 2)
+                round1(4 * k + 2)
+                mm2(4 * u1 + 2)
+                mm2(4 * u1 + 3)
+                add2(4 * u1)
+                add1(4 * k + 3)
+                round1(4 * k + 3)
+                mm3(4 * u2 + 3)
+                add2(4 * u1 + 1)
+                for c in range(2):
+                    turn(2 * k - 2 + c)
+                add2(4 * u1 + 2)
+                turn(2 * k)
+                add2(4 * u1 + 3)
+                turn(2 * k + 1)
+                for c in range(2):
+                    gather1(2 * k - 2 + c)
+                mm3(4 * u2 + 1)
+                mm3(4 * u2 + 2)
+                finish_vector(4 * u2 + 3, G_COLS, F, False)
+                empty3(4 * u2 + 3, G_COLS)
                 empty3(4 * u2 + 1)
-            add2(4 * u1 + 2)
-            turn(2 * k)
-            turn(2 * k + 1)
-            mm3(4 * u2 + 2)
-            add2(4 * u1 + 3)
-            for t in (1, 0) if k in (2, 6) else (1, 3, 0):
-                mm1(4 * k + 4 + t, ahead)
-            gather1(2 * k)
-            gather1(2 * k + 1)
-            finish_vector(4 * u2 + 3, g_cols(u2), F, False)
-            if k == 6:
-                empty3(4 * u2 + 1)
-            empty3(4 * u2 + 2)
-            if g_cols(u2):
-                empty3(4 * u2 + 3, g_cols(u2))
-            else:
-                give_bank("o", 4 * u2 + 3)
-            if k < 5:
-                s_interleave(P_END if k < 4 else F)
+                empty3(4 * u2 + 2)
 
-        mm2(26)
-        for t in (2, 3):
-            add1(28 + t)
-            round1(28 + t)
-        turn(14)
-        mm2(27)
-        mm3(23)
-        turn(15)
-        gather1(14)
-        gather1(15)
-        hold = [free_banks.pop(0) for n in range(len(free_banks))]
-        add2(24)
-        hold.append(free_banks.pop(0))
-        add2(25)
-        mm3(21)
-        add2(26)
-        mm3(22)
-        free_banks.extend(hold)
-        add2(27)
-        finish_vector(23, 0, F // 2)
-        empty3(21)
-        empty3(22, F // 2, False)
-        quant2(6)
+        mm1(31)
+        pair_quantize(7)
+        late(3, G_COLS, "x_3_0")
+        for c in range(2):
+            turn(12 + c)
+        add1(28)
+        round1(28)
+        gather1(12)
+        add1(29)
+        round1(29)
+        gather1(13)
+        for t in range(2):
+            mm2(20 + t)
+        add1(30)
+        round1(30)
+        add1(31)
+        round_gpsimd(31)
+        for t in range(2, 4):
+            mm2(20 + t)
+        mm3(16)
+        add2(20)
+        mm3(17)
+        add2(21)
+        for c in range(2):
+            turn(14 + c)
+        empty3(17)
+        add2(22)
+        mm3(18)
+        add2(23)
+        mm3(19)
+        finish_vector(16)
+        for c in range(2):
+            gather1(14 + c)
+        empty3(18)
+        pair_quantize(8)
         quant1(7)
-        scale_late(5, F // 2, "h1g_%d" % H1G[7], 1)
+        scale_gpsimd(17, F, "h1g_7")
+        mm3(20)
+        finish_vector(19, T_COLS, F, False)
+        empty3(19, T_COLS)
+        scale_gpsimd(18, F + T_COLS)
+        for t in range(4):
+            mm2(24 + t)
+        finish_vector(20)
+        mm3(23)
+        add2(24)
+        store_scaled(17)
+        mm3(21)
+        add2(25)
+        mm3(22)
+        empty3(21)
+        add2(26)
+        mm2(28)
+        empty3(22)
+        add2(27)
+        mm2(29)
+        finish_vector(23, T_COLS, F, False)
+        store_scaled(18)
+        empty3(23, T_COLS)
+        quant2(6)
+        scale_gpsimd(21, F, "h2g_6")
+        scale_gpsimd(22, F + T_COLS)
+        mm2(30)
+        mm2(31)
         mm3(24)
-        mm3(25)
-        finish_vector(23, F // 2, F)
-        finish_vector(22, F // 2, F)
-        for t in (0, 2, 1, 3):
-            mm2(28 + t)
-        finish_vector(24)
-        empty3(25, F // 2, False)
-        scale_half(25)
         add2(28)
-        hold = [free_banks.pop(0) for n in range(len(free_banks))]
+        mm3(25)
         add2(29)
-        mm3(26)
+        finish_vector(24)
+        store_scaled(21)
+        hold = [free_banks.pop(0) for n in range(len(free_banks))]
         add2(30)
+        mm3(26)
+        add2(31)
         mm3(27)
         free_banks.extend(hold)
-        store_late(5, F // 2, 1)
-        add2(31)
-        store_half(25)
-        finish_vector(25, F // 2, F)
+        finish_vector(25)
+        store_scaled(22)
         quant2(7)
         finish_vector(26)
         finish_vector(27)
-        for t in (0, 2, 1, 3):
+        for t in range(4):
             mm3(28 + t)
         for t in range(4):
             finish_vector(28 + t)

@@ -15,6 +15,7 @@ U16 = mybir.dt.uint16
 FP8X4 = mybir.dt.float8_e4m3fn_x4
 FP4X4 = mybir.dt.float4_e2m1fn_x4
 ALU = mybir.AluOpType
+ACT = mybir.ActivationFunctionType
 
 NP = 128
 SPLIT = 160
@@ -22,10 +23,12 @@ SPLIT1 = 240
 K0 = 3
 RUN = 2
 G_COLS = 352
-T_COLS = 128
+T_COLS = 256
+P7_COLS = 288
+T9_COLS = 512
 X2_S = 384
 X5_S = 224
-X7_G = 384
+X7_G = 416
 P_HEAD = (224, 288)
 
 
@@ -321,11 +324,11 @@ def tile_parcel_band_hemisphere_coupling_t2_kernel(
                 give_bank("o", i)
             store(i, lo, hi, res[:])
 
-        def empty3(i, hi=F, free=True):
+        def empty3(i, hi=F, free=True, lo=0):
             u, m = divmod(i, 4)
             if u not in raw:
                 raw[u] = work.tile([NP, 4 * F], F32, name="raw_%d" % u, tag="raw", bufs=3)
-            nc.scalar.copy(out=raw[u][:, F * m : F * m + hi], in_=o[i][:, :hi])
+            nc.scalar.copy(out=raw[u][:, F * m + lo : F * m + hi], in_=o[i][:, lo:hi])
             if free:
                 give_bank("o", i)
 
@@ -346,6 +349,107 @@ def tile_parcel_band_hemisphere_coupling_t2_kernel(
             for n in range((width + F - 1) // F):
                 cols = min(F, width - F * n)
                 store(i + n, 0, cols, scaled[i][:, F * n : F * n + cols])
+
+        def scale_block(i, count, lo, hi, after=None):
+            u, m = divmod(i, 4)
+            src = raw[u][:].rearrange("p (m f) -> p m f", f=F)[:, m : m + count, lo:hi]
+            dst = src
+            if after is not None:
+                late = work.tile([NP, count, hi - lo], F32, name="block_%d" % i, tag=after, bufs=1, align_bytes=64)
+                dst = late[:]
+            factor = gain_b[:, lo:hi].unsqueeze(1).to_broadcast([NP, count, hi - lo])
+            nc.gpsimd.tensor_tensor(out=dst, in0=src, in1=factor, op=ALU.mult)
+            scaled[i] = (dst, lo, hi)
+
+        def store_block(i):
+            u, m = divmod(i, 4)
+            res, lo, hi = scaled[i]
+            rows = outs[u % 2][NP * m : NP * (m + res.shape[1]), u // 2, lo:hi]
+            nc.sync.dma_start(out=rows.rearrange("(m p) f -> p m f", p=NP), in_=res)
+
+        gain_f32 = keep.tile([NP, 2 * NP], F32, name="gain_f32")
+        gain_col = keep.tile([NP, 2], F32, name="gain_col")
+        side, side_sb, back, turned = {}, {}, {}, {}
+
+        def gain_turn():
+            bank = psum.tile([NP, 2, NP], F32, name="gain_turned", tag=take_bank("g", 0), bufs=1)
+            for b in range(2):
+                nc.tensor.transpose(bank[:, b, :], gain_f32[:, NP * b : NP * b + NP], ident[:])
+            side["gain"] = bank
+
+        def gain_column():
+            nc.scalar.copy(out=gain_col[:], in_=side["gain"][:, :, 0])
+            give_bank("g", 0)
+
+        def mm3_side(u, b):
+            bank = psum.tile([NP, F], F32, name="side_%d_%d" % (u, b), tag=take_bank("s", (u, b)), bufs=1)
+            nc.tensor.matmul_mx(
+                out=bank[:],
+                lhsT=h2c[u][:, NP * b : NP * b + NP].bitcast(FP8X4),
+                lhsT_scale=h2s[u][:, NP * b : NP * b + NP],
+                rhs=c_w[:, u % 2, :].bitcast(FP4X4),
+                rhs_scale=c_s[:, u % 2, :],
+                start=True,
+                stop=True,
+            )
+            side[u, b] = bank
+
+        def scale_side(u, b):
+            sb = work.tile([NP, F], F32, name="side_sb_%d_%d" % (u, b), tag="side_sb", bufs=3)
+            nc.scalar.activation(out=sb[:], in_=side[u, b][:], func=ACT.Copy, scale=gain_col[:, b : b + 1])
+            give_bank("s", (u, b))
+            side_sb[u, b] = sb
+
+        def turn_side(u, b):
+            bank = psum.tile([NP, 4, NP], F32, name="back_%d_%d" % (u, b), tag=take_bank("b", (u, b)), bufs=1)
+            for m in range(4):
+                nc.tensor.transpose(bank[:, m, :], side_sb[u, b][:, NP * m : NP * m + NP], ident[:])
+            back[u, b] = bank
+
+        def empty_side(u, b, blocks):
+            if u not in turned:
+                turned[u] = work.tile([NP, 4, NP * blocks], F32, name="turned_%d" % u, bufs=1)
+            nc.scalar.copy(out=turned[u][:, :, NP * b : NP * b + NP], in_=back[u, b][:])
+            give_bank("b", (u, b))
+
+        def store_side(u):
+            cols = turned[u].shape[2]
+            nc.sync.dma_start(out=outs[u % 2][:, u // 2, :cols].rearrange("(m p) f -> p m f", p=NP), in_=turned[u][:])
+
+        def mm3_pair(u, j):
+            bank = psum.tile([NP, 2, F // 2], F32, name="op_%d_%d" % (u, j), tag=take_bank("p", j), bufs=1)
+            for n in range(2):
+                m = 2 * j + n
+                nc.tensor.matmul_mx(
+                    out=bank[:, n, :],
+                    lhsT=c_w[:, u % 2, 256 * m : 256 * m + 256].bitcast(FP4X4),
+                    lhsT_scale=c_s[:, u % 2, NP * m : NP * m + NP],
+                    rhs=h2c[u][:, F // 2 :].bitcast(FP8X4),
+                    rhs_scale=h2s[u][:, F // 2 :],
+                    start=True,
+                    stop=True,
+                )
+            side[u, "p", j] = bank
+
+        def finish_pair(u, j, count=2):
+            res = work.tile([NP, count, F // 2], F32, name="resp_%d_%d" % (u, j), tag="res", bufs=8)
+            nc.vector.tensor_tensor(
+                out=res[:],
+                in0=side[u, "p", j][:, :count, :],
+                in1=gain_b[:, F // 2 :].unsqueeze(1).to_broadcast([NP, count, F // 2]),
+                op=ALU.mult,
+            )
+            if count == 2:
+                give_bank("p", j)
+            rows = outs[u % 2][2 * NP * j : NP * (2 * j + count), u // 2, F // 2 :]
+            nc.sync.dma_start(out=rows.rearrange("(m p) f -> p m f", p=NP), in_=res[:])
+
+        def empty_second(u, j):
+            if u not in raw:
+                raw[u] = work.tile([NP, 4 * F], F32, name="raw_%d" % u, tag="raw", bufs=3)
+            m = 2 * j + 1
+            nc.scalar.copy(out=raw[u][:, F * m + F // 2 : F * m + F], in_=side[u, "p", j][:, 1, :])
+            give_bank("p", j)
 
         def round_gpsimd(i):
             u, t = divmod(i, 4)
@@ -446,6 +550,10 @@ def tile_parcel_band_hemisphere_coupling_t2_kernel(
                 late(k - 4, G_COLS, "h1g_0" if k == 4 else "xg_0")
                 for c in range(2):
                     gather1(2 * k - 2 + c)
+                if k == 4:
+                    nc.scalar.copy(out=gain_f32[:], in_=gain_b[:, : 2 * NP])
+                else:
+                    gain_column()
                 mm2(4 * u1)
                 mm2(4 * u1 + 1)
                 mm3(4 * u2)
@@ -512,6 +620,8 @@ def tile_parcel_band_hemisphere_coupling_t2_kernel(
                 turn(2 * k + 1)
                 for c in range(2):
                     gather1(2 * k - 2 + c)
+                if k == 5:
+                    gain_turn()
                 mm3(4 * u2 + 1)
                 mm3(4 * u2 + 2)
                 finish_vector(4 * u2 + 3, G_COLS, F, False)
@@ -524,71 +634,86 @@ def tile_parcel_band_hemisphere_coupling_t2_kernel(
         late(3, G_COLS, "x_3_0")
         for c in range(2):
             turn(12 + c)
+        mm3(16)
         add1(28)
         round1(28)
         gather1(12)
         add1(29)
         round1(29)
-        gather1(13)
+        empty3(16, P7_COLS, False, NP)
         for t in range(2):
             mm2(20 + t)
         add1(30)
         round1(30)
+        gather1(13)
         add1(31)
         round_gpsimd(31)
+        scale_block(16, 1, NP, P7_COLS)
         for t in range(2, 4):
             mm2(20 + t)
-        mm3(16)
         add2(20)
-        mm3(17)
-        add2(21)
         for c in range(2):
             turn(14 + c)
-        empty3(17)
+        add2(21)
+        mm3(17)
         add2(22)
         mm3(18)
         add2(23)
         mm3(19)
-        finish_vector(16)
+        finish_vector(16, P7_COLS, F)
+        mm3_side(4, 0)
+        store_block(16)
         for c in range(2):
             gather1(14 + c)
-        empty3(18)
+        empty3(17, F, True, NP)
+        empty3(18, F, True, NP)
+        scale_side(4, 0)
         pair_quantize(8)
         quant1(7)
-        scale_gpsimd(17, F, "h1g_7")
-        mm3(20)
+        scale_block(17, 2, NP, F, "h1g_7")
+        mm2(24)
+        mm2(25)
         finish_vector(19, T_COLS, F, False)
-        empty3(19, T_COLS)
-        scale_gpsimd(18, F + T_COLS)
-        for t in range(4):
-            mm2(24 + t)
-        finish_vector(20)
-        mm3(23)
+        empty3(19, T_COLS, True, NP)
+        scale_block(19, 1, NP, T_COLS)
+        for b in range(2):
+            mm3_side(5, b)
         add2(24)
-        store_scaled(17)
-        mm3(21)
+        mm2(26)
+        mm2(27)
+        for b in range(2):
+            scale_side(5, b)
         add2(25)
-        mm3(22)
-        empty3(21)
+        mm3_pair(5, 0)
+        turn_side(4, 0)
+        store_block(17)
         add2(26)
-        mm2(28)
-        empty3(22)
+        for b in range(2):
+            turn_side(5, b)
+        empty_side(4, 0, 1)
         add2(27)
+        mm2(28)
+        mm3_pair(5, 1)
         mm2(29)
-        finish_vector(23, T_COLS, F, False)
-        store_scaled(18)
-        empty3(23, T_COLS)
+        finish_pair(5, 0, 1)
+        store_block(19)
+        store_side(4)
+        empty_second(5, 0)
+        for b in range(2):
+            empty_side(5, b, 2)
         quant2(6)
-        scale_gpsimd(21, F, "h2g_6")
-        scale_gpsimd(22, F + T_COLS)
+        scale_block(21, 1, F // 2, F, "h2g_6")
+        mm3(24)
         mm2(30)
         mm2(31)
-        mm3(24)
         add2(28)
+        store_side(5)
+        empty3(24, T9_COLS, False)
+        scale_block(24, 1, 0, T9_COLS)
         mm3(25)
         add2(29)
-        finish_vector(24)
-        store_scaled(21)
+        finish_pair(5, 1)
+        store_block(21)
         hold = [free_banks.pop(0) for n in range(len(free_banks))]
         add2(30)
         mm3(26)
@@ -596,7 +721,9 @@ def tile_parcel_band_hemisphere_coupling_t2_kernel(
         mm3(27)
         free_banks.extend(hold)
         finish_vector(25)
-        store_scaled(22)
+        if T9_COLS < F:
+            finish_vector(24, T9_COLS, F)
+        store_block(24)
         quant2(7)
         finish_vector(26)
         finish_vector(27)

@@ -23,10 +23,8 @@ SPLIT1 = 240
 K0 = 3
 RUN = 2
 G_COLS = 352
-T_COLS = 256
-P7_COLS = 288
-T9_COLS = 512
-X2_S = 384
+P7_COLS = 192
+X2_S = 448
 X5_S = 224
 X7_G = 416
 P_HEAD = (224, 288)
@@ -318,7 +316,7 @@ def tile_parcel_band_hemisphere_coupling_t2_kernel(
             nc.sync.dma_start(out=outs[u % 2][NP * m : NP * m + NP, u // 2, lo:hi], in_=res)
 
         def finish_vector(i, lo=0, hi=F, free=True):
-            res = work.tile([NP, hi - lo], F32, name="res_%d_%d" % (i, lo), tag="res", bufs=8)
+            res = work.tile([NP, hi - lo], F32, name="res_%d_%d" % (i, lo), tag="res", bufs=7)
             nc.vector.tensor_tensor(out=res[:], in0=o[i][:, lo:hi], in1=gain_b[:, lo:hi], op=ALU.mult)
             if free:
                 give_bank("o", i)
@@ -350,26 +348,9 @@ def tile_parcel_band_hemisphere_coupling_t2_kernel(
                 cols = min(F, width - F * n)
                 store(i + n, 0, cols, scaled[i][:, F * n : F * n + cols])
 
-        def scale_block(i, count, lo, hi, after=None):
-            u, m = divmod(i, 4)
-            src = raw[u][:].rearrange("p (m f) -> p m f", f=F)[:, m : m + count, lo:hi]
-            dst = src
-            if after is not None:
-                late = work.tile([NP, count, hi - lo], F32, name="block_%d" % i, tag=after, bufs=1, align_bytes=64)
-                dst = late[:]
-            factor = gain_b[:, lo:hi].unsqueeze(1).to_broadcast([NP, count, hi - lo])
-            nc.gpsimd.tensor_tensor(out=dst, in0=src, in1=factor, op=ALU.mult)
-            scaled[i] = (dst, lo, hi)
-
-        def store_block(i):
-            u, m = divmod(i, 4)
-            res, lo, hi = scaled[i]
-            rows = outs[u % 2][NP * m : NP * (m + res.shape[1]), u // 2, lo:hi]
-            nc.sync.dma_start(out=rows.rearrange("(m p) f -> p m f", p=NP), in_=res)
-
         gain_f32 = keep.tile([NP, 2 * NP], F32, name="gain_f32")
         gain_col = keep.tile([NP, 2], F32, name="gain_col")
-        side, side_sb, back, turned = {}, {}, {}, {}
+        side, side_sb, back, stage = {}, {}, {}, {}
 
         def gain_turn():
             bank = psum.tile([NP, 2, NP], F32, name="gain_turned", tag=take_bank("g", 0), bufs=1)
@@ -400,21 +381,46 @@ def tile_parcel_band_hemisphere_coupling_t2_kernel(
             give_bank("s", (u, b))
             side_sb[u, b] = sb
 
-        def turn_side(u, b):
+        def turn_side(u, b, first=0):
             bank = psum.tile([NP, 4, NP], F32, name="back_%d_%d" % (u, b), tag=take_bank("b", (u, b)), bufs=1)
-            for m in range(4):
+            for m in range(first, 4):
                 nc.tensor.transpose(bank[:, m, :], side_sb[u, b][:, NP * m : NP * m + NP], ident[:])
             back[u, b] = bank
 
-        def empty_side(u, b, blocks):
-            if u not in turned:
-                turned[u] = work.tile([NP, 4, NP * blocks], F32, name="turned_%d" % u, bufs=1)
-            nc.scalar.copy(out=turned[u][:, :, NP * b : NP * b + NP], in_=back[u, b][:])
+        def empty_side(u, b, first=0):
+            nc.scalar.copy(out=stage[u][:, first:, NP * b : NP * b + NP], in_=back[u, b][:, first:, :])
             give_bank("b", (u, b))
 
-        def store_side(u):
-            cols = turned[u].shape[2]
-            nc.sync.dma_start(out=outs[u % 2][:, u // 2, :cols].rearrange("(m p) f -> p m f", p=NP), in_=turned[u][:])
+        def finish_in_place(i, lo):
+            u, m = divmod(i, 4)
+            nc.vector.tensor_tensor(
+                out=raw[u][:, F * m + lo : F * m + F], in0=o[i][:, lo:], in1=gain_b[:, lo:], op=ALU.mult
+            )
+            give_bank("o", i)
+
+        def open_stage(u, after):
+            stage[u] = work.tile([NP, 4, F], F32, name="stage_%d" % u, tag=after, bufs=1, align_bytes=64)
+
+        def store_stage(u, rows):
+            dst = outs[u % 2][:, u // 2, :].rearrange("(m p) f -> p m f", p=NP)
+            nc.sync.dma_start(out=dst[:, rows, :], in_=stage[u][:, rows, :])
+
+        def gain_rows(count, lo, hi):
+            return gain_b[:, lo:hi].unsqueeze(1).to_broadcast([NP, count, hi - lo])
+
+        def raw_rows(u):
+            if u not in raw:
+                raw[u] = work.tile([NP, 4 * F], F32, name="raw_%d" % u, tag="raw", bufs=3)
+            return raw[u][:].rearrange("p (m f) -> p m f", f=F)
+
+        def stage_gpsimd(u, rows, count, lo, hi):
+            nc.gpsimd.tensor_tensor(
+                out=stage[u][:, rows, lo:hi], in0=raw_rows(u)[:, rows, lo:hi], in1=gain_rows(count, lo, hi), op=ALU.mult
+            )
+
+        def stage_vector(i, lo, hi):
+            u, m = divmod(i, 4)
+            nc.vector.tensor_tensor(out=stage[u][:, m, lo:hi], in0=o[i][:, lo:hi], in1=gain_b[:, lo:hi], op=ALU.mult)
 
         def mm3_pair(u, j):
             bank = psum.tile([NP, 2, F // 2], F32, name="op_%d_%d" % (u, j), tag=take_bank("p", j), bufs=1)
@@ -431,24 +437,13 @@ def tile_parcel_band_hemisphere_coupling_t2_kernel(
                 )
             side[u, "p", j] = bank
 
-        def finish_pair(u, j, count=2):
-            res = work.tile([NP, count, F // 2], F32, name="resp_%d_%d" % (u, j), tag="res", bufs=8)
+        def finish_first(u):
             nc.vector.tensor_tensor(
-                out=res[:],
-                in0=side[u, "p", j][:, :count, :],
-                in1=gain_b[:, F // 2 :].unsqueeze(1).to_broadcast([NP, count, F // 2]),
-                op=ALU.mult,
+                out=stage[u][:, 0, F // 2 :], in0=side[u, "p", 0][:, 0, :], in1=gain_b[:, F // 2 :], op=ALU.mult
             )
-            if count == 2:
-                give_bank("p", j)
-            rows = outs[u % 2][2 * NP * j : NP * (2 * j + count), u // 2, F // 2 :]
-            nc.sync.dma_start(out=rows.rearrange("(m p) f -> p m f", p=NP), in_=res[:])
 
-        def empty_second(u, j):
-            if u not in raw:
-                raw[u] = work.tile([NP, 4 * F], F32, name="raw_%d" % u, tag="raw", bufs=3)
-            m = 2 * j + 1
-            nc.scalar.copy(out=raw[u][:, F * m + F // 2 : F * m + F], in_=side[u, "p", j][:, 1, :])
+        def empty_pair(u, j, first=0):
+            nc.scalar.copy(out=raw_rows(u)[:, 2 * j + first : 2 * j + 2, F // 2 :], in_=side[u, "p", j][:, first:, :])
             give_bank("p", j)
 
         def round_gpsimd(i):
@@ -475,9 +470,9 @@ def tile_parcel_band_hemisphere_coupling_t2_kernel(
         x_quantize(1)
         perm_aw(1, 0, 2)
         perm_as(1)
-        x_interleave(2, X2_S, F, "G", "a_raw_1_0")
-        x_interleave(2, 0, X2_S, "S")
+        x_interleave(2, 0, X2_S, "S", "xw_1")
         x_interleave(3, 0, F, "G")
+        x_interleave(2, X2_S, F, "G")
 
         mm1(1, (1,))
         mm1(0, (1,))
@@ -640,42 +635,47 @@ def tile_parcel_band_hemisphere_coupling_t2_kernel(
         gather1(12)
         add1(29)
         round1(29)
-        empty3(16, P7_COLS, False, NP)
+        empty3(16, P7_COLS, False)
         for t in range(2):
             mm2(20 + t)
+        mm3_side(4, 0)
         add1(30)
         round1(30)
-        gather1(13)
         add1(31)
         round_gpsimd(31)
-        scale_block(16, 1, NP, P7_COLS)
+        scale_gpsimd(16, P7_COLS)
         for t in range(2, 4):
             mm2(20 + t)
         add2(20)
-        for c in range(2):
-            turn(14 + c)
+        turn(14)
+        gather1(13)
+        scale_side(4, 0)
         add2(21)
+        turn(15)
         mm3(17)
         add2(22)
         mm3(18)
         add2(23)
         mm3(19)
-        finish_vector(16, P7_COLS, F)
-        mm3_side(4, 0)
-        store_block(16)
-        for c in range(2):
-            gather1(14 + c)
+        finish_in_place(16, P7_COLS)
+        store(16, 0, F, raw[4][:, :F])
+        gather1(14)
+        gather1(15)
+        turn_side(4, 0, 1)
         empty3(17, F, True, NP)
         empty3(18, F, True, NP)
-        scale_side(4, 0)
+        empty3(19, F // 2, False, NP)
         pair_quantize(8)
         quant1(7)
-        scale_block(17, 2, NP, F, "h1g_7")
+        open_stage(4, "h1g_7")
+        open_stage(5, "stage_5")
+        stage_gpsimd(4, slice(1, 4), 3, NP, F // 2)
+        stage_gpsimd(4, slice(1, 3), 2, F // 2, F)
         mm2(24)
         mm2(25)
-        finish_vector(19, T_COLS, F, False)
-        empty3(19, T_COLS, True, NP)
-        scale_block(19, 1, NP, T_COLS)
+        stage_vector(19, F // 2, F)
+        give_bank("o", 19)
+        empty_side(4, 0, 1)
         for b in range(2):
             mm3_side(5, b)
         add2(24)
@@ -684,36 +684,35 @@ def tile_parcel_band_hemisphere_coupling_t2_kernel(
         for b in range(2):
             scale_side(5, b)
         add2(25)
+        mm3_pair(5, 1)
         mm3_pair(5, 0)
-        turn_side(4, 0)
-        store_block(17)
+        store_stage(4, slice(3, 4))
         add2(26)
         for b in range(2):
             turn_side(5, b)
-        empty_side(4, 0, 1)
+        empty_pair(5, 1)
         add2(27)
         mm2(28)
-        mm3_pair(5, 1)
         mm2(29)
-        finish_pair(5, 0, 1)
-        store_block(19)
-        store_side(4)
-        empty_second(5, 0)
-        for b in range(2):
-            empty_side(5, b, 2)
+        empty_side(5, 0)
+        finish_first(5)
+        store_stage(4, slice(1, 3))
+        empty_pair(5, 0, 1)
+        empty_side(5, 1)
         quant2(6)
-        scale_block(21, 1, F // 2, F, "h2g_6")
+        store_stage(5, slice(0, 1))
         mm3(24)
         mm2(30)
         mm2(31)
-        add2(28)
-        store_side(5)
-        empty3(24, T9_COLS, False)
-        scale_block(24, 1, 0, T9_COLS)
         mm3(25)
+        for m in range(1, 4):
+            stage_gpsimd(5, slice(m, m + 1), 1, F // 2, F)
+        add2(28)
         add2(29)
-        finish_pair(5, 1)
-        store_block(21)
+        store_stage(5, slice(1, 2))
+        store_stage(5, slice(2, 3))
+        finish_vector(24)
+        store_stage(5, slice(3, 4))
         hold = [free_banks.pop(0) for n in range(len(free_banks))]
         add2(30)
         mm3(26)
@@ -721,9 +720,6 @@ def tile_parcel_band_hemisphere_coupling_t2_kernel(
         mm3(27)
         free_banks.extend(hold)
         finish_vector(25)
-        if T9_COLS < F:
-            finish_vector(24, T9_COLS, F)
-        store_block(24)
         quant2(7)
         finish_vector(26)
         finish_vector(27)

@@ -23,10 +23,10 @@ SPLIT1 = 240
 K0 = 3
 RUN = 2
 G_COLS = 352
-P7_COLS = 192
-X2_S = 448
+P7_COLS = 128
+X2_S = 352
 X5_S = 224
-X7_G = 416
+X7_G = 384
 P_HEAD = (224, 288)
 
 
@@ -316,7 +316,7 @@ def tile_parcel_band_hemisphere_coupling_t2_kernel(
             nc.sync.dma_start(out=outs[u % 2][NP * m : NP * m + NP, u // 2, lo:hi], in_=res)
 
         def finish_vector(i, lo=0, hi=F, free=True):
-            res = work.tile([NP, hi - lo], F32, name="res_%d_%d" % (i, lo), tag="res", bufs=7)
+            res = work.tile([NP, hi - lo], F32, name="res_%d_%d" % (i, lo), tag="res", bufs=8)
             nc.vector.tensor_tensor(out=res[:], in0=o[i][:, lo:hi], in1=gain_b[:, lo:hi], op=ALU.mult)
             if free:
                 give_bank("o", i)
@@ -376,19 +376,19 @@ def tile_parcel_band_hemisphere_coupling_t2_kernel(
             side[u, b] = bank
 
         def scale_side(u, b):
-            sb = work.tile([NP, F], F32, name="side_sb_%d_%d" % (u, b), tag="side_sb", bufs=3)
+            sb = work.tile([NP, F], F32, name="side_sb_%d_%d" % (u, b), tag="side_sb", bufs=2)
             nc.scalar.activation(out=sb[:], in_=side[u, b][:], func=ACT.Copy, scale=gain_col[:, b : b + 1])
             give_bank("s", (u, b))
             side_sb[u, b] = sb
 
-        def turn_side(u, b, first=0):
+        def turn_side(u, b):
             bank = psum.tile([NP, 4, NP], F32, name="back_%d_%d" % (u, b), tag=take_bank("b", (u, b)), bufs=1)
-            for m in range(first, 4):
+            for m in range(4):
                 nc.tensor.transpose(bank[:, m, :], side_sb[u, b][:, NP * m : NP * m + NP], ident[:])
             back[u, b] = bank
 
-        def empty_side(u, b, first=0):
-            nc.scalar.copy(out=stage[u][:, first:, NP * b : NP * b + NP], in_=back[u, b][:, first:, :])
+        def empty_side(u, b):
+            nc.scalar.copy(out=stage[u][:, :, NP * b : NP * b + NP], in_=back[u, b][:])
             give_bank("b", (u, b))
 
         def finish_in_place(i, lo):
@@ -417,10 +417,6 @@ def tile_parcel_band_hemisphere_coupling_t2_kernel(
             nc.gpsimd.tensor_tensor(
                 out=stage[u][:, rows, lo:hi], in0=raw_rows(u)[:, rows, lo:hi], in1=gain_rows(count, lo, hi), op=ALU.mult
             )
-
-        def stage_vector(i, lo, hi):
-            u, m = divmod(i, 4)
-            nc.vector.tensor_tensor(out=stage[u][:, m, lo:hi], in0=o[i][:, lo:hi], in1=gain_b[:, lo:hi], op=ALU.mult)
 
         def mm3_pair(u, j):
             bank = psum.tile([NP, 2, F // 2], F32, name="op_%d_%d" % (u, j), tag=take_bank("p", j), bufs=1)
@@ -470,9 +466,9 @@ def tile_parcel_band_hemisphere_coupling_t2_kernel(
         x_quantize(1)
         perm_aw(1, 0, 2)
         perm_as(1)
-        x_interleave(2, 0, X2_S, "S", "xw_1")
+        x_interleave(2, X2_S, F, "G", "a_raw_1_0")
+        x_interleave(2, 0, X2_S, "S")
         x_interleave(3, 0, F, "G")
-        x_interleave(2, X2_S, F, "G")
 
         mm1(1, (1,))
         mm1(0, (1,))
@@ -638,7 +634,6 @@ def tile_parcel_band_hemisphere_coupling_t2_kernel(
         empty3(16, P7_COLS, False)
         for t in range(2):
             mm2(20 + t)
-        mm3_side(4, 0)
         add1(30)
         round1(30)
         add1(31)
@@ -649,7 +644,6 @@ def tile_parcel_band_hemisphere_coupling_t2_kernel(
         add2(20)
         turn(14)
         gather1(13)
-        scale_side(4, 0)
         add2(21)
         turn(15)
         mm3(17)
@@ -661,21 +655,15 @@ def tile_parcel_band_hemisphere_coupling_t2_kernel(
         store(16, 0, F, raw[4][:, :F])
         gather1(14)
         gather1(15)
-        turn_side(4, 0, 1)
-        empty3(17, F, True, NP)
-        empty3(18, F, True, NP)
-        empty3(19, F // 2, False, NP)
+        empty3(17)
+        empty3(18)
         pair_quantize(8)
         quant1(7)
-        open_stage(4, "h1g_7")
+        scale_gpsimd(17, 2 * F, "h1g_7")
         open_stage(5, "stage_5")
-        stage_gpsimd(4, slice(1, 4), 3, NP, F // 2)
-        stage_gpsimd(4, slice(1, 3), 2, F // 2, F)
         mm2(24)
         mm2(25)
-        stage_vector(19, F // 2, F)
-        give_bank("o", 19)
-        empty_side(4, 0, 1)
+        finish_vector(19)
         for b in range(2):
             mm3_side(5, b)
         add2(24)
@@ -686,19 +674,18 @@ def tile_parcel_band_hemisphere_coupling_t2_kernel(
         add2(25)
         mm3_pair(5, 1)
         mm3_pair(5, 0)
-        store_stage(4, slice(3, 4))
+        mm2(28)
         add2(26)
+        mm2(29)
+        empty_pair(5, 1)
         for b in range(2):
             turn_side(5, b)
-        empty_pair(5, 1)
         add2(27)
-        mm2(28)
-        mm2(29)
-        empty_side(5, 0)
         finish_first(5)
-        store_stage(4, slice(1, 3))
+        store_scaled(17)
         empty_pair(5, 0, 1)
-        empty_side(5, 1)
+        for b in range(2):
+            empty_side(5, b)
         quant2(6)
         store_stage(5, slice(0, 1))
         mm3(24)

@@ -23,11 +23,10 @@ SPLIT1 = 240
 K0 = 3
 RUN = 2
 G_COLS = 352
-P7_COLS = 128
+P7_COLS = 192
 X2_S = 352
 X5_S = 224
-X7_G = 384
-P_HEAD = (224, 288)
+P_HEAD = (224, 192)
 
 
 def tile_parcel_band_hemisphere_coupling_t2_kernel(
@@ -144,13 +143,13 @@ def tile_parcel_band_hemisphere_coupling_t2_kernel(
             else:
                 nc.scalar.copy(out=dst, in_=src)
 
-        todo = [[5, 0, X5_S], [6, 0, F], [7, 0, F - X7_G]]
+        todo = [[5, 0, X5_S], [6, 0, F]]
 
         def s_interleave(width):
             while width > 0 and todo:
                 v, lo, hi = todo[0]
                 n = min(width, hi - lo)
-                x_interleave(v, lo, lo + n, "S", "xg_0" if v not in xg else None)
+                x_interleave(v, lo, lo + n, "S", "x_1_0" if v not in xg else None)
                 width = width - n
                 if lo + n == hi:
                     todo.pop(0)
@@ -442,17 +441,6 @@ def tile_parcel_band_hemisphere_coupling_t2_kernel(
             nc.scalar.copy(out=raw_rows(u)[:, 2 * j + first : 2 * j + 2, F // 2 :], in_=side[u, "p", j][:, first:, :])
             give_bank("p", j)
 
-        def round_gpsimd(i):
-            u, t = divmod(i, 4)
-            nc.gpsimd.tensor_scalar(
-                out=h1b[u][:, t, :].rearrange("p (a m e) -> p a m e", a=2, e=2),
-                in0=h1[u][:, t, :].rearrange("p (m a e) -> p a m e", a=2, e=2),
-                scalar1=1.0,
-                scalar2=0.0,
-                op0=ALU.mult,
-                op1=ALU.add,
-            )
-
         x_interleave(0, 0, SPLIT, "S", "xg_0")
         perm_aw(0, 0, 1)
         perm_as(0)
@@ -520,6 +508,7 @@ def tile_parcel_band_hemisphere_coupling_t2_kernel(
         mm1(13)
         add1(11)
         mm1(14)
+        round1(11)
         s_interleave(P_HEAD[1])
 
         def late(u, cols, after):
@@ -538,13 +527,11 @@ def tile_parcel_band_hemisphere_coupling_t2_kernel(
                 mm1(4 * k)
                 mm1(4 * k + 1)
                 pair_quantize(k)
-                late(k - 4, G_COLS, "h1g_0" if k == 4 else "xg_0")
+                late(k - 4, G_COLS, "h1g_0" if k == 4 else "x_1_0")
                 for c in range(2):
                     gather1(2 * k - 2 + c)
-                if k == 4:
+                if k == 6:
                     nc.scalar.copy(out=gain_f32[:], in_=gain_b[:, : 2 * NP])
-                else:
-                    gain_column()
                 mm2(4 * u1)
                 mm2(4 * u1 + 1)
                 mm3(4 * u2)
@@ -578,8 +565,7 @@ def tile_parcel_band_hemisphere_coupling_t2_kernel(
             else:
                 pair_quantize(k)
                 if k == 3:
-                    round_gpsimd(11)
-                    x_interleave(7, F - X7_G, F, "G")
+                    x_interleave(7, 0, F, "G")
                 else:
                     late(k - 4, G_COLS, "x_%d_0" % (k // 2))
                 mm3(4 * u2)
@@ -611,8 +597,6 @@ def tile_parcel_band_hemisphere_coupling_t2_kernel(
                 turn(2 * k + 1)
                 for c in range(2):
                     gather1(2 * k - 2 + c)
-                if k == 5:
-                    gain_turn()
                 mm3(4 * u2 + 1)
                 mm3(4 * u2 + 2)
                 finish_vector(4 * u2 + 3, G_COLS, F, False)
@@ -626,19 +610,17 @@ def tile_parcel_band_hemisphere_coupling_t2_kernel(
         for c in range(2):
             turn(12 + c)
         mm3(16)
-        add1(28)
-        round1(28)
+        for t in range(2):
+            add1(28 + t)
+            round1(28 + t)
         gather1(12)
-        add1(29)
-        round1(29)
         empty3(16, P7_COLS, False)
+        scale_gpsimd(16, P7_COLS)
         for t in range(2):
             mm2(20 + t)
-        add1(30)
-        round1(30)
-        add1(31)
-        round_gpsimd(31)
-        scale_gpsimd(16, P7_COLS)
+        for t in range(2, 4):
+            add1(28 + t)
+            round1(28 + t)
         for t in range(2, 4):
             mm2(20 + t)
         add2(20)
@@ -646,6 +628,7 @@ def tile_parcel_band_hemisphere_coupling_t2_kernel(
         gather1(13)
         add2(21)
         turn(15)
+        gain_turn()
         mm3(17)
         add2(22)
         mm3(18)
@@ -655,6 +638,7 @@ def tile_parcel_band_hemisphere_coupling_t2_kernel(
         store(16, 0, F, raw[4][:, :F])
         gather1(14)
         gather1(15)
+        gain_column()
         empty3(17)
         empty3(18)
         pair_quantize(8)

@@ -381,14 +381,21 @@ def tile_parcel_band_hemisphere_coupling_t2_kernel(
             side_sb[u, b] = sb
 
         def turn_side(u, b):
-            bank = psum.tile([NP, 4, NP], F32, name="back_%d_%d" % (u, b), tag=take_bank("b", (u, b)), bufs=1)
             for m in range(4):
-                nc.tensor.transpose(bank[:, m, :], side_sb[u, b][:, NP * m : NP * m + NP], ident[:])
-            back[u, b] = bank
+                j, n = divmod(m, 2)
+                if j not in back:
+                    back[j] = psum.tile([NP, 2, 2 * NP], F32, name="back_%d" % j, tag=take_bank("b", j), bufs=1)
+                dst = back[j][:, n, NP * b : NP * b + NP]
+                nc.tensor.transpose(dst, side_sb[u, b][:, NP * m : NP * m + NP], ident[:])
 
-        def empty_side(u, b):
-            nc.scalar.copy(out=stage[u][:, :, NP * b : NP * b + NP], in_=back[u, b][:])
-            give_bank("b", (u, b))
+        def empty_side(m):
+            j, n = divmod(m, 2)
+            nc.scalar.copy(out=stage[m][:, : F // 2], in_=back[j][:, n, :])
+            if n == 1:
+                give_bank("b", j)
+
+        for m in range(4):
+            stage[m] = work.tile([NP, F], F32, name="stage_%d" % m, bufs=1)
 
         def finish_in_place(i, lo):
             u, m = divmod(i, 4)
@@ -397,25 +404,14 @@ def tile_parcel_band_hemisphere_coupling_t2_kernel(
             )
             give_bank("o", i)
 
-        def open_stage(u, after):
-            stage[u] = work.tile([NP, 4, F], F32, name="stage_%d" % u, tag=after, bufs=1, align_bytes=64)
-
-        def store_stage(u, rows):
-            dst = outs[u % 2][:, u // 2, :].rearrange("(m p) f -> p m f", p=NP)
-            nc.sync.dma_start(out=dst[:, rows, :], in_=stage[u][:, rows, :])
-
-        def gain_rows(count, lo, hi):
-            return gain_b[:, lo:hi].unsqueeze(1).to_broadcast([NP, count, hi - lo])
-
         def raw_rows(u):
             if u not in raw:
                 raw[u] = work.tile([NP, 4 * F], F32, name="raw_%d" % u, tag="raw", bufs=3)
             return raw[u][:].rearrange("p (m f) -> p m f", f=F)
 
-        def stage_gpsimd(u, rows, count, lo, hi):
-            nc.gpsimd.tensor_tensor(
-                out=stage[u][:, rows, lo:hi], in0=raw_rows(u)[:, rows, lo:hi], in1=gain_rows(count, lo, hi), op=ALU.mult
-            )
+        def stage_gpsimd(u, m):
+            src = raw[u][:, F * m + F // 2 : F * m + F]
+            nc.gpsimd.tensor_tensor(out=stage[m][:, F // 2 :], in0=src, in1=gain_b[:, F // 2 :], op=ALU.mult)
 
         def mm3_pair(u, j):
             bank = psum.tile([NP, 2, F // 2], F32, name="op_%d_%d" % (u, j), tag=take_bank("p", j), bufs=1)
@@ -434,7 +430,7 @@ def tile_parcel_band_hemisphere_coupling_t2_kernel(
 
         def finish_first(u):
             nc.vector.tensor_tensor(
-                out=stage[u][:, 0, F // 2 :], in0=side[u, "p", 0][:, 0, :], in1=gain_b[:, F // 2 :], op=ALU.mult
+                out=stage[0][:, F // 2 :], in0=side[u, "p", 0][:, 0, :], in1=gain_b[:, F // 2 :], op=ALU.mult
             )
 
         def empty_pair(u, j, first=0):
@@ -643,8 +639,8 @@ def tile_parcel_band_hemisphere_coupling_t2_kernel(
         empty3(18)
         pair_quantize(8)
         quant1(7)
-        scale_gpsimd(17, 2 * F, "h1g_7")
-        open_stage(5, "stage_5")
+        scale_gpsimd(17, F, "h1g_7")
+        scale_gpsimd(18, F)
         mm2(24)
         mm2(25)
         finish_vector(19)
@@ -656,6 +652,7 @@ def tile_parcel_band_hemisphere_coupling_t2_kernel(
         for b in range(2):
             scale_side(5, b)
         add2(25)
+        store_scaled(17)
         mm3_pair(5, 1)
         mm3_pair(5, 0)
         mm2(28)
@@ -666,24 +663,24 @@ def tile_parcel_band_hemisphere_coupling_t2_kernel(
             turn_side(5, b)
         add2(27)
         finish_first(5)
-        store_scaled(17)
+        store_scaled(18)
         empty_pair(5, 0, 1)
-        for b in range(2):
-            empty_side(5, b)
+        for m in range(4):
+            empty_side(m)
         quant2(6)
-        store_stage(5, slice(0, 1))
+        store(20, 0, F, stage[0][:])
         mm3(24)
         mm2(30)
         mm2(31)
         mm3(25)
         for m in range(1, 4):
-            stage_gpsimd(5, slice(m, m + 1), 1, F // 2, F)
+            stage_gpsimd(5, m)
         add2(28)
         add2(29)
-        store_stage(5, slice(1, 2))
-        store_stage(5, slice(2, 3))
+        store(21, 0, F, stage[1][:])
+        store(22, 0, F, stage[2][:])
         finish_vector(24)
-        store_stage(5, slice(3, 4))
+        store(23, 0, F, stage[3][:])
         hold = [free_banks.pop(0) for n in range(len(free_banks))]
         add2(30)
         mm3(26)

@@ -18,15 +18,16 @@ ALU = mybir.AluOpType
 ACT = mybir.ActivationFunctionType
 
 NP = 128
-SPLIT = 160
-SPLIT1 = 240
+SPLIT = 176
+SPLIT1 = 176
 K0 = 3
 RUN = 2
 G_COLS = 352
 P7_COLS = 192
-X2_S = 352
-X5_S = 224
-P_HEAD = (224, 192)
+X2_S = 224
+X3_S = 128
+X5_S = 192
+P_HEAD = (192, 192)
 
 
 def tile_parcel_band_hemisphere_coupling_t2_kernel(
@@ -84,9 +85,9 @@ def tile_parcel_band_hemisphere_coupling_t2_kernel(
             for r in range(4):
                 nc.sync.dma_start(out=dst[r:NP:32].bitcast(I32), in_=src[:, r:16:4, :].rearrange("g q n -> q g n"))
 
+        load_x(0, 0)
         load_a(0, 0, 1)
         load_scales(a_sraw[0], sc_scales.bitcast(I32)[:, :, :NP])
-        load_x(0, 0)
         load_x(0, 1)
         load_a(0, 1, 2)
         load_a(1, 0, 2)
@@ -104,15 +105,15 @@ def tile_parcel_band_hemisphere_coupling_t2_kernel(
         nc.sync.dma_start(out=gain_b, in_=gain.partition_broadcast(NP))
 
         def perm_aw(h, lo, hi):
-            nc.vector.tensor_copy(
+            nc.scalar.copy(
                 out=a_w[h][:, lo:hi, :].bitcast(U16).rearrange("p g (t m) -> p g t m", t=4),
                 in_=a_raw[h, lo][:].bitcast(U16).rearrange("p g (m t) -> p g t m", t=4),
             )
 
-        def perm_as(h):
+        def perm_as(h, lo, hi):
             nc.vector.tensor_copy(
-                out=a_s[h][:].rearrange("p g (t m) -> p g t m", t=4),
-                in_=a_sraw[h][:].rearrange("p g (m t) -> p g t m", t=4),
+                out=a_s[h][:, lo:hi, :].rearrange("p g (t m) -> p g t m", t=4),
+                in_=a_sraw[h][:, lo:hi, :].rearrange("p g (m t) -> p g t m", t=4),
             )
 
         xg, xc, xsc, window, pair = {}, {}, {}, {}, {}
@@ -438,73 +439,72 @@ def tile_parcel_band_hemisphere_coupling_t2_kernel(
             give_bank("p", j)
 
         x_interleave(0, 0, SPLIT, "S", "xg_0")
-        perm_aw(0, 0, 1)
-        perm_as(0)
         x_interleave(0, SPLIT, F, "V")
+        perm_aw(0, 0, 1)
+        perm_as(0, 0, 1)
         x_quantize(0)
         for t in range(K0):
             mm1(t, (0,))
         x_interleave(1, 0, SPLIT1, "S", "xg_1")
         x_interleave(1, SPLIT1, F, "V")
         perm_aw(0, 1, 2)
+        perm_as(0, 1, 2)
         x_quantize(1)
         perm_aw(1, 0, 2)
-        perm_as(1)
-        x_interleave(2, X2_S, F, "G", "a_raw_1_0")
+        perm_as(1, 0, 2)
+        x_interleave(2, X2_S, F, "G", "xg_1")
         x_interleave(2, 0, X2_S, "S")
-        x_interleave(3, 0, F, "G")
+        x_interleave(3, X3_S, F, "G")
 
-        mm1(1, (1,))
-        mm1(0, (1,))
+        for t in range(K0):
+            mm1(t, (1,))
         mm1(3)
-        mm1(2, (1,))
-        mm1(5)
         mm1(4)
+        mm1(5)
         for t in range(2):
             add1(t)
             round1(t)
         mm1(6)
+        turn(0)
         for t in range(2, 4):
             add1(t)
             round1(t)
-        for c in range(2):
-            turn(c)
-            gather1(c)
+        turn(1)
         mm1(7)
+        x_interleave(3, 0, X3_S, "S")
+        for c in range(2):
+            gather1(c)
         for t in range(4, 7):
             add1(t)
+
         window_quantize(1)
         mm1(8)
         quant1(0)
-        x_interleave(4, 0, F, "G", "h1g_0")
+        x_interleave(4, 0, F, "G", "xg_1")
         x_interleave(5, X5_S, F, "G")
         add1(7)
         for t in range(4, 8):
             round1(t)
-        for t in (0, 2, 1, 3):
-            mm2(t)
-        mm1(9)
+        for b in range(4):
+            mm2(b)
         add1(8)
+        round1(8)
         s_interleave(P_HEAD[0])
+        mm1(9)
+        mm1(10)
         add2(0)
         add2(1)
-        for c in (2, 3):
-            turn(c)
-            gather1(c)
-        mm1(10)
+        turn(2)
+        turn(3)
         add2(2)
-        mm1(11)
         add2(3)
-        round1(8)
-        add1(9)
-        round1(9)
-        mm1(12)
-        add1(10)
-        round1(10)
-        mm1(13)
-        add1(11)
-        mm1(14)
-        round1(11)
+        mm1(11)
+        gather1(2)
+        gather1(3)
+        for t in range(1, 4):
+            mm1(11 + t)
+            add1(8 + t)
+            round1(8 + t)
         s_interleave(P_HEAD[1])
 
         def late(u, cols, after):
@@ -523,7 +523,7 @@ def tile_parcel_band_hemisphere_coupling_t2_kernel(
                 mm1(4 * k)
                 mm1(4 * k + 1)
                 pair_quantize(k)
-                late(k - 4, G_COLS, "h1g_0" if k == 4 else "x_1_0")
+                late(k - 4, G_COLS, "xg_1" if k == 4 else "x_1_0")
                 for c in range(2):
                     gather1(2 * k - 2 + c)
                 if k == 6:

@@ -22,12 +22,14 @@ SPLIT = 176
 SPLIT1 = 176
 K0 = 3
 RUN = 2
-G_COLS = 352
+G_COLS = 336
 P7_COLS = 192
 X2_S = 224
 X3_S = 128
 X5_S = 192
 P_HEAD = (192, 192)
+X7_S = 176
+S_X = {3: 384, 4: 112, 5: 0, 6: 0, 7: 0}
 
 
 def tile_parcel_band_hemisphere_coupling_t2_kernel(
@@ -66,8 +68,6 @@ def tile_parcel_band_hemisphere_coupling_t2_kernel(
 
         nc.gpsimd.memset(a_sraw[0][:].bitcast(I32), 0)
         nc.vector.memset(a_sraw[1][:].bitcast(I32), 0)
-        nc.vector.memset(b_s[:].bitcast(I32), 0)
-        nc.vector.memset(c_s[:].bitcast(I32), 0)
         make_identity(nc, ident[:])
 
         def load_x(w, k):
@@ -144,7 +144,7 @@ def tile_parcel_band_hemisphere_coupling_t2_kernel(
             else:
                 nc.scalar.copy(out=dst, in_=src)
 
-        todo = [[5, 0, X5_S], [6, 0, F]]
+        todo = [[5, 0, X5_S], [6, 0, F], [7, 0, X7_S]]
 
         def s_interleave(width):
             while width > 0 and todo:
@@ -187,18 +187,18 @@ def tile_parcel_band_hemisphere_coupling_t2_kernel(
         free_banks = ["bank_%d" % b for b in range(8)]
         bank_of = {}
 
-        def take_bank(kind, i):
-            bank_of[kind, i] = free_banks.pop(0)
+        def take_bank(kind, i, newest=False):
+            bank_of[kind, i] = free_banks.pop(-1 if newest else 0)
             return bank_of[kind, i]
 
         def give_bank(kind, i):
             free_banks.append(bank_of[kind, i])
 
-        def mm1(i, passes=(0, 1)):
+        def mm1(i, passes=(0, 1), newest=False):
             u, t = divmod(i, 4)
             w, h = divmod(u, 2)
             if i not in d:
-                d[i] = psum.tile([NP, F], F32, name="d_%d" % i, tag=take_bank("d", i), bufs=1)
+                d[i] = psum.tile([NP, F], F32, name="d_%d" % i, tag=take_bank("d", i, newest), bufs=1)
             acc = d[i]
             for k in passes:
                 nc.tensor.matmul_mx(
@@ -348,13 +348,13 @@ def tile_parcel_band_hemisphere_coupling_t2_kernel(
                 cols = min(F, width - F * n)
                 store(i + n, 0, cols, scaled[i][:, F * n : F * n + cols])
 
-        gain_f32 = keep.tile([NP, 2 * NP], F32, name="gain_f32")
-        gain_col = keep.tile([NP, 2], F32, name="gain_col")
-        side, side_sb, back, stage = {}, {}, {}, {}
+        gain_f32 = keep.tile([NP, F], F32, name="gain_f32")
+        gain_col = keep.tile([NP, 4], F32, name="gain_col")
+        side, side_sb, back = {}, {}, {}
 
         def gain_turn():
-            bank = psum.tile([NP, 2, NP], F32, name="gain_turned", tag=take_bank("g", 0), bufs=1)
-            for b in range(2):
+            bank = psum.tile([NP, 4, NP], F32, name="gain_turned", tag=take_bank("g", 0), bufs=1)
+            for b in range(4):
                 nc.tensor.transpose(bank[:, b, :], gain_f32[:, NP * b : NP * b + NP], ident[:])
             side["gain"] = bank
 
@@ -362,41 +362,38 @@ def tile_parcel_band_hemisphere_coupling_t2_kernel(
             nc.scalar.copy(out=gain_col[:], in_=side["gain"][:, :, 0])
             give_bank("g", 0)
 
-        def mm3_side(u, b):
-            bank = psum.tile([NP, F], F32, name="side_%d_%d" % (u, b), tag=take_bank("s", (u, b)), bufs=1)
-            nc.tensor.matmul_mx(
-                out=bank[:],
-                lhsT=h2c[u][:, NP * b : NP * b + NP].bitcast(FP8X4),
-                lhsT_scale=h2s[u][:, NP * b : NP * b + NP],
-                rhs=c_w[:, u % 2, :].bitcast(FP4X4),
-                rhs_scale=c_s[:, u % 2, :],
-                start=True,
-                stop=True,
-            )
-            side[u, b] = bank
+        def mm3_side(i):
+            u, m = divmod(i, 4)
+            bank = psum.tile([NP, 4, NP], F32, name="side_%d" % i, tag=take_bank("s", i), bufs=1)
+            for b in range(4):
+                nc.tensor.matmul_mx(
+                    out=bank[:, b, :],
+                    lhsT=h2c[u][:, NP * b : NP * b + NP].bitcast(FP8X4),
+                    lhsT_scale=h2s[u][:, NP * b : NP * b + NP],
+                    rhs=c_w[:, u % 2, 256 * m : 256 * m + 256].bitcast(FP4X4),
+                    rhs_scale=c_s[:, u % 2, NP * m : NP * m + NP],
+                    start=True,
+                    stop=True,
+                )
+            side[i] = bank
 
-        def scale_side(u, b):
-            sb = work.tile([NP, F], F32, name="side_sb_%d_%d" % (u, b), tag="side_sb", bufs=2)
-            nc.scalar.activation(out=sb[:], in_=side[u, b][:], func=ACT.Copy, scale=gain_col[:, b : b + 1])
-            give_bank("s", (u, b))
-            side_sb[u, b] = sb
+        def scale_side(i):
+            sb = work.tile([NP, 4, NP], F32, name="side_sb_%d" % i, tag="side_sb", bufs=2)
+            for b in range(4):
+                nc.scalar.activation(out=sb[:, b, :], in_=side[i][:, b, :], func=ACT.Copy, scale=gain_col[:, b : b + 1])
+            give_bank("s", i)
+            side_sb[i] = sb
 
-        def turn_side(u, b):
-            for m in range(4):
-                j, n = divmod(m, 2)
-                if j not in back:
-                    back[j] = psum.tile([NP, 2, 2 * NP], F32, name="back_%d" % j, tag=take_bank("b", j), bufs=1)
-                dst = back[j][:, n, NP * b : NP * b + NP]
-                nc.tensor.transpose(dst, side_sb[u, b][:, NP * m : NP * m + NP], ident[:])
+        def turn_side(i):
+            back[i] = psum.tile([NP, 4, NP], F32, name="back_%d" % i, tag=take_bank("b", i), bufs=1)
+            for b in range(4):
+                nc.tensor.transpose(back[i][:, b, :], side_sb[i][:, b, :], ident[:])
 
-        def empty_side(m):
-            j, n = divmod(m, 2)
-            nc.scalar.copy(out=stage[m][:, : F // 2], in_=back[j][:, n, :])
-            if n == 1:
-                give_bank("b", j)
-
-        for m in range(4):
-            stage[m] = work.tile([NP, F], F32, name="stage_%d" % m, bufs=1)
+        def empty_side(i):
+            res = work.tile([NP, F], F32, name="sres_%d" % i, tag="res", bufs=8)
+            nc.scalar.copy(out=res[:], in_=back[i][:].rearrange("p b q -> p (b q)"))
+            give_bank("b", i)
+            store(i, 0, F, res[:])
 
         def finish_in_place(i, lo):
             u, m = divmod(i, 4)
@@ -405,38 +402,16 @@ def tile_parcel_band_hemisphere_coupling_t2_kernel(
             )
             give_bank("o", i)
 
-        def raw_rows(u):
-            if u not in raw:
-                raw[u] = work.tile([NP, 4 * F], F32, name="raw_%d" % u, tag="raw", bufs=3)
-            return raw[u][:].rearrange("p (m f) -> p m f", f=F)
+        halves = {}
 
-        def stage_gpsimd(u, m):
-            src = raw[u][:, F * m + F // 2 : F * m + F]
-            nc.gpsimd.tensor_tensor(out=stage[m][:, F // 2 :], in0=src, in1=gain_b[:, F // 2 :], op=ALU.mult)
-
-        def mm3_pair(u, j):
-            bank = psum.tile([NP, 2, F // 2], F32, name="op_%d_%d" % (u, j), tag=take_bank("p", j), bufs=1)
-            for n in range(2):
-                m = 2 * j + n
-                nc.tensor.matmul_mx(
-                    out=bank[:, n, :],
-                    lhsT=c_w[:, u % 2, 256 * m : 256 * m + 256].bitcast(FP4X4),
-                    lhsT_scale=c_s[:, u % 2, NP * m : NP * m + NP],
-                    rhs=h2c[u][:, F // 2 :].bitcast(FP8X4),
-                    rhs_scale=h2s[u][:, F // 2 :],
-                    start=True,
-                    stop=True,
-                )
-            side[u, "p", j] = bank
-
-        def finish_first(u):
-            nc.vector.tensor_tensor(
-                out=stage[0][:, F // 2 :], in0=side[u, "p", 0][:, 0, :], in1=gain_b[:, F // 2 :], op=ALU.mult
-            )
-
-        def empty_pair(u, j, first=0):
-            nc.scalar.copy(out=raw_rows(u)[:, 2 * j + first : 2 * j + 2, F // 2 :], in_=side[u, "p", j][:, first:, :])
-            give_bank("p", j)
+        def finish_half(i, second):
+            if not second:
+                halves[i] = work.tile([NP, F], F32, name="hres_%d" % i, tag="res", bufs=8)
+            cols = slice(F // 2, F) if second else slice(0, F // 2)
+            nc.vector.tensor_tensor(out=halves[i][:, cols], in0=o[i][:, cols], in1=gain_b[:, cols], op=ALU.mult)
+            if second:
+                give_bank("o", i)
+                store(i, 0, F, halves[i][:])
 
         x_interleave(0, 0, SPLIT, "S", "xg_0")
         x_interleave(0, SPLIT, F, "V")
@@ -511,185 +486,144 @@ def tile_parcel_band_hemisphere_coupling_t2_kernel(
             scale_gpsimd(4 * u + 1, 2 * F + cols, after)
             store_scaled(4 * u + 1)
 
-        def now(u):
-            empty3(4 * u)
-            scale_gpsimd(4 * u, F)
-            store_scaled(4 * u)
+        def now(i):
+            empty3(i)
+            scale_gpsimd(i, F)
+            store_scaled(i)
+
+        def sum1(i):
+            add1(i)
+            round1(i)
+
+        def share(u):
+            finish_vector(4 * u + 3, G_COLS, F, False)
+
+        pair_quantize(3)
+        x_interleave(7, X7_S, F, "G")
+        for b in range(2):
+            mm2(4 + b)
+        mm3(0)
+        sum1(12)
+        add1(13)
+        mm2(6)
+        mm2(7)
+        now(0)
+        round1(13)
+        add2(4)
+        nc.scalar.copy(out=gain3[:, F : 2 * F], in_=gain_b)
+        nc.scalar.copy(out=gain3[:, 2 * F :], in_=gain_b[:, :G_COLS])
+        turn(4)
+        turn(5)
+        add2(5)
+        add2(6)
+        gather1(4)
+        mm3(3)
+        mm3(1)
+        add2(7)
+        gather1(5)
+        mm3(2)
+        share(0)
+        mm1(15)
+        empty3(1)
+        empty3(2)
+        empty3(3, G_COLS)
 
         for k in range(3, 7):
-            u1, u2 = k - 2, k - 3
-            if k % 2 == 0:
-                window_quantize(k // 2)
-                mm1(4 * k)
-                mm1(4 * k + 1)
-                pair_quantize(k)
-                late(k - 4, G_COLS, "xg_1" if k == 4 else "x_1_0")
-                for c in range(2):
-                    gather1(2 * k - 2 + c)
-                if k == 6:
-                    nc.scalar.copy(out=gain_f32[:], in_=gain_b[:, : 2 * NP])
-                mm2(4 * u1)
-                mm2(4 * u1 + 1)
-                mm3(4 * u2)
-                for t in range(2):
-                    add1(4 * k + t)
-                    round1(4 * k + t)
-                mm2(4 * u1 + 2)
-                mm2(4 * u1 + 3)
-                now(u2)
-                s_interleave(F)
-                add2(4 * u1)
-                mm3(4 * u2 + 3)
-                add2(4 * u1 + 1)
-                mm3(4 * u2 + 1)
-                mm1(4 * k + 2)
-                add2(4 * u1 + 2)
-                finish_vector(4 * u2 + 3, G_COLS, F, False)
-                mm1(4 * k + 3)
-                empty3(4 * u2 + 3, G_COLS)
-                add2(4 * u1 + 3)
-                mm3(4 * u2 + 2)
-                empty3(4 * u2 + 1)
-                add1(4 * k + 2)
+            u1, u2 = k - 1, k - 2
+            if k in (3, 5):
+                window_quantize(k // 2 + 1)
+            pair_quantize(k + 1)
+            late(k - 3, G_COLS, ("xg_1" if k == 3 else "x_1_0") if k in (3, 5) else None)
+            if k < 7:
                 mm1(4 * k + 4)
-                empty3(4 * u2 + 2)
-                round1(4 * k + 2)
-                add1(4 * k + 3)
                 mm1(4 * k + 5)
-                mm1(4 * k + 6)
-                round1(4 * k + 3)
-            else:
-                pair_quantize(k)
-                if k == 3:
-                    x_interleave(7, 0, F, "G")
-                else:
-                    late(k - 4, G_COLS, "x_%d_0" % (k // 2))
-                mm3(4 * u2)
-                mm2(4 * u1)
-                mm1(4 * k + 3)
-                add1(4 * k)
-                round1(4 * k)
-                now(u2)
-                if k == 3:
-                    nc.scalar.copy(out=gain3[:, F : 2 * F], in_=gain_b)
-                    nc.scalar.copy(out=gain3[:, 2 * F :], in_=gain_b[:, :G_COLS])
-                add1(4 * k + 1)
-                round1(4 * k + 1)
-                mm2(4 * u1 + 1)
-                add1(4 * k + 2)
-                round1(4 * k + 2)
-                mm2(4 * u1 + 2)
-                mm2(4 * u1 + 3)
-                add2(4 * u1)
-                add1(4 * k + 3)
-                round1(4 * k + 3)
-                mm3(4 * u2 + 3)
-                add2(4 * u1 + 1)
-                for c in range(2):
-                    turn(2 * k - 2 + c)
-                add2(4 * u1 + 2)
-                turn(2 * k)
-                add2(4 * u1 + 3)
-                turn(2 * k + 1)
-                for c in range(2):
-                    gather1(2 * k - 2 + c)
-                mm3(4 * u2 + 1)
-                mm3(4 * u2 + 2)
-                finish_vector(4 * u2 + 3, G_COLS, F, False)
-                empty3(4 * u2 + 3, G_COLS)
-                empty3(4 * u2 + 1)
-                empty3(4 * u2 + 2)
+            s_interleave(S_X[k])
+            if k == 5:
+                nc.scalar.copy(out=gain_f32[:], in_=gain_b)
+            for b in range(4):
+                mm2(4 * u1 + b)
+            sum1(4 * k + 2)
+            sum1(4 * k + 3)
+            mm3(4 * u2)
+            add2(4 * u1)
+            turn(2 * k)
+            turn(2 * k + 1)
+            add2(4 * u1 + 1)
+            add2(4 * u1 + 2)
+            now(4 * u2)
+            mm3(4 * u2 + 1)
+            mm3(4 * u2 + 3)
+            add2(4 * u1 + 3)
+            gather1(2 * k)
+            gather1(2 * k + 1)
+            mm3(4 * u2 + 2)
+            empty3(4 * u2 + 1)
+            mm1(4 * k + 6)
+            add1(4 * k + 4)
+            empty3(4 * u2 + 2)
+            if k < 6:
+                mm1(4 * k + 7)
+            add1(4 * k + 5)
+            if k == 6:
+                mm1(4 * k + 7, newest=True)
+            share(u2)
+            empty3(4 * u2 + 3, G_COLS)
+            round1(4 * k + 4)
+            round1(4 * k + 5)
 
-        mm1(31)
-        pair_quantize(7)
-        late(3, G_COLS, "x_3_0")
-        for c in range(2):
-            turn(12 + c)
-        mm3(16)
-        for t in range(2):
-            add1(28 + t)
-            round1(28 + t)
-        gather1(12)
-        empty3(16, P7_COLS, False)
-        scale_gpsimd(16, P7_COLS)
-        for t in range(2):
-            mm2(20 + t)
-        for t in range(2, 4):
-            add1(28 + t)
-            round1(28 + t)
-        for t in range(2, 4):
-            mm2(20 + t)
-        add2(20)
-        turn(14)
-        gather1(13)
-        add2(21)
-        turn(15)
-        gain_turn()
-        mm3(17)
-        add2(22)
-        mm3(18)
-        add2(23)
-        mm3(19)
-        finish_in_place(16, P7_COLS)
-        store(16, 0, F, raw[4][:, :F])
-        gather1(14)
-        gather1(15)
-        gain_column()
-        empty3(17)
-        empty3(18)
         pair_quantize(8)
-        quant1(7)
-        scale_gpsimd(17, F, "h1g_7")
-        scale_gpsimd(18, F)
-        mm2(24)
-        mm2(25)
-        finish_vector(19)
-        for b in range(2):
-            mm3_side(5, b)
-        add2(24)
-        mm2(26)
+        late(4, G_COLS, None)
+        gain_turn()
+        for b in range(3):
+            mm2(24 + b)
+        gain_column()
         mm2(27)
-        for b in range(2):
-            scale_side(5, b)
+        sum1(30)
+        sum1(31)
+        mm3(20)
+        add2(24)
+        turn(14)
+        turn(15)
         add2(25)
-        store_scaled(17)
-        mm3_pair(5, 1)
-        mm3_pair(5, 0)
-        mm2(28)
+        mm3(23)
         add2(26)
-        mm2(29)
-        empty_pair(5, 1)
-        for b in range(2):
-            turn_side(5, b)
+        gather1(14)
+        mm3_side(21)
         add2(27)
-        finish_first(5)
-        store_scaled(18)
-        empty_pair(5, 0, 1)
-        for m in range(4):
-            empty_side(m)
+        gather1(15)
+        mm3(22)
+        finish_half(20, False)
+        scale_side(21)
+        empty3(23)
         quant2(6)
-        store(20, 0, F, stage[0][:])
+        turn_side(21)
+        quant1(7)
+        scale_gpsimd(23, F, "h2g_6")
         mm3(24)
+        empty_side(21)
+        finish_half(20, True)
+        mm2(28)
+        mm2(29)
+        finish_vector(22)
+        empty3(24)
+        mm3_side(25)
         mm2(30)
         mm2(31)
-        mm3(25)
-        for m in range(1, 4):
-            stage_gpsimd(5, m)
+        store_scaled(23)
+        scale_side(25)
         add2(28)
+        scale_gpsimd(24, F)
+        turn_side(25)
         add2(29)
-        store(21, 0, F, stage[1][:])
-        store(22, 0, F, stage[2][:])
-        finish_vector(24)
-        store(23, 0, F, stage[3][:])
-        hold = [free_banks.pop(0) for n in range(len(free_banks))]
-        add2(30)
         mm3(26)
-        add2(31)
+        add2(30)
+        store_scaled(24)
+        empty_side(25)
         mm3(27)
-        free_banks.extend(hold)
-        finish_vector(25)
+        add2(31)
+        finish_half(26, False)
         quant2(7)
-        finish_vector(26)
+        finish_half(26, True)
         finish_vector(27)
         for t in range(4):
             mm3(28 + t)

@@ -23,6 +23,7 @@ SPLIT1 = 176
 K0 = 3
 RUN = 2
 G_COLS = 336
+G_LAST = 256
 P7_COLS = 192
 X2_S = 224
 X3_S = 128
@@ -296,10 +297,10 @@ def tile_parcel_band_hemisphere_coupling_t2_kernel(
         def quant2(u):
             h2c[u], h2s[u] = quantize(h2g[u].rearrange("p f t -> p (f t)"), "h2_%d" % u, "one", 4)
 
-        def mm3(i):
+        def mm3(i, newest=False):
             u, m = divmod(i, 4)
             g = u % 2
-            bank = psum.tile([NP, F], F32, name="o_%d" % i, tag=take_bank("o", i), bufs=1)
+            bank = psum.tile([NP, F], F32, name="o_%d" % i, tag=take_bank("o", i, newest), bufs=1)
             nc.tensor.matmul_mx(
                 out=bank[:],
                 lhsT=c_w[:, g, 256 * m : 256 * m + 256].bitcast(FP4X4),
@@ -495,8 +496,8 @@ def tile_parcel_band_hemisphere_coupling_t2_kernel(
             add1(i)
             round1(i)
 
-        def share(u):
-            finish_vector(4 * u + 3, G_COLS, F, False)
+        def share(u, cols=G_COLS):
+            finish_vector(4 * u + 3, cols, F, False)
 
         pair_quantize(3)
         x_interleave(7, X7_S, F, "G")
@@ -549,6 +550,8 @@ def tile_parcel_band_hemisphere_coupling_t2_kernel(
             turn(2 * k)
             turn(2 * k + 1)
             add2(4 * u1 + 1)
+            if k == 5:
+                gain_turn()
             add2(4 * u1 + 2)
             now(4 * u2)
             mm3(4 * u2 + 1)
@@ -556,6 +559,8 @@ def tile_parcel_band_hemisphere_coupling_t2_kernel(
             add2(4 * u1 + 3)
             gather1(2 * k)
             gather1(2 * k + 1)
+            if k == 5:
+                gain_column()
             mm3(4 * u2 + 2)
             empty3(4 * u2 + 1)
             mm1(4 * k + 6)
@@ -566,50 +571,52 @@ def tile_parcel_band_hemisphere_coupling_t2_kernel(
             add1(4 * k + 5)
             if k == 6:
                 mm1(4 * k + 7, newest=True)
-            share(u2)
-            empty3(4 * u2 + 3, G_COLS)
+            cols = G_LAST if k == 6 else G_COLS
+            share(u2, cols)
+            empty3(4 * u2 + 3, cols)
             round1(4 * k + 4)
             round1(4 * k + 5)
 
         pair_quantize(8)
-        late(4, G_COLS, None)
-        gain_turn()
+        scale_gpsimd(18, F + G_LAST)
+        store_scaled(18)
+        scale_gpsimd(17, F)
+        store_scaled(17)
         for b in range(3):
             mm2(24 + b)
-        gain_column()
-        mm2(27)
+        mm3_side(20)
         sum1(30)
+        mm2(27)
         sum1(31)
-        mm3(20)
+        scale_side(20)
+        mm3(22)
         add2(24)
         turn(14)
-        turn(15)
         add2(25)
-        mm3(23)
+        turn(15)
         add2(26)
+        turn_side(20)
+        mm3(21)
         gather1(14)
-        mm3_side(21)
         add2(27)
         gather1(15)
-        mm3(22)
-        finish_half(20, False)
-        scale_side(21)
-        empty3(23)
+        mm3(23)
+        finish_half(22, False)
+        empty_side(20)
+        empty3(21)
         quant2(6)
-        turn_side(21)
         quant1(7)
-        scale_gpsimd(23, F, "h2g_6")
+        scale_gpsimd(21, F, "h2g_6")
         mm3(24)
-        empty_side(21)
-        finish_half(20, True)
+        mm3_side(25)
+        finish_half(22, True)
         mm2(28)
         mm2(29)
-        finish_vector(22)
+        finish_vector(23)
         empty3(24)
-        mm3_side(25)
         mm2(30)
         mm2(31)
-        store_scaled(23)
+        store_scaled(21)
         scale_side(25)
         add2(28)
         scale_gpsimd(24, F)
@@ -619,11 +626,10 @@ def tile_parcel_band_hemisphere_coupling_t2_kernel(
         add2(30)
         store_scaled(24)
         empty_side(25)
-        mm3(27)
         add2(31)
-        finish_half(26, False)
+        mm3(27, newest=True)
+        finish_vector(26)
         quant2(7)
-        finish_half(26, True)
         finish_vector(27)
         for t in range(4):
             mm3(28 + t)

@@ -29,8 +29,8 @@ X2_S = 224
 X3_S = 128
 X5_S = 192
 P_HEAD = (192, 192)
-X7_S = 176
-S_X = {3: 384, 4: 112, 5: 0, 6: 0, 7: 0}
+X6_S = 192
+S_X = {3: 384, 4: 128, 5: 0, 6: 0, 7: 0}
 
 
 def tile_parcel_band_hemisphere_coupling_t2_kernel(
@@ -101,9 +101,9 @@ def tile_parcel_band_hemisphere_coupling_t2_kernel(
         load_x(2, 1)
         load_x(3, 0)
         load_scales(c_s, hs_scales.bitcast(I32))
-        load_x(3, 1)
         nc.sync.dma_start(out=c_w[:].bitcast(I32), in_=hs_words.bitcast(I32).rearrange("g p n -> p g n"))
         nc.sync.dma_start(out=gain_b, in_=gain.partition_broadcast(NP))
+        load_x(3, 1)
 
         def perm_aw(h, lo, hi):
             nc.scalar.copy(
@@ -145,7 +145,7 @@ def tile_parcel_band_hemisphere_coupling_t2_kernel(
             else:
                 nc.scalar.copy(out=dst, in_=src)
 
-        todo = [[5, 0, X5_S], [6, 0, F], [7, 0, X7_S]]
+        todo = [[5, 0, X5_S], [6, 0, X6_S], [7, 0, F]]
 
         def s_interleave(width):
             while width > 0 and todo:
@@ -500,7 +500,7 @@ def tile_parcel_band_hemisphere_coupling_t2_kernel(
             finish_vector(4 * u + 3, cols, F, False)
 
         pair_quantize(3)
-        x_interleave(7, X7_S, F, "G")
+        x_interleave(6, X6_S, F, "G")
         for b in range(2):
             mm2(4 + b)
         mm3(0)

@@ -19,14 +19,14 @@ ACT = mybir.ActivationFunctionType
 
 NP = 128
 SPLIT = 176
-SPLIT1 = 176
+SPLIT1 = 88
 K0 = 3
 RUN = 2
 G_COLS = 336
 G_LAST = 256
 P7_COLS = 192
-X2_S = 224
-X3_S = 128
+X2_S = 272
+X3_S = 112
 X5_S = 192
 P_HEAD = (192, 192)
 X6_S = 192
@@ -414,32 +414,71 @@ def tile_parcel_band_hemisphere_coupling_t2_kernel(
                 give_bank("o", i)
                 store(i, 0, F, halves[i][:])
 
+        first = {}
+
+        def mm1_first(half, k):
+            if k == 0:
+                first[half] = psum.tile([NP, F // 2], F32, name="d_0_%d" % half, tag=take_bank("f", half), bufs=1)
+            cols = slice(half * F // 2, (half + 1) * F // 2)
+            nc.tensor.matmul_mx(
+                out=first[half][:],
+                lhsT=a_w[0][:, k, :256].bitcast(FP4X4),
+                lhsT_scale=a_s[0][:, k, :NP],
+                rhs=xc[k][:, cols].bitcast(FP8X4),
+                rhs_scale=xsc[k][:, cols],
+                start=(k == 0),
+                stop=(k == 1),
+            )
+
+        def add1_first(half):
+            if half == 0:
+                h1[0] = work.tile([NP, 4, F], F32, name="h1_0", tag="h1", bufs=4)
+            cols = slice(half * F // 2, (half + 1) * F // 2)
+            nc.vector.scalar_tensor_tensor(
+                out=h1[0][:, 0, cols], in0=first[half][:], scalar=0.0, in1=xs[0, 0][:, 0, cols], op0=ALU.max, op1=ALU.add
+            )
+            give_bank("f", half)
+
         x_interleave(0, 0, SPLIT, "S", "xg_0")
         x_interleave(0, SPLIT, F, "V")
         perm_aw(0, 0, 1)
         perm_as(0, 0, 1)
         x_quantize(0)
-        for t in range(K0):
+        for half in range(2):
+            mm1_first(half, 0)
+        for t in range(1, K0):
             mm1(t, (0,))
-        x_interleave(1, 0, SPLIT1, "S", "xg_1")
-        x_interleave(1, SPLIT1, F, "V")
-        perm_aw(0, 1, 2)
         perm_as(0, 1, 2)
-        x_quantize(1)
+        for half in range(2):
+            lo = half * F // 2
+            x_interleave(1, lo, lo + SPLIT1, "S", "xg_1" if half == 0 else None)
+            x_interleave(1, lo + SPLIT1, lo + F // 2, "V")
+        perm_aw(0, 1, 2)
+        x1c = work.tile([NP, F], U32, name="c_x1", tag="c_one", bufs=4, align_bytes=64)
+        x1s = work.tile([NP, F], U8, name="s_x1", tag="s_one", bufs=4, align_bytes=64)
+        xc[1], xsc[1] = x1c[:], x1s[:]
+        for half in range(2):
+            cols = slice(half * F // 2, (half + 1) * F // 2)
+            nc.vector.quantize_mx(
+                out=x1c[:, cols].bitcast(FP8X4), scales=x1s[:, cols], in_=xg[1][:, cols, :].rearrange("p f t -> p (f t)")
+            )
+            mm1_first(half, 1)
         perm_aw(1, 0, 2)
         perm_as(1, 0, 2)
+        for half in range(2):
+            add1_first(half)
         x_interleave(2, X2_S, F, "G", "xg_1")
         x_interleave(2, 0, X2_S, "S")
         x_interleave(3, X3_S, F, "G")
 
-        for t in range(K0):
+        for t in range(1, K0):
             mm1(t, (1,))
         mm1(3)
         mm1(4)
         mm1(5)
-        for t in range(2):
-            add1(t)
-            round1(t)
+        round1(0)
+        add1(1)
+        round1(1)
         mm1(6)
         turn(0)
         for t in range(2, 4):
@@ -501,9 +540,9 @@ def tile_parcel_band_hemisphere_coupling_t2_kernel(
 
         pair_quantize(3)
         x_interleave(6, X6_S, F, "G")
-        for b in range(2):
-            mm2(4 + b)
+        mm2(4)
         mm3(0)
+        mm2(5)
         sum1(12)
         add1(13)
         mm2(6)
@@ -513,12 +552,12 @@ def tile_parcel_band_hemisphere_coupling_t2_kernel(
         add2(4)
         nc.scalar.copy(out=gain3[:, F : 2 * F], in_=gain_b)
         nc.scalar.copy(out=gain3[:, 2 * F :], in_=gain_b[:, :G_COLS])
+        mm3(3)
         turn(4)
-        turn(5)
         add2(5)
+        turn(5)
         add2(6)
         gather1(4)
-        mm3(3)
         mm3(1)
         add2(7)
         gather1(5)
@@ -628,8 +667,9 @@ def tile_parcel_band_hemisphere_coupling_t2_kernel(
         empty_side(25)
         add2(31)
         mm3(27, newest=True)
-        finish_vector(26)
+        finish_half(26, False)
         quant2(7)
+        finish_half(26, True)
         finish_vector(27)
         for t in range(4):
             mm3(28 + t)

@@ -18,19 +18,19 @@ ALU = mybir.AluOpType
 ACT = mybir.ActivationFunctionType
 
 NP = 128
+P2_S = 112
 SPLIT = 176
 SPLIT1 = 88
 K0 = 3
 RUN = 2
 G_COLS = 336
 G_LAST = 256
-P7_COLS = 192
 X2_S = 272
-X3_S = 112
+X3_S = 80
 X5_S = 192
 P_HEAD = (192, 192)
 X6_S = 192
-S_X = {3: 384, 4: 128, 5: 0, 6: 0, 7: 0}
+S_X = {3: 304, 4: 96, 5: 0, 6: 0}
 
 
 def tile_parcel_band_hemisphere_coupling_t2_kernel(
@@ -61,6 +61,8 @@ def tile_parcel_band_hemisphere_coupling_t2_kernel(
         c_s = keep.tile([NP, 2, H], U8, name="c_s", align_bytes=64)
         gain3 = keep.tile([NP, 2 * F + G_COLS], BF16, name="gain3")
         gain_b = gain3[:, :F]
+        gain_rows = keep.tile([4, NP], BF16, name="gain_rows")
+        gain_f32 = keep.tile([NP, NP], F32, name="gain_f32")
         xs = {}
         for w in range(T):
             for k in range(2):
@@ -69,6 +71,7 @@ def tile_parcel_band_hemisphere_coupling_t2_kernel(
 
         nc.gpsimd.memset(a_sraw[0][:].bitcast(I32), 0)
         nc.vector.memset(a_sraw[1][:].bitcast(I32), 0)
+        nc.vector.memset(gain_f32[:], 0.0)
         make_identity(nc, ident[:])
 
         def load_x(w, k):
@@ -97,6 +100,7 @@ def tile_parcel_band_hemisphere_coupling_t2_kernel(
         load_x(1, 1)
         load_scales(b_s, fb_scales.bitcast(I32))
         nc.sync.dma_start(out=b_w[:].bitcast(I32), in_=fb_words.bitcast(I32)[0])
+        nc.sync.dma_start(out=gain_rows[:], in_=gain.rearrange("(b p) -> b p", b=4))
         load_x(2, 0)
         load_x(2, 1)
         load_x(3, 0)
@@ -104,6 +108,8 @@ def tile_parcel_band_hemisphere_coupling_t2_kernel(
         nc.sync.dma_start(out=c_w[:].bitcast(I32), in_=hs_words.bitcast(I32).rearrange("g p n -> p g n"))
         nc.sync.dma_start(out=gain_b, in_=gain.partition_broadcast(NP))
         load_x(3, 1)
+        nc.sync.dma_start(out=gain3[:, F : 2 * F], in_=gain_b)
+        nc.sync.dma_start(out=gain3[:, 2 * F :], in_=gain_b[:, :G_COLS])
 
         def perm_aw(h, lo, hi):
             nc.scalar.copy(
@@ -349,18 +355,16 @@ def tile_parcel_band_hemisphere_coupling_t2_kernel(
                 cols = min(F, width - F * n)
                 store(i + n, 0, cols, scaled[i][:, F * n : F * n + cols])
 
-        gain_f32 = keep.tile([NP, F], F32, name="gain_f32")
         gain_col = keep.tile([NP, 4], F32, name="gain_col")
         side, side_sb, back = {}, {}, {}
 
         def gain_turn():
-            bank = psum.tile([NP, 4, NP], F32, name="gain_turned", tag=take_bank("g", 0), bufs=1)
-            for b in range(4):
-                nc.tensor.transpose(bank[:, b, :], gain_f32[:, NP * b : NP * b + NP], ident[:])
+            bank = psum.tile([NP, NP], F32, name="gain_turned", tag=take_bank("g", 0), bufs=1)
+            nc.tensor.transpose(bank[:], gain_f32[:], ident[:])
             side["gain"] = bank
 
         def gain_column():
-            nc.scalar.copy(out=gain_col[:], in_=side["gain"][:, :, 0])
+            nc.scalar.copy(out=gain_col[:], in_=side["gain"][:, :4])
             give_bank("g", 0)
 
         def mm3_side(i):
@@ -396,21 +400,14 @@ def tile_parcel_band_hemisphere_coupling_t2_kernel(
             give_bank("b", i)
             store(i, 0, F, res[:])
 
-        def finish_in_place(i, lo):
-            u, m = divmod(i, 4)
-            nc.vector.tensor_tensor(
-                out=raw[u][:, F * m + lo : F * m + F], in0=o[i][:, lo:], in1=gain_b[:, lo:], op=ALU.mult
-            )
-            give_bank("o", i)
-
         halves = {}
 
-        def finish_half(i, second):
-            if not second:
+        def finish_part(i, lo, hi):
+            if lo == 0:
                 halves[i] = work.tile([NP, F], F32, name="hres_%d" % i, tag="res", bufs=8)
-            cols = slice(F // 2, F) if second else slice(0, F // 2)
+            cols = slice(lo, hi)
             nc.vector.tensor_tensor(out=halves[i][:, cols], in0=o[i][:, cols], in1=gain_b[:, cols], op=ALU.mult)
-            if second:
+            if hi == F:
                 give_bank("o", i)
                 store(i, 0, F, halves[i][:])
 
@@ -502,6 +499,7 @@ def tile_parcel_band_hemisphere_coupling_t2_kernel(
             round1(t)
         for b in range(4):
             mm2(b)
+        nc.scalar.copy(out=gain_f32[:4, :], in_=gain_rows[:])
         add1(8)
         round1(8)
         s_interleave(P_HEAD[0])
@@ -522,8 +520,8 @@ def tile_parcel_band_hemisphere_coupling_t2_kernel(
             round1(8 + t)
         s_interleave(P_HEAD[1])
 
-        def late(u, cols, after):
-            scale_gpsimd(4 * u + 1, 2 * F + cols, after)
+        def late(u, width, after):
+            scale_gpsimd(4 * u + 1, width, after)
             store_scaled(4 * u + 1)
 
         def now(i):
@@ -536,7 +534,7 @@ def tile_parcel_band_hemisphere_coupling_t2_kernel(
             round1(i)
 
         def share(u, cols=G_COLS):
-            finish_vector(4 * u + 3, cols, F, False)
+            finish_vector(u, cols, F, False)
 
         pair_quantize(3)
         x_interleave(6, X6_S, F, "G")
@@ -550,19 +548,20 @@ def tile_parcel_band_hemisphere_coupling_t2_kernel(
         now(0)
         round1(13)
         add2(4)
-        nc.scalar.copy(out=gain3[:, F : 2 * F], in_=gain_b)
-        nc.scalar.copy(out=gain3[:, 2 * F :], in_=gain_b[:, :G_COLS])
+        s_interleave(P2_S)
         mm3(3)
         turn(4)
         add2(5)
         turn(5)
+        gain_turn()
         add2(6)
         gather1(4)
         mm3(1)
         add2(7)
         gather1(5)
+        gain_column()
         mm3(2)
-        share(0)
+        share(3)
         mm1(15)
         empty3(1)
         empty3(2)
@@ -573,13 +572,11 @@ def tile_parcel_band_hemisphere_coupling_t2_kernel(
             if k in (3, 5):
                 window_quantize(k // 2 + 1)
             pair_quantize(k + 1)
-            late(k - 3, G_COLS, ("xg_1" if k == 3 else "x_1_0") if k in (3, 5) else None)
+            late(k - 3, 2 * F + G_COLS, ("xg_1" if k == 3 else "x_1_0") if k in (3, 5) else None)
             if k < 7:
                 mm1(4 * k + 4)
                 mm1(4 * k + 5)
             s_interleave(S_X[k])
-            if k == 5:
-                nc.scalar.copy(out=gain_f32[:], in_=gain_b)
             for b in range(4):
                 mm2(4 * u1 + b)
             sum1(4 * k + 2)
@@ -589,8 +586,6 @@ def tile_parcel_band_hemisphere_coupling_t2_kernel(
             turn(2 * k)
             turn(2 * k + 1)
             add2(4 * u1 + 1)
-            if k == 5:
-                gain_turn()
             add2(4 * u1 + 2)
             now(4 * u2)
             mm3(4 * u2 + 1)
@@ -598,8 +593,6 @@ def tile_parcel_band_hemisphere_coupling_t2_kernel(
             add2(4 * u1 + 3)
             gather1(2 * k)
             gather1(2 * k + 1)
-            if k == 5:
-                gain_column()
             mm3(4 * u2 + 2)
             empty3(4 * u2 + 1)
             mm1(4 * k + 6)
@@ -611,7 +604,7 @@ def tile_parcel_band_hemisphere_coupling_t2_kernel(
             if k == 6:
                 mm1(4 * k + 7, newest=True)
             cols = G_LAST if k == 6 else G_COLS
-            share(u2, cols)
+            share(4 * u2 + 3, cols)
             empty3(4 * u2 + 3, cols)
             round1(4 * k + 4)
             round1(4 * k + 5)
@@ -640,7 +633,7 @@ def tile_parcel_band_hemisphere_coupling_t2_kernel(
         add2(27)
         gather1(15)
         mm3(23)
-        finish_half(22, False)
+        finish_part(22, 0, F // 2)
         empty_side(20)
         empty3(21)
         quant2(6)
@@ -648,7 +641,7 @@ def tile_parcel_band_hemisphere_coupling_t2_kernel(
         scale_gpsimd(21, F, "h2g_6")
         mm3(24)
         mm3_side(25)
-        finish_half(22, True)
+        finish_part(22, F // 2, F)
         mm2(28)
         mm2(29)
         finish_vector(23)
@@ -667,9 +660,9 @@ def tile_parcel_band_hemisphere_coupling_t2_kernel(
         empty_side(25)
         add2(31)
         mm3(27, newest=True)
-        finish_half(26, False)
+        finish_part(26, 0, F // 2)
         quant2(7)
-        finish_half(26, True)
+        finish_part(26, F // 2, F)
         finish_vector(27)
         for t in range(4):
             mm3(28 + t)

@@ -18,6 +18,7 @@ ALU = mybir.AluOpType
 ACT = mybir.ActivationFunctionType
 
 NP = 128
+NOW16 = 400
 P2_S = 112
 SPLIT = 176
 SPLIT1 = 88
@@ -26,9 +27,9 @@ RUN = 2
 G_COLS = 336
 G_LAST = 256
 X2_S = 272
-X3_S = 80
-X5_S = 192
-P_HEAD = (192, 192)
+X3_S = 144
+X5_S = 224
+P_HEAD = (224, 192)
 X6_S = 192
 S_X = {3: 304, 4: 96, 5: 0, 6: 0}
 
@@ -266,6 +267,20 @@ def tile_parcel_band_hemisphere_coupling_t2_kernel(
             )
             give_bank("t", j)
 
+        def turn_one(i):
+            u, t = divmod(i, 4)
+            bank = psum.tile([NP, 2, NP], F32, name="h1o_%d" % i, tag=take_bank("o1", i), bufs=1)
+            words = h1b[u][:, t, :].bitcast(F32)
+            for a in range(2):
+                nc.tensor.transpose(bank[:, a, :], words[:, NP * a : NP * a + NP], ident[:])
+            h1t["one", i] = bank
+
+        def gather_one(i):
+            u, t = divmod(i, 4)
+            words = h1g[u].bitcast(F32).rearrange("p (t q a) -> p t q a", t=4, a=2)
+            nc.scalar.copy(out=words[:, t, :, :], in_=h1t["one", i][:].rearrange("p a q -> p q a"))
+            give_bank("o1", i)
+
         def quant1(u):
             h1c[u], h1s[u] = quantize(h1g[u], "h1_%d" % u, "one", 4)
 
@@ -348,6 +363,15 @@ def tile_parcel_band_hemisphere_coupling_t2_kernel(
                 dst = late[:]
             nc.gpsimd.tensor_tensor(out=dst, in0=src, in1=gain3[:, :width], op=ALU.mult)
             scaled[i] = dst
+
+        def scale_run(i, lo, width):
+            u, m = divmod(i, 4)
+            run = raw[u][:, F * m + lo : F * m + lo + width]
+            nc.gpsimd.tensor_tensor(out=run, in0=run, in1=gain3[:, lo : lo + width], op=ALU.mult)
+
+        def store_raw(i, hi=F):
+            u, m = divmod(i, 4)
+            store(i, 0, hi, raw[u][:, F * m : F * m + hi])
 
         def store_scaled(i):
             width = scaled[i].shape[1]
@@ -478,23 +502,27 @@ def tile_parcel_band_hemisphere_coupling_t2_kernel(
         round1(1)
         mm1(6)
         turn(0)
-        for t in range(2, 4):
-            add1(t)
-            round1(t)
-        turn(1)
+        add1(2)
+        round1(2)
+        add1(3)
+        turn_one(2)
         mm1(7)
         x_interleave(3, 0, X3_S, "S")
-        for c in range(2):
-            gather1(c)
+        round1(3)
+        turn_one(3)
+        gather1(0)
+        gather_one(2)
+        gather_one(3)
         for t in range(4, 7):
             add1(t)
 
         window_quantize(1)
         mm1(8)
-        quant1(0)
-        x_interleave(4, 0, F, "G", "xg_1")
-        x_interleave(5, X5_S, F, "G")
+        mm1(9)
         add1(7)
+        quant1(0)
+        x_interleave(4, 0, F, "G", "h1g_0")
+        x_interleave(5, X5_S, F, "G")
         for t in range(4, 8):
             round1(t)
         for b in range(4):
@@ -502,8 +530,8 @@ def tile_parcel_band_hemisphere_coupling_t2_kernel(
         nc.scalar.copy(out=gain_f32[:4, :], in_=gain_rows[:])
         add1(8)
         round1(8)
+        add1(9)
         s_interleave(P_HEAD[0])
-        mm1(9)
         mm1(10)
         add2(0)
         add2(1)
@@ -514,7 +542,9 @@ def tile_parcel_band_hemisphere_coupling_t2_kernel(
         mm1(11)
         gather1(2)
         gather1(3)
-        for t in range(1, 4):
+        round1(9)
+        mm1(12)
+        for t in range(2, 4):
             mm1(11 + t)
             add1(8 + t)
             round1(8 + t)
@@ -572,7 +602,7 @@ def tile_parcel_band_hemisphere_coupling_t2_kernel(
             if k in (3, 5):
                 window_quantize(k // 2 + 1)
             pair_quantize(k + 1)
-            late(k - 3, 2 * F + G_COLS, ("xg_1" if k == 3 else "x_1_0") if k in (3, 5) else None)
+            late(k - 3, 2 * F + G_COLS, ("h1g_0" if k == 3 else "x_1_0") if k in (3, 5) else None)
             if k < 7:
                 mm1(4 * k + 4)
                 mm1(4 * k + 5)
@@ -587,7 +617,11 @@ def tile_parcel_band_hemisphere_coupling_t2_kernel(
             turn(2 * k + 1)
             add2(4 * u1 + 1)
             add2(4 * u1 + 2)
-            now(4 * u2)
+            if k < 6:
+                now(4 * u2)
+            else:
+                empty3(16)
+                scale_run(16, 0, NOW16)
             mm3(4 * u2 + 1)
             mm3(4 * u2 + 3)
             add2(4 * u1 + 3)
@@ -604,44 +638,46 @@ def tile_parcel_band_hemisphere_coupling_t2_kernel(
             if k == 6:
                 mm1(4 * k + 7, newest=True)
             cols = G_LAST if k == 6 else G_COLS
-            share(4 * u2 + 3, cols)
-            empty3(4 * u2 + 3, cols)
+            if k < 6:
+                share(4 * u2 + 3, cols)
+            empty3(4 * u2 + 3, cols, k < 6)
             round1(4 * k + 4)
             round1(4 * k + 5)
 
         pair_quantize(8)
+        scale_run(16, NOW16, 2 * F - NOW16)
+        store_raw(16)
+        store_raw(17)
         scale_gpsimd(18, F + G_LAST)
         store_scaled(18)
-        scale_gpsimd(17, F)
-        store_scaled(17)
         for b in range(3):
             mm2(24 + b)
         mm3_side(20)
         sum1(30)
         mm2(27)
         sum1(31)
-        scale_side(20)
-        mm3(22)
         add2(24)
         turn(14)
         add2(25)
         turn(15)
+        mm3(21)
+        mm3(22)
+        scale_side(20)
         add2(26)
         turn_side(20)
-        mm3(21)
         gather1(14)
         add2(27)
         gather1(15)
+        finish_vector(19, G_LAST)
         mm3(23)
-        finish_part(22, 0, F // 2)
-        empty_side(20)
         empty3(21)
+        empty_side(20)
         quant2(6)
         quant1(7)
         scale_gpsimd(21, F, "h2g_6")
         mm3(24)
         mm3_side(25)
-        finish_part(22, F // 2, F)
+        finish_vector(22)
         mm2(28)
         mm2(29)
         finish_vector(23)

@@ -18,18 +18,19 @@ ALU = mybir.AluOpType
 ACT = mybir.ActivationFunctionType
 
 NP = 128
-NOW16 = 400
-P2_S = 112
+G15 = 320
+NOW = {3: 400, 4: 112, 5: 464, 6: 384}
+P2_S = 176
 SPLIT = 176
 SPLIT1 = 88
 K0 = 3
 RUN = 2
 G_COLS = 336
-G_LAST = 256
+G_LAST = 240
 X2_S = 272
-X3_S = 144
-X5_S = 224
-P_HEAD = (224, 192)
+X3_S = 160
+X5_S = 272
+P_HEAD = (272, 128)
 X6_S = 192
 S_X = {3: 304, 4: 96, 5: 0, 6: 0}
 
@@ -60,7 +61,7 @@ def tile_parcel_band_hemisphere_coupling_t2_kernel(
         b_s = keep.tile([NP, 1, F], U8, name="b_s", align_bytes=64)
         c_w = keep.tile([NP, 2, 2 * H], U8, name="c_w", align_bytes=64)
         c_s = keep.tile([NP, 2, H], U8, name="c_s", align_bytes=64)
-        gain3 = keep.tile([NP, 2 * F + G_COLS], BF16, name="gain3")
+        gain3 = keep.tile([NP, 4 * F], BF16, name="gain3")
         gain_b = gain3[:, :F]
         gain_rows = keep.tile([4, NP], BF16, name="gain_rows")
         gain_f32 = keep.tile([NP, NP], F32, name="gain_f32")
@@ -110,7 +111,7 @@ def tile_parcel_band_hemisphere_coupling_t2_kernel(
         nc.sync.dma_start(out=gain_b, in_=gain.partition_broadcast(NP))
         load_x(3, 1)
         nc.sync.dma_start(out=gain3[:, F : 2 * F], in_=gain_b)
-        nc.sync.dma_start(out=gain3[:, 2 * F :], in_=gain_b[:, :G_COLS])
+        nc.sync.dma_start(out=gain3[:, 2 * F :], in_=gain3[:, : 2 * F])
 
         def perm_aw(h, lo, hi):
             nc.scalar.copy(
@@ -333,6 +334,30 @@ def tile_parcel_band_hemisphere_coupling_t2_kernel(
             )
             o[i] = bank
 
+        def mm3_cols(i, half):
+            u, m = divmod(i, 4)
+            cols = slice(half * F // 2, (half + 1) * F // 2)
+            bank = psum.tile([NP, F // 2], F32, name="o_%d_%d" % (i, half), tag=take_bank("o", (i, half)), bufs=1)
+            nc.tensor.matmul_mx(
+                out=bank[:],
+                lhsT=c_w[:, u % 2, 256 * m : 256 * m + 256].bitcast(FP4X4),
+                lhsT_scale=c_s[:, u % 2, NP * m : NP * m + NP],
+                rhs=h2c[u][:, cols].bitcast(FP8X4),
+                rhs_scale=h2s[u][:, cols],
+                start=True,
+                stop=True,
+            )
+            o[i, half] = bank
+
+        def finish_cols(i, half):
+            if half == 0:
+                halves[i] = work.tile([NP, F], F32, name="hres_%d" % i, tag="res", bufs=8)
+            cols = slice(half * F // 2, (half + 1) * F // 2)
+            nc.vector.tensor_tensor(out=halves[i][:, cols], in0=o[i, half][:], in1=gain_b[:, cols], op=ALU.mult)
+            give_bank("o", (i, half))
+            if half == 1:
+                store(i, 0, F, halves[i][:])
+
         def store(i, lo, hi, res):
             u, m = divmod(i, 4)
             nc.sync.dma_start(out=outs[u % 2][NP * m : NP * m + NP, u // 2, lo:hi], in_=res)
@@ -364,10 +389,15 @@ def tile_parcel_band_hemisphere_coupling_t2_kernel(
             nc.gpsimd.tensor_tensor(out=dst, in0=src, in1=gain3[:, :width], op=ALU.mult)
             scaled[i] = dst
 
-        def scale_run(i, lo, width):
+        def scale_run(i, lo, width, after=None):
             u, m = divmod(i, 4)
             run = raw[u][:, F * m + lo : F * m + lo + width]
-            nc.gpsimd.tensor_tensor(out=run, in0=run, in1=gain3[:, lo : lo + width], op=ALU.mult)
+            dst = run
+            if after is not None:
+                held = work.tile([NP, width], F32, name="late_%d" % i, tag=after, bufs=1, align_bytes=64)
+                dst = held[:]
+            nc.gpsimd.tensor_tensor(out=dst, in0=run, in1=gain3[:, lo : lo + width], op=ALU.mult)
+            return dst
 
         def store_raw(i, hi=F):
             u, m = divmod(i, 4)
@@ -437,26 +467,26 @@ def tile_parcel_band_hemisphere_coupling_t2_kernel(
 
         first = {}
 
-        def mm1_first(half, k):
+        def mm1_first(half, k, w=0):
             if k == 0:
-                first[half] = psum.tile([NP, F // 2], F32, name="d_0_%d" % half, tag=take_bank("f", half), bufs=1)
+                first[half] = psum.tile([NP, F // 2], F32, name="d_%d_%d" % (8 * w, half), tag=take_bank("f", half), bufs=1)
             cols = slice(half * F // 2, (half + 1) * F // 2)
             nc.tensor.matmul_mx(
                 out=first[half][:],
                 lhsT=a_w[0][:, k, :256].bitcast(FP4X4),
                 lhsT_scale=a_s[0][:, k, :NP],
-                rhs=xc[k][:, cols].bitcast(FP8X4),
-                rhs_scale=xsc[k][:, cols],
+                rhs=xc[2 * w + k][:, cols].bitcast(FP8X4),
+                rhs_scale=xsc[2 * w + k][:, cols],
                 start=(k == 0),
                 stop=(k == 1),
             )
 
-        def add1_first(half):
+        def add1_first(half, w=0):
             if half == 0:
-                h1[0] = work.tile([NP, 4, F], F32, name="h1_0", tag="h1", bufs=4)
+                h1[2 * w] = work.tile([NP, 4, F], F32, name="h1_%d" % (2 * w), tag="h1", bufs=4)
             cols = slice(half * F // 2, (half + 1) * F // 2)
             nc.vector.scalar_tensor_tensor(
-                out=h1[0][:, 0, cols], in0=first[half][:], scalar=0.0, in1=xs[0, 0][:, 0, cols], op0=ALU.max, op1=ALU.add
+                out=h1[2 * w][:, 0, cols], in0=first[half][:], scalar=0.0, in1=xs[w, 0][:, 0, cols], op0=ALU.max, op1=ALU.add
             )
             give_bank("f", half)
 
@@ -602,10 +632,24 @@ def tile_parcel_band_hemisphere_coupling_t2_kernel(
             if k in (3, 5):
                 window_quantize(k // 2 + 1)
             pair_quantize(k + 1)
-            late(k - 3, 2 * F + G_COLS, ("h1g_0" if k == 3 else "x_1_0") if k in (3, 5) else None)
-            if k < 7:
-                mm1(4 * k + 4)
-                mm1(4 * k + 5)
+            if k == 3:
+                late(0, 2 * F + G_COLS, "h1g_0")
+            elif k == 4:
+                scale_run(4, NOW[3], 4 * F - NOW[3])
+                for i in range(4, 8):
+                    store_raw(i)
+            elif k == 5:
+                held = scale_run(8, NOW[4], 3 * F - NOW[4], "x_1_0")
+                store(8, NOW[4], F, held[:, : F - NOW[4]])
+                store(9, 0, F, held[:, F - NOW[4] : 2 * F - NOW[4]])
+                store(10, 0, F, held[:, 2 * F - NOW[4] :])
+            else:
+                scale_run(12, NOW[5], 3 * F + G15 - NOW[5])
+                for i in range(12 if NOW[5] < F else 13, 15):
+                    store_raw(i)
+                store_raw(15, G15)
+            mm1(4 * k + 4)
+            mm1(4 * k + 5)
             s_interleave(S_X[k])
             for b in range(4):
                 mm2(4 * u1 + b)
@@ -617,35 +661,47 @@ def tile_parcel_band_hemisphere_coupling_t2_kernel(
             turn(2 * k + 1)
             add2(4 * u1 + 1)
             add2(4 * u1 + 2)
-            if k < 6:
-                now(4 * u2)
-            else:
-                empty3(16)
-                scale_run(16, 0, NOW16)
+            empty3(4 * u2)
+            scale_run(4 * u2, 0, NOW[k])
+            if k == 4:
+                store_raw(8, NOW[4])
+            if NOW[k] == F:
+                store_raw(4 * u2)
             mm3(4 * u2 + 1)
-            mm3(4 * u2 + 3)
+            if k != 4:
+                mm3(4 * u2 + 3)
+            else:
+                mm3_side(11)
             add2(4 * u1 + 3)
             gather1(2 * k)
             gather1(2 * k + 1)
             mm3(4 * u2 + 2)
+            if k == 4:
+                scale_side(11)
             empty3(4 * u2 + 1)
             mm1(4 * k + 6)
             add1(4 * k + 4)
             empty3(4 * u2 + 2)
             if k < 6:
-                mm1(4 * k + 7)
+                mm1(4 * k + 7, (0,) if k == 4 else (0, 1))
             add1(4 * k + 5)
             if k == 6:
                 mm1(4 * k + 7, newest=True)
-            cols = G_LAST if k == 6 else G_COLS
-            if k < 6:
-                share(4 * u2 + 3, cols)
-            empty3(4 * u2 + 3, cols, k < 6)
+                empty3(19, G_LAST, False)
+            if k == 3:
+                empty3(7)
+            if k == 4:
+                turn_side(11)
+                mm1(23, (1,))
+                empty_side(11)
+            if k == 5:
+                share(15, G15)
+                empty3(15, G15)
             round1(4 * k + 4)
             round1(4 * k + 5)
 
         pair_quantize(8)
-        scale_run(16, NOW16, 2 * F - NOW16)
+        scale_run(16, NOW[6], 2 * F - NOW[6])
         store_raw(16)
         store_raw(17)
         scale_gpsimd(18, F + G_LAST)
@@ -674,7 +730,7 @@ def tile_parcel_band_hemisphere_coupling_t2_kernel(
         empty_side(20)
         quant2(6)
         quant1(7)
-        scale_gpsimd(21, F, "h2g_6")
+        scale_gpsimd(21, F, "h1g_7")
         mm3(24)
         mm3_side(25)
         finish_vector(22)
@@ -700,7 +756,11 @@ def tile_parcel_band_hemisphere_coupling_t2_kernel(
         quant2(7)
         finish_part(26, F // 2, F)
         finish_vector(27)
-        for t in range(4):
+        for half in range(2):
+            mm3_cols(28, half)
+        for t in range(1, 4):
             mm3(28 + t)
-        for t in range(4):
+        for half in range(2):
+            finish_cols(28, half)
+        for t in range(1, 4):
             finish_vector(28 + t)

from contextlib import ExitStack

import concourse.mybir as mybir
from concourse.masks import make_identity

P, T, F, H = 1024, 4, 512, 512
FLOPS = 2 * P * P * T * F + 2 * P * T * F * F + 2 * 2 * H * H * T * F

F32 = mybir.dt.float32
BF16 = mybir.dt.bfloat16
U32 = mybir.dt.uint32
I32 = mybir.dt.int32
U8 = mybir.dt.uint8
U16 = mybir.dt.uint16
FP8X4 = mybir.dt.float8_e4m3fn_x4
FP4X4 = mybir.dt.float4_e2m1fn_x4
ALU = mybir.AluOpType
ACT = mybir.ActivationFunctionType

NP = 128
G15 = 320
NOW = {3: 400, 4: 112, 5: 464, 6: 384}
P2_S = 176
SPLIT = 176
SPLIT1 = 88
K0 = 3
RUN = 2
G_COLS = 336
G_LAST = 240
X2_S = 272
X3_S = 160
X5_S = 272
P_HEAD = (272, 128)
X6_S = 192
S_X = {3: 304, 4: 96, 5: 0, 6: 0}


def tile_parcel_band_hemisphere_coupling_t2_kernel(
    tc, x, sc_words, sc_scales, fb_words, fb_scales, hs_words, hs_scales, gain, out_left, out_right
):
    nc = tc.nc
    outs = (out_right, out_left)
    with ExitStack() as ctx:
        keep = ctx.enter_context(tc.tile_pool(name="keep", bufs=1))
        work = ctx.enter_context(tc.tile_pool(name="work", bufs=2))
        psum = ctx.enter_context(tc.psum_pool(name="psum", bufs=2))
        ctx.enter_context(tc.manual_schedule())

        ident = keep.tile([NP, NP], F32, name="ident")
        a_raw, a_w, a_s = {}, {}, {}
        for h in range(2):
            a_w[h] = keep.tile([NP, 2, P], U8, name="a_w_%d" % h, align_bytes=64)
            a_s[h] = keep.tile([NP, 2, H], U8, name="a_s_%d" % h, align_bytes=64)
        for h, lo, hi in ((0, 0, 1), (0, 1, 2), (1, 0, 2)):
            tag = "a_raw_%d_%d" % (h, lo)
            a_raw[h, lo] = work.tile([NP, hi - lo, P], U8, name=tag, tag=tag, bufs=1, align_bytes=64)
        a_sraw = {}
        for h in range(2):
            a_sraw[h] = work.tile([NP, 2, H], U8, name="a_sraw_%d" % h, tag="a_sraw_%d" % h, bufs=1, align_bytes=64)
        b_w = keep.tile([NP, 2 * F], U8, name="b_w", align_bytes=64)
        b_s = keep.tile([NP, 1, F], U8, name="b_s", align_bytes=64)
        c_w = keep.tile([NP, 2, 2 * H], U8, name="c_w", align_bytes=64)
        c_s = keep.tile([NP, 2, H], U8, name="c_s", align_bytes=64)
        gain3 = keep.tile([NP, 4 * F], BF16, name="gain3")
        gain_b = gain3[:, :F]
        gain_rows = keep.tile([4, NP], BF16, name="gain_rows")
        gain_f32 = keep.tile([NP, NP], F32, name="gain_f32")
        xs = {}
        for w in range(T):
            for k in range(2):
                xt = work.tile([NP, 4, F], BF16, name="x_%d_%d" % (w, k), tag="x_%d_%d" % (w, k), bufs=1, align_bytes=64)
                xs[w, k] = xt

        nc.gpsimd.memset(a_sraw[0][:].bitcast(I32), 0)
        nc.vector.memset(a_sraw[1][:].bitcast(I32), 0)
        nc.vector.memset(gain_f32[:], 0.0)
        make_identity(nc, ident[:])

        def load_x(w, k):
            nc.sync.dma_start(out=xs[w, k][:], in_=x[512 * k : 512 * k + 512, w, :].rearrange("(p t) f -> p t f", t=4))

        a_src = sc_words.bitcast(I32)

        def load_a(h, lo, hi):
            nc.sync.dma_start(
                out=a_raw[h, lo][:].bitcast(I32),
                in_=a_src[lo:hi, :, 256 * h : 256 * h + 256].rearrange("g p n -> p g n"),
            )

        def load_scales(dst, src):
            for r in range(4):
                nc.sync.dma_start(out=dst[r:NP:32].bitcast(I32), in_=src[:, r:16:4, :].rearrange("g q n -> q g n"))

        load_x(0, 0)
        load_a(0, 0, 1)
        load_scales(a_sraw[0], sc_scales.bitcast(I32)[:, :, :NP])
        load_x(0, 1)
        load_a(0, 1, 2)
        load_a(1, 0, 2)
        load_scales(a_sraw[1], sc_scales.bitcast(I32)[:, :, NP:])
        load_x(1, 0)
        load_x(1, 1)
        load_scales(b_s, fb_scales.bitcast(I32))
        nc.sync.dma_start(out=b_w[:].bitcast(I32), in_=fb_words.bitcast(I32)[0])
        nc.sync.dma_start(out=gain_rows[:], in_=gain.rearrange("(b p) -> b p", b=4))
        load_x(2, 0)
        load_x(2, 1)
        load_x(3, 0)
        load_scales(c_s, hs_scales.bitcast(I32))
        nc.sync.dma_start(out=c_w[:].bitcast(I32), in_=hs_words.bitcast(I32).rearrange("g p n -> p g n"))
        nc.sync.dma_start(out=gain_b, in_=gain.partition_broadcast(NP))
        load_x(3, 1)
        nc.sync.dma_start(out=gain3[:, F : 2 * F], in_=gain_b)
        nc.sync.dma_start(out=gain3[:, 2 * F :], in_=gain3[:, : 2 * F])

        def perm_aw(h, lo, hi):
            nc.scalar.copy(
                out=a_w[h][:, lo:hi, :].bitcast(U16).rearrange("p g (t m) -> p g t m", t=4),
                in_=a_raw[h, lo][:].bitcast(U16).rearrange("p g (m t) -> p g t m", t=4),
            )

        def perm_as(h, lo, hi):
            nc.vector.tensor_copy(
                out=a_s[h][:, lo:hi, :].rearrange("p g (t m) -> p g t m", t=4),
                in_=a_sraw[h][:, lo:hi, :].rearrange("p g (m t) -> p g t m", t=4),
            )

        xg, xc, xsc, window, pair = {}, {}, {}, {}, {}

        def x_interleave(v, lo, hi, eng, slot=None):
            w, k = divmod(v, 2)
            if slot is not None and w == 0:
                one = work.tile([NP, F, 4], BF16, name="xg_%d" % v, tag=slot, bufs=1, align_bytes=64)
                xg[v] = one[:]
            elif slot is not None:
                window[w] = work.tile([NP, 2 * F, 4], BF16, name="xw_%d" % w, tag=slot, bufs=1, align_bytes=64)
                xg[2 * w], xg[2 * w + 1] = window[w][:, :F, :], window[w][:, F:, :]
            tile = xg[v]
            if eng == "G":
                nc.gpsimd.tensor_scalar(
                    out=tile[:, lo:hi, :],
                    in0=xs[w, k][:, :, lo:hi].rearrange("p t c -> p c t"),
                    scalar1=1.0,
                    scalar2=0.0,
                    op0=ALU.mult,
                    op1=ALU.add,
                )
                return
            dst = tile[:, lo:hi, :].rearrange("p (c i) t -> p c t i", i=4)
            src = xs[w, k][:, :, lo:hi].rearrange("p t (c i) -> p c t i", i=4)
            if eng == "V":
                nc.vector.tensor_copy(out=dst, in_=src)
            else:
                nc.scalar.copy(out=dst, in_=src)

        todo = [[5, 0, X5_S], [6, 0, X6_S], [7, 0, F]]

        def s_interleave(width):
            while width > 0 and todo:
                v, lo, hi = todo[0]
                n = min(width, hi - lo)
                x_interleave(v, lo, lo + n, "S", "x_1_0" if v not in xg else None)
                width = width - n
                if lo + n == hi:
                    todo.pop(0)
                else:
                    todo[0] = [v, lo + n, hi]

        def quantize(src, name, tag, bufs):
            width = src.shape[1] // 4
            c = work.tile([NP, width], U32, name="c_" + name, tag="c_" + tag, bufs=bufs, align_bytes=64)
            s = work.tile([NP, width], U8, name="s_" + name, tag="s_" + tag, bufs=bufs, align_bytes=64)
            nc.vector.quantize_mx(out=c[:].bitcast(FP8X4), scales=s[:], in_=src)
            return c[:], s[:]

        def x_quantize(v):
            xc[v], xsc[v] = quantize(xg[v].rearrange("p f t -> p (f t)"), "x%d" % v, "one", 4)

        def window_quantize(w):
            c, s = quantize(window[w][:].rearrange("p f t -> p (f t)"), "w%d" % w, "window", 2)
            for k in range(2):
                xc[2 * w + k], xsc[2 * w + k] = c[:, F * k : F * k + F], s[:, F * k : F * k + F]

        def pair_half(k, half):
            if k not in pair:
                pair[k] = work.tile([NP, 2, 4 * F], BF16, name="pair_%d" % k, tag="pair", bufs=2, align_bytes=64)
            return pair[k][:, half, :]

        def pair_quantize(k):
            c, s = quantize(pair[k][:].rearrange("p h n -> p (h n)"), "p%d" % k, "pair", 2)
            h1c[k - 2], h1s[k - 2] = c[:, :F], s[:, :F]
            h2c[k - 3], h2s[k - 3] = c[:, F:], s[:, F:]

        d, h1, h1t, h1g, h1c, h1s, e, h2g, h2c, h2s, o, raw, h1b = ({} for i in range(13))

        free_banks = ["bank_%d" % b for b in range(8)]
        bank_of = {}

        def take_bank(kind, i, newest=False):
            bank_of[kind, i] = free_banks.pop(-1 if newest else 0)
            return bank_of[kind, i]

        def give_bank(kind, i):
            free_banks.append(bank_of[kind, i])

        def mm1(i, passes=(0, 1), newest=False):
            u, t = divmod(i, 4)
            w, h = divmod(u, 2)
            if i not in d:
                d[i] = psum.tile([NP, F], F32, name="d_%d" % i, tag=take_bank("d", i, newest), bufs=1)
            acc = d[i]
            for k in passes:
                nc.tensor.matmul_mx(
                    out=acc[:],
                    lhsT=a_w[h][:, k, 256 * t : 256 * t + 256].bitcast(FP4X4),
                    lhsT_scale=a_s[h][:, k, NP * t : NP * t + NP],
                    rhs=xc[2 * w + k].bitcast(FP8X4),
                    rhs_scale=xsc[2 * w + k],
                    start=(k == 0),
                    stop=(k == 1),
                )

        def add1(i, lo=0, hi=F):
            u, t = divmod(i, 4)
            w, h = divmod(u, 2)
            if t == 0:
                h1[u] = work.tile([NP, 4, F], F32, name="h1_%d" % u, tag="h1", bufs=4)
            nc.vector.scalar_tensor_tensor(
                out=h1[u][:, t, lo:hi],
                in0=d[i][:, lo:hi],
                scalar=0.0,
                in1=xs[w, h][:, t, lo:hi],
                op0=ALU.max,
                op1=ALU.add,
            )
            if hi == F:
                give_bank("d", i)

        def round1(i):
            u, t = divmod(i, 4)
            if t == 0:
                h1b[u] = work.tile([NP, 4, F], BF16, name="h1b_%d" % u, tag="h1b", bufs=2)
            nc.scalar.copy(
                out=h1b[u][:, t, :].rearrange("p (a n m e) -> p n a m e", a=2, m=4, e=2),
                in_=h1[u][:, t, :].rearrange("p (n m a e) -> p n a m e", a=2, m=4, e=2),
            )

        def turn(j):
            u, c = divmod(j, 2)
            bank = psum.tile([NP, 2, 2, NP], F32, name="h1t_%d" % j, tag=take_bank("t", j), bufs=1)
            for t in range(2):
                words = h1b[u][:, 2 * c + t, :].bitcast(F32)
                for a in range(2):
                    nc.tensor.transpose(bank[:, t, a, :], words[:, NP * a : NP * a + NP], ident[:])
            h1t[j] = bank

        def gather1(j):
            u, c = divmod(j, 2)
            if c == 0 and u in (0, 7):
                one = work.tile([NP, 4 * F], BF16, name="h1g_%d" % u, tag="h1g_%d" % u, bufs=1, align_bytes=64)
                h1g[u] = one[:]
            elif c == 0:
                h1g[u] = pair_half(u + 2, 0)
            words = h1g[u].bitcast(F32).rearrange("p (t q a) -> p t q a", t=4, a=2)
            nc.scalar.copy(
                out=words[:, 2 * c : 2 * c + 2, :, :],
                in_=h1t[j][:].rearrange("p t a q -> p t q a"),
            )
            give_bank("t", j)

        def turn_one(i):
            u, t = divmod(i, 4)
            bank = psum.tile([NP, 2, NP], F32, name="h1o_%d" % i, tag=take_bank("o1", i), bufs=1)
            words = h1b[u][:, t, :].bitcast(F32)
            for a in range(2):
                nc.tensor.transpose(bank[:, a, :], words[:, NP * a : NP * a + NP], ident[:])
            h1t["one", i] = bank

        def gather_one(i):
            u, t = divmod(i, 4)
            words = h1g[u].bitcast(F32).rearrange("p (t q a) -> p t q a", t=4, a=2)
            nc.scalar.copy(out=words[:, t, :, :], in_=h1t["one", i][:].rearrange("p a q -> p q a"))
            give_bank("o1", i)

        def quant1(u):
            h1c[u], h1s[u] = quantize(h1g[u], "h1_%d" % u, "one", 4)

        def mm2(i):
            u, b = divmod(i, 4)
            bank = psum.tile([NP, 4, NP], F32, name="e_%d" % i, tag=take_bank("e", i), bufs=1)
            for t in range(4):
                nc.tensor.matmul_mx(
                    out=bank[:, t, :],
                    lhsT=h1c[u][:, NP * t : NP * t + NP].bitcast(FP8X4),
                    lhsT_scale=h1s[u][:, NP * t : NP * t + NP],
                    rhs=b_w[:, 256 * b : 256 * b + 256].bitcast(FP4X4),
                    rhs_scale=b_s[:, 0, NP * b : NP * b + NP],
                    start=True,
                    stop=True,
                )
            e[i] = bank

        def add2(i):
            u, b = divmod(i, 4)
            if b == 0 and u >= 6:
                one = work.tile([NP, F, 4], BF16, name="h2g_%d" % u, tag="h2g_%d" % u, bufs=1, align_bytes=64)
                h2g[u] = one[:]
            elif b == 0:
                h2g[u] = pair_half(u + 3, 1).rearrange("p (f t) -> p f t", t=4)
            cols = slice(NP * b, NP * b + NP)
            nc.vector.tensor_tensor(
                out=h2g[u][:, cols, :].rearrange("p (a i) t -> p a t i", i=RUN),
                in0=e[i][:].rearrange("p t (a i) -> p a t i", i=RUN),
                in1=h1[u][:, :, cols].rearrange("p t (a i) -> p a t i", i=RUN),
                op=ALU.add,
            )
            give_bank("e", i)

        def quant2(u):
            h2c[u], h2s[u] = quantize(h2g[u].rearrange("p f t -> p (f t)"), "h2_%d" % u, "one", 4)

        def mm3(i, newest=False):
            u, m = divmod(i, 4)
            g = u % 2
            bank = psum.tile([NP, F], F32, name="o_%d" % i, tag=take_bank("o", i, newest), bufs=1)
            nc.tensor.matmul_mx(
                out=bank[:],
                lhsT=c_w[:, g, 256 * m : 256 * m + 256].bitcast(FP4X4),
                lhsT_scale=c_s[:, g, NP * m : NP * m + NP],
                rhs=h2c[u].bitcast(FP8X4),
                rhs_scale=h2s[u],
                start=True,
                stop=True,
            )
            o[i] = bank

        def mm3_cols(i, half):
            u, m = divmod(i, 4)
            cols = slice(half * F // 2, (half + 1) * F // 2)
            bank = psum.tile([NP, F // 2], F32, name="o_%d_%d" % (i, half), tag=take_bank("o", (i, half)), bufs=1)
            nc.tensor.matmul_mx(
                out=bank[:],
                lhsT=c_w[:, u % 2, 256 * m : 256 * m + 256].bitcast(FP4X4),
                lhsT_scale=c_s[:, u % 2, NP * m : NP * m + NP],
                rhs=h2c[u][:, cols].bitcast(FP8X4),
                rhs_scale=h2s[u][:, cols],
                start=True,
                stop=True,
            )
            o[i, half] = bank

        def finish_cols(i, half):
            if half == 0:
                halves[i] = work.tile([NP, F], F32, name="hres_%d" % i, tag="res", bufs=8)
            cols = slice(half * F // 2, (half + 1) * F // 2)
            nc.vector.tensor_tensor(out=halves[i][:, cols], in0=o[i, half][:], in1=gain_b[:, cols], op=ALU.mult)
            give_bank("o", (i, half))
            if half == 1:
                store(i, 0, F, halves[i][:])

        def store(i, lo, hi, res):
            u, m = divmod(i, 4)
            nc.sync.dma_start(out=outs[u % 2][NP * m : NP * m + NP, u // 2, lo:hi], in_=res)

        def finish_vector(i, lo=0, hi=F, free=True):
            res = work.tile([NP, hi - lo], F32, name="res_%d_%d" % (i, lo), tag="res", bufs=8)
            nc.vector.tensor_tensor(out=res[:], in0=o[i][:, lo:hi], in1=gain_b[:, lo:hi], op=ALU.mult)
            if free:
                give_bank("o", i)
            store(i, lo, hi, res[:])

        def empty3(i, hi=F, free=True, lo=0):
            u, m = divmod(i, 4)
            if u not in raw:
                raw[u] = work.tile([NP, 4 * F], F32, name="raw_%d" % u, tag="raw", bufs=3)
            nc.scalar.copy(out=raw[u][:, F * m + lo : F * m + hi], in_=o[i][:, lo:hi])
            if free:
                give_bank("o", i)

        scaled = {}

        def scale_gpsimd(i, width, after=None):
            u, m = divmod(i, 4)
            src = raw[u][:, F * m : F * m + width]
            dst = src
            if after is not None:
                late = work.tile([NP, width], F32, name="late_%d" % i, tag=after, bufs=1, align_bytes=64)
                dst = late[:]
            nc.gpsimd.tensor_tensor(out=dst, in0=src, in1=gain3[:, :width], op=ALU.mult)
            scaled[i] = dst

        def scale_run(i, lo, width, after=None):
            u, m = divmod(i, 4)
            run = raw[u][:, F * m + lo : F * m + lo + width]
            dst = run
            if after is not None:
                held = work.tile([NP, width], F32, name="late_%d" % i, tag=after, bufs=1, align_bytes=64)
                dst = held[:]
            nc.gpsimd.tensor_tensor(out=dst, in0=run, in1=gain3[:, lo : lo + width], op=ALU.mult)
            return dst

        def store_raw(i, hi=F):
            u, m = divmod(i, 4)
            store(i, 0, hi, raw[u][:, F * m : F * m + hi])

        def store_scaled(i):
            width = scaled[i].shape[1]
            for n in range((width + F - 1) // F):
                cols = min(F, width - F * n)
                store(i + n, 0, cols, scaled[i][:, F * n : F * n + cols])

        gain_col = keep.tile([NP, 4], F32, name="gain_col")
        side, side_sb, back = {}, {}, {}

        def gain_turn():
            bank = psum.tile([NP, NP], F32, name="gain_turned", tag=take_bank("g", 0), bufs=1)
            nc.tensor.transpose(bank[:], gain_f32[:], ident[:])
            side["gain"] = bank

        def gain_column():
            nc.scalar.copy(out=gain_col[:], in_=side["gain"][:, :4])
            give_bank("g", 0)

        def mm3_side(i):
            u, m = divmod(i, 4)
            bank = psum.tile([NP, 4, NP], F32, name="side_%d" % i, tag=take_bank("s", i), bufs=1)
            for b in range(4):
                nc.tensor.matmul_mx(
                    out=bank[:, b, :],
                    lhsT=h2c[u][:, NP * b : NP * b + NP].bitcast(FP8X4),
                    lhsT_scale=h2s[u][:, NP * b : NP * b + NP],
                    rhs=c_w[:, u % 2, 256 * m : 256 * m + 256].bitcast(FP4X4),
                    rhs_scale=c_s[:, u % 2, NP * m : NP * m + NP],
                    start=True,
                    stop=True,
                )
            side[i] = bank

        def scale_side(i):
            sb = work.tile([NP, 4, NP], F32, name="side_sb_%d" % i, tag="side_sb", bufs=2)
            for b in range(4):
                nc.scalar.activation(out=sb[:, b, :], in_=side[i][:, b, :], func=ACT.Copy, scale=gain_col[:, b : b + 1])
            give_bank("s", i)
            side_sb[i] = sb

        def turn_side(i):
            back[i] = psum.tile([NP, 4, NP], F32, name="back_%d" % i, tag=take_bank("b", i), bufs=1)
            for b in range(4):
                nc.tensor.transpose(back[i][:, b, :], side_sb[i][:, b, :], ident[:])

        def empty_side(i):
            res = work.tile([NP, F], F32, name="sres_%d" % i, tag="res", bufs=8)
            nc.scalar.copy(out=res[:], in_=back[i][:].rearrange("p b q -> p (b q)"))
            give_bank("b", i)
            store(i, 0, F, res[:])

        halves = {}

        def finish_part(i, lo, hi):
            if lo == 0:
                halves[i] = work.tile([NP, F], F32, name="hres_%d" % i, tag="res", bufs=8)
            cols = slice(lo, hi)
            nc.vector.tensor_tensor(out=halves[i][:, cols], in0=o[i][:, cols], in1=gain_b[:, cols], op=ALU.mult)
            if hi == F:
                give_bank("o", i)
                store(i, 0, F, halves[i][:])

        first = {}

        def mm1_first(half, k, w=0):
            if k == 0:
                first[half] = psum.tile([NP, F // 2], F32, name="d_%d_%d" % (8 * w, half), tag=take_bank("f", half), bufs=1)
            cols = slice(half * F // 2, (half + 1) * F // 2)
            nc.tensor.matmul_mx(
                out=first[half][:],
                lhsT=a_w[0][:, k, :256].bitcast(FP4X4),
                lhsT_scale=a_s[0][:, k, :NP],
                rhs=xc[2 * w + k][:, cols].bitcast(FP8X4),
                rhs_scale=xsc[2 * w + k][:, cols],
                start=(k == 0),
                stop=(k == 1),
            )

        def add1_first(half, w=0):
            if half == 0:
                h1[2 * w] = work.tile([NP, 4, F], F32, name="h1_%d" % (2 * w), tag="h1", bufs=4)
            cols = slice(half * F // 2, (half + 1) * F // 2)
            nc.vector.scalar_tensor_tensor(
                out=h1[2 * w][:, 0, cols], in0=first[half][:], scalar=0.0, in1=xs[w, 0][:, 0, cols], op0=ALU.max, op1=ALU.add
            )
            give_bank("f", half)

        x_interleave(0, 0, SPLIT, "S", "xg_0")
        x_interleave(0, SPLIT, F, "V")
        perm_aw(0, 0, 1)
        perm_as(0, 0, 1)
        x_quantize(0)
        for half in range(2):
            mm1_first(half, 0)
        for t in range(1, K0):
            mm1(t, (0,))
        perm_as(0, 1, 2)
        for half in range(2):
            lo = half * F // 2
            x_interleave(1, lo, lo + SPLIT1, "S", "xg_1" if half == 0 else None)
            x_interleave(1, lo + SPLIT1, lo + F // 2, "V")
        perm_aw(0, 1, 2)
        x1c = work.tile([NP, F], U32, name="c_x1", tag="c_one", bufs=4, align_bytes=64)
        x1s = work.tile([NP, F], U8, name="s_x1", tag="s_one", bufs=4, align_bytes=64)
        xc[1], xsc[1] = x1c[:], x1s[:]
        for half in range(2):
            cols = slice(half * F // 2, (half + 1) * F // 2)
            nc.vector.quantize_mx(
                out=x1c[:, cols].bitcast(FP8X4), scales=x1s[:, cols], in_=xg[1][:, cols, :].rearrange("p f t -> p (f t)")
            )
            mm1_first(half, 1)
        perm_aw(1, 0, 2)
        perm_as(1, 0, 2)
        for half in range(2):
            add1_first(half)
        x_interleave(2, X2_S, F, "G", "xg_1")
        x_interleave(2, 0, X2_S, "S")
        x_interleave(3, X3_S, F, "G")

        for t in range(1, K0):
            mm1(t, (1,))
        mm1(3)
        mm1(4)
        mm1(5)
        round1(0)
        add1(1)
        round1(1)
        mm1(6)
        turn(0)
        add1(2)
        round1(2)
        add1(3)
        turn_one(2)
        mm1(7)
        x_interleave(3, 0, X3_S, "S")
        round1(3)
        turn_one(3)
        gather1(0)
        gather_one(2)
        gather_one(3)
        for t in range(4, 7):
            add1(t)

        window_quantize(1)
        mm1(8)
        mm1(9)
        add1(7)
        quant1(0)
        x_interleave(4, 0, F, "G", "h1g_0")
        x_interleave(5, X5_S, F, "G")
        for t in range(4, 8):
            round1(t)
        for b in range(4):
            mm2(b)
        nc.scalar.copy(out=gain_f32[:4, :], in_=gain_rows[:])
        add1(8)
        round1(8)
        add1(9)
        s_interleave(P_HEAD[0])
        mm1(10)
        add2(0)
        add2(1)
        turn(2)
        turn(3)
        add2(2)
        add2(3)
        mm1(11)
        gather1(2)
        gather1(3)
        round1(9)
        mm1(12)
        for t in range(2, 4):
            mm1(11 + t)
            add1(8 + t)
            round1(8 + t)
        s_interleave(P_HEAD[1])

        def late(u, width, after):
            scale_gpsimd(4 * u + 1, width, after)
            store_scaled(4 * u + 1)

        def now(i):
            empty3(i)
            scale_gpsimd(i, F)
            store_scaled(i)

        def sum1(i):
            add1(i)
            round1(i)

        def share(u, cols=G_COLS):
            finish_vector(u, cols, F, False)

        pair_quantize(3)
        x_interleave(6, X6_S, F, "G")
        mm2(4)
        mm3(0)
        mm2(5)
        sum1(12)
        add1(13)
        mm2(6)
        mm2(7)
        now(0)
        round1(13)
        add2(4)
        s_interleave(P2_S)
        mm3(3)
        turn(4)
        add2(5)
        turn(5)
        gain_turn()
        add2(6)
        gather1(4)
        mm3(1)
        add2(7)
        gather1(5)
        gain_column()
        mm3(2)
        share(3)
        mm1(15)
        empty3(1)
        empty3(2)
        empty3(3, G_COLS)

        for k in range(3, 7):
            u1, u2 = k - 1, k - 2
            if k in (3, 5):
                window_quantize(k // 2 + 1)
            pair_quantize(k + 1)
            if k == 3:
                late(0, 2 * F + G_COLS, "h1g_0")
            elif k == 4:
                scale_run(4, NOW[3], 4 * F - NOW[3])
                for i in range(4, 8):
                    store_raw(i)
            elif k == 5:
                held = scale_run(8, NOW[4], 3 * F - NOW[4], "x_1_0")
                store(8, NOW[4], F, held[:, : F - NOW[4]])
                store(9, 0, F, held[:, F - NOW[4] : 2 * F - NOW[4]])
                store(10, 0, F, held[:, 2 * F - NOW[4] :])
            else:
                scale_run(12, NOW[5], 3 * F + G15 - NOW[5])
                for i in range(12 if NOW[5] < F else 13, 15):
                    store_raw(i)
                store_raw(15, G15)
            mm1(4 * k + 4)
            mm1(4 * k + 5)
            s_interleave(S_X[k])
            for b in range(4):
                mm2(4 * u1 + b)
            sum1(4 * k + 2)
            sum1(4 * k + 3)
            mm3(4 * u2)
            add2(4 * u1)
            turn(2 * k)
            turn(2 * k + 1)
            add2(4 * u1 + 1)
            add2(4 * u1 + 2)
            empty3(4 * u2)
            scale_run(4 * u2, 0, NOW[k])
            if k == 4:
                store_raw(8, NOW[4])
            if NOW[k] == F:
                store_raw(4 * u2)
            mm3(4 * u2 + 1)
            if k != 4:
                mm3(4 * u2 + 3)
            else:
                mm3_side(11)
            add2(4 * u1 + 3)
            gather1(2 * k)
            gather1(2 * k + 1)
            mm3(4 * u2 + 2)
            if k == 4:
                scale_side(11)
            empty3(4 * u2 + 1)
            mm1(4 * k + 6)
            add1(4 * k + 4)
            empty3(4 * u2 + 2)
            if k < 6:
                mm1(4 * k + 7, (0,) if k == 4 else (0, 1))
            add1(4 * k + 5)
            if k == 6:
                mm1(4 * k + 7, newest=True)
                empty3(19, G_LAST, False)
            if k == 3:
                empty3(7)
            if k == 4:
                turn_side(11)
                mm1(23, (1,))
                empty_side(11)
            if k == 5:
                share(15, G15)
                empty3(15, G15)
            round1(4 * k + 4)
            round1(4 * k + 5)

        pair_quantize(8)
        scale_run(16, NOW[6], 2 * F - NOW[6])
        store_raw(16)
        store_raw(17)
        scale_gpsimd(18, F + G_LAST)
        store_scaled(18)
        for b in range(3):
            mm2(24 + b)
        mm3_side(20)
        sum1(30)
        mm2(27)
        sum1(31)
        add2(24)
        turn(14)
        add2(25)
        turn(15)
        mm3(21)
        mm3(22)
        scale_side(20)
        add2(26)
        turn_side(20)
        gather1(14)
        add2(27)
        gather1(15)
        finish_vector(19, G_LAST)
        mm3(23)
        empty3(21)
        empty_side(20)
        quant2(6)
        quant1(7)
        scale_gpsimd(21, F, "h1g_7")
        mm3(24)
        mm3_side(25)
        finish_vector(22)
        mm2(28)
        mm2(29)
        finish_vector(23)
        empty3(24)
        mm2(30)
        mm2(31)
        store_scaled(21)
        scale_side(25)
        add2(28)
        scale_gpsimd(24, F)
        turn_side(25)
        add2(29)
        mm3(26)
        add2(30)
        store_scaled(24)
        empty_side(25)
        add2(31)
        mm3(27, newest=True)
        finish_part(26, 0, F // 2)
        quant2(7)
        finish_part(26, F // 2, F)
        finish_vector(27)
        for half in range(2):
            mm3_cols(28, half)
        for t in range(1, 4):
            mm3(28 + t)
        for half in range(2):
            finish_cols(28, half)
        for t in range(1, 4):
            finish_vector(28 + t)
